import numpy as np, ml_dtypes
CORES = [2,6,10,14,18,22,26,30]
N = 8
BF = ml_dtypes.bfloat16
def gentries(a):
    return np.ascontiguousarray(a.reshape(8, 16, -1).transpose(0, 2, 1)).reshape(8, -1)
def gtable(e):
    e = np.asarray(e); return np.ascontiguousarray(e.reshape(8, -1, 16).transpose(0, 2, 1)).reshape(128, -1).astype(np.int32)
W, CELLS, K, RO, TH1, TH2 = 4096, 1024, 128, 5, 240, 640
def world(rng, fam, uneven):
    X = np.zeros((N, 8, W, 16), np.int64)
    for g in range(8):
        P = int(fam[g]); pr = rng.integers(0, 256, (P, 16))
        if uneven: pr = np.floor(rng.random((P, 16)) * np.exp2(8 * rng.random((P, 1)))).astype(np.int64)
        w = rng.integers(0, P, (N, W)); s = rng.choice(np.array([2, 8, 24]), (N, W, 1))
        X[:, g] = np.clip(pr[w] + rng.integers(-24, 25, (N, W, 16)) * s // 24, 0, 255)
    return X
def parts(rng, fam, uneven=False):
    return (world(rng, fam, uneven), rng.integers(0, W, (N, 8, CELLS, 16)), rng.integers(0, CELLS, (N, 8, K)), rng.integers(0, 256, (N, 8, K, 16)),
            rng.integers(0, 256, (N, 8, 16, 16)), rng.integers(0, 256, (N, 8, 16)))
def half(a):
    return np.ascontiguousarray(a).astype(np.float32).astype(BF)
def pack(X, ce, v, z, kp, wv):
    return {"px": half(X.transpose(0, 1, 3, 2).reshape(N, 128, W)), "ce": np.ascontiguousarray(ce.transpose(0, 1, 3, 2).reshape(N, 128, CELLS)).astype(np.int32),
            "v0": np.stack([gtable(a) for a in v]), "z0": half(z.transpose(0, 1, 3, 2).reshape(N, 128, K)), "kap": half(kp.reshape(N, 128, 16)), "wu": half(wv.reshape(N, 128, 1))}
def cut(a):
    return a // 16 + (np.arange(16) < a % 16)
def setup_inputs(rng):
    return pack(*parts(rng, rng.choice(np.array([8, 10, 12, 16]), 8)))
def setup_inputs_spread(rng):
    X, ce, v, z, kp, wv = parts(rng, rng.permutation(np.array([2, 4, 8, 12, 16, 32, 64, 128])), True)
    e = rng.choice(np.array([1.0, 2.0, 6.0]), (N, 8, CELLS, 1)); ce = np.floor(W * rng.random(ce.shape) ** e).astype(np.int64)
    v = np.floor(CELLS * rng.random(v.shape) ** 3).astype(np.int64)
    z = np.floor(rng.random(z.shape) * np.exp2(8 * rng.random((N, 8, K, 1)))).astype(np.int64)
    kp = np.floor(256 * rng.random(kp.shape) ** rng.choice(np.array([0.5, 1.0, 4.0]), (N, 8, 1, 16))).astype(np.int64)
    wv = np.floor(256 * rng.random(wv.shape) ** 2).astype(np.int64)
    return pack(X, ce, v, z, kp, wv)
def setup_inputs_ends(rng):
    def mix(n):
        return np.where(rng.random((N, 8, n, 1)) < 0.5, 255 * rng.integers(0, 2, (N, 8, n, 16)), 255 * rng.integers(0, 2, (N, 8, n, 1)))
    i = np.arange(16); R = 255 * (i < 9)
    X = mix(W); X[:, :, W - 1] = 255; X[:, :, 0] = 0; X[:, 3, 0] = 255
    X[:, 7, W - 1] = R; X[:, 7, 0] = 255 * (i < 4); X[:, 7, W - 2] = 255
    kind = rng.integers(0, 6, (N, 8, CELLS, 1)); slot = rng.integers(0, 16, (N, 8, CELLS, 1)); coin = rng.integers(0, 2, (N, 8, CELLS, 16))
    on = np.where(kind == 0, 0, np.where(kind == 1, i == slot, np.where(kind == 2, (i == 0) | (i == 15), np.where(kind == 3, 1, coin))))
    ce = (W - 1) * on.astype(np.int64)
    ce = np.where((kind == 5) & (rng.random(ce.shape) < 0.5), rng.integers(0, W, ce.shape), ce)
    ce[:, 7, CELLS - 1] = 0; ce[:, 7, CELLS - 1, 15] = W - 1; ce[:, 7, 0] = 0; ce[:, 7, 0, 14:] = W - 2
    v = np.where(rng.random((N, 8, K)) < 0.8, (CELLS - 1) * rng.integers(0, 2, (N, 8, K)), rng.integers(0, CELLS, (N, 8, K)))
    v[:, :, 0] = 0; v[:, :, K - 1] = CELLS - 1; v[:, 7, K - 2] = 0
    z = mix(K); z[:, 6] = np.where(rng.random((N, K, 1)) < 0.8, 255, z[:, 6]); z[:, 7, K - 2:] = 255; z[:, :, K - 1] = 255
    kp = np.where(rng.random((N, 8, 16, 16)) < 0.15, rng.integers(0, 256, (N, 8, 16, 16)), 255 * rng.integers(0, 2, (N, 8, 16, 16)))
    wv = np.where(rng.random((N, 8, 16)) < 0.15, rng.integers(0, 256, (N, 8, 16)), 255 * rng.integers(0, 2, (N, 8, 16)))
    kp[:, 6] = 255; wv[:, 6] = 255
    last = np.where(i == 0, 255, np.where(i == 1, 2, 0))
    wv[:, 7] = np.where(i < 9, last, wv[:, 7]); kp[:, 7, :, 15] = np.where(i < 9, last, kp[:, 7, :, 15])
    ce[:, 4, CELLS - 1] = 0; ce[:, 4, 0] = i + 1
    X[:, 4, 1] = 255 * (i < 2); X[:, 4, 2:17] = 255 * (i >= 2)
    ce[:, 5, CELLS - 1] = (W - 1) * (i == 0); ce[:, 5, 0] = (W - 1) * (i == 0); wv[:, 5] = last
    kp[:, 5] = 255 * (kp[:, 5] > 127); X[:, 5, (65025 * np.arange(17)) & (W - 1)] = 0
    ce[:, 2, CELLS - 1] = np.where(i < 15, 1 + i % 10, W - 1); ce[:, 2, CELLS - 256] = 0; wv[:, 2] = last
    X[:, 2, 1:11] = 255; X[:, 2, 1:11, 0] = 254 - np.arange(10)
    return pack(X, ce, v, z, kp, wv)
def setup_inputs_corners(rng):
    X, ce, v, z, kp, wv = parts(rng, np.full(8, 12)); T = 64
    X = np.where(rng.random(X.shape) < 0.5, rng.integers(100, 128, X.shape), rng.integers(0, 21, X.shape))
    for g in range(8):
        ba = rng.integers(128, 224, (T, 16))
        for r in range(N):
            pl = (ba @ kp[r, g]) & (W - 1); cl = (ba @ wv[r, g]) & (CELLS - 1)
            own = rng.permutation(np.setdiff1d(np.arange(W), pl))[:5 * T].reshape(5, T)
            X[r, g, own[0]] = ba
            for i in range(1, 4): X[r, g, own[i]] = ba - cut(TH1 - 2 + i)
            st = rng.permutation(np.setdiff1d(np.arange(CELLS), cl))[:T]; ce[r, g, st, rng.integers(0, 16, T)] = own[0]
            for t in range(T):
                qs = rng.permutation(16); am = int(rng.choice(np.array([0, TH2 - 1, TH2, TH2 + 1])))
                X[r, g, pl[t, qs[1]]] = ba[t] - cut(am + int(rng.integers(0, 2))); X[r, g, pl[t, qs[0]]] = ba[t] - cut(am)
                n = int(rng.choice(np.array([0, 1, 1, 2, 2, 3, 15, 16])))
                ce[r, g, cl[t]] = rng.permutation(np.concatenate([own[rng.integers(0, 2, n), t], own[rng.integers(2, 5, 16 - n), t]]))
            tl = rng.permutation(np.arange(K) % T); v[r, g] = st[tl]; z[r, g] = ba[tl]
    return pack(X, ce, v, z, kp, wv)
def setup_inputs_crowd(rng):
    fam = np.full(8, 10); fam[4] = 1
    X, ce, v, z, kp, wv = parts(rng, fam); X[:, 5] = rng.integers(0, 256, (N, W, 16))
    for g in (0, 1, 4, 5):
        v[:, g] = v[:, g, :1].copy(); z[:, g] = z[:, g, :1].copy()
    for g in (1, 5):
        for r in range(N):
            o = int(rng.choice(np.array([0, K - 1, int(rng.integers(0, K))])))
            v[r, g, o] = (v[r, g, o] + 1 + int(rng.integers(0, CELLS - 1))) % CELLS; z[r, g, o] = rng.integers(0, 256, 16)
    wv[:, 2] = 0; kp[:, 2] = 0; kp[:, 6] = 0; v[:, 3] = v[:, 3, :1].copy()
    return pack(X, ce, v, z, kp, wv)
def setup_inputs_ties(rng):
    X, ce, v, z, kp, wv = parts(rng, np.full(8, 12)); val = np.array([0, 64, 128, 255])
    for g in range(8):
        a = rng.choice(val, (12, 16)); b = rng.choice(val, (6, 8))
        pool = np.concatenate([a, a[:, ::-1], np.concatenate([b, b[:, ::-1]], axis=1)])
        X[:, g] = pool[rng.integers(0, 30, (N, W))]
    h = rng.choice(val, (N, 8, K, 8)); z = np.concatenate([h, h[..., ::-1]], axis=3)
    return pack(X, ce, v, z, kp, wv)
def check_inputs(d):
    bad = []
    for k, hi in (("px", 255), ("ce", W - 1), ("v0", CELLS - 1), ("z0", 255), ("kap", 255), ("wu", 255)):
        a = np.asarray(d[k]).astype(np.float64)
        if not (np.min(a) >= 0 and np.max(a) <= hi): bad.append("range of " + k)
        elif not np.all(a == np.floor(a)): bad.append("whole numbers in " + k)
    return bad
def ints(a):
    return a.astype(np.float32).astype(np.int64)
def first(key):
    w = np.zeros(key.shape, bool)
    for g in range(8): w[g, np.unique(key[g], return_index=True)[1]] = True
    return w
def one(a, k):
    return np.take_along_axis(a, k.reshape(8, K, *([1] * (a.ndim - 2))), 2)[:, :, 0]
def reference(px, ce, v0, z0, kap, wu):
    X = ints(px).reshape(N, 8, 16, W).transpose(0, 1, 3, 2).copy()
    C = ce.astype(np.int64).reshape(N, 8, 16, CELLS).transpose(0, 1, 3, 2).copy()
    kp = ints(kap).reshape(N, 8, 16, 16); wv = ints(wu).reshape(N, 8, 16)
    v = [gentries(a).astype(np.int64) for a in v0]; z = [a for a in ints(z0).reshape(N, 8, 16, K).transpose(0, 1, 3, 2)]
    al = [np.zeros((8, K), np.int64) for p in range(N)]
    g2 = np.arange(8)[:, None]; g3 = g2[:, :, None]; lane = np.arange(K)[None, :] + np.zeros((8, 1), np.int64)
    for t in range(RO):
        hx = []; hn = []
        for p in range(N):
            L = C[p][g2, v[p]]; x = X[p][g3, L]
            k = np.argmax(np.add.reduce(np.minimum(x, z[p][:, :, None, :]), axis=3), axis=2)
            hx.append(one(x, k)); hn.append(one(L, k))
        nv = []; nz = []; na = []; F = []; nm = []; live = []
        for p in range(N):
            o = (p - 1) % N; x = hx[o]; zz = z[o]; a = al[o]
            b = np.add.reduce(wv[p][:, None, :] * x, axis=2) & (CELLS - 1)
            M = C[p][g2, b]; y = X[p][g3, M]
            d = np.add.reduce(np.abs(y - x[:, :, None, :]), axis=3); j = np.argmin(d, axis=2)
            ex = np.add.reduce((d < TH1).astype(np.int64), axis=2) >= 2 + (a & 1)
            s = np.add.reduce(np.minimum(y, x[:, :, None, :]), axis=3); np.put_along_axis(s, j[:, :, None], -1, 2); m = np.argmax(s, axis=2)
            yj = one(y, j); Mj = one(M, j)
            F.append(np.maximum(x, one(y, m))); nm.append(one(M, m)); live.append(~ex)
            win = first(np.where(ex, Mj, W + b)); new = (yj + x) >> 1
            g, l = np.nonzero(win & ex); X[p][g, Mj[g, l]] = new[g, l]
            g, l = np.nonzero(win & ~ex); C[p][g, b[g, l], j[g, l]] = hn[o][g, l]
            nz.append(np.where(ex[:, :, None], np.abs(zz - yj), zz)); na.append(a + ex); nv.append(b)
        for p in range(N):
            o = (p - 1) % N; f = F[o]; on = live[o]
            c = (f @ kp[p]) & (W - 1); w = X[p][g3, c]
            d = np.add.reduce(np.abs(w - f[:, :, None, :]), axis=3); q = np.argmin(d, axis=2)
            rec = one(d, q) < TH2; cq = one(c, q); wq = one(w, q); cc = cq & (CELLS - 1)
            win = first(np.where(on, np.where(rec, cq, W + cc), -1 - lane)) & on; new = (wq + f) >> 1
            g, l = np.nonzero(win & rec); X[p][g, cq[g, l]] = new[g, l]
            g, l = np.nonzero(win & ~rec); C[p][g, cc[g, l], q[g, l]] = nm[o][g, l]
            nz[o] = np.where(on[:, :, None], (nz[o] + wq) >> 1, nz[o])
        v = nv; z = nz; al = na
    return {"yx": X.transpose(0, 1, 3, 2).reshape(N, 128, W).astype(np.float32).astype(BF), "yc": C.transpose(0, 1, 3, 2).reshape(N, 128, CELLS).astype(np.float32),
            "yz": np.stack(z).transpose(0, 1, 3, 2).reshape(N, 128, K).astype(np.float32).astype(BF), "yv": np.stack([gtable(a) for a in v]).astype(np.float32), "ya": np.stack(al).astype(np.float32)}

@@ -1,0 +1,625 @@
+from concourse.bass import DstId, RemoteDMATransfer
+from concourse.mybir import AluOpType, ActivationFunctionType
+
+A = AluOpType
+F = ActivationFunctionType
+N, RO = 8, 5
+XO, CO, TW, SM = 128, 4224, 5248, 5408
+MG = 12582912.0
+BIG = 16777216.0
+SEG = [8 * c * (c + 1) + 3 * c for c in range(8)]
+NL = 2 * RO
+f32, bf, i32, u16 = "float32", "bfloat16", "int32", "uint16"
+MB = ("I", "S", "SB", "S2", "nI", "nI2", "I4", "I1", "BSb", "WUm", "KP", "PM1")
+MF = ("I32", "nI32", "BO32", "BS32", "POS", "CS", "CH")
+PS = ("E0", "E1", "E2", "E3", "PD", "PX", "PM", "A0")
+CYC, PCYC, HOP = 1.04e-3, 0.52e-3, 0.06
+VCMP = (7, 6, 5, 4)
+PASSES = 8
+KEPT = {}
+CHUNKS = ((0, 256, "E3"), (256, 768, "E0"), (768, 1280, "E1"), (1280, 1664, "E2"), (1664, 1920, "E3"), (1920, 2048, "E0"))
+
+
+def _sb(w, d):
+    return ("sbuf", [128, w], d)
+
+
+SCRATCH = {
+    "TB": _sb(SM, f32), "HB": _sb(TW, f32), "HU": _sb(1184, u16), "WU": _sb(1184, u16), "CI": _sb(1032, i32), "SF": _sb(160, f32), "SH": _sb(176, bf),
+    "Y": _sb(2048, bf), "AB": _sb(2048, bf), "EP": _sb(2048, bf), "OH": _sb(2048, bf), "WD": _sb(2048, bf),
+    "MB": _sb(128 * len(MB), bf), "MF": _sb(128 * len(MF), f32),
+    "IOT": _sb(1024, f32), "CP": _sb(128, f32), "PI": _sb(8, i32), "COL": _sb(16, f32), "G8": _sb(16, f32),
+    "MASK": _sb(256, bf), "RB": _sb(256, f32), "RR": _sb(128, f32), "R0": _sb(128, f32), "RC": _sb(128, f32),
+    "GL": _sb(32, f32), "FL": _sb(2, u16), "CMP": _sb(600, bf), "CD": _sb(600, bf), "WO": _sb(600, bf),
+    "SMB": _sb(32, bf), "KS": _sb(32, f32), "VR": _sb(128, f32),
+    "vl": _sb(16, u16), "L16": _sb(128, u16), "Lf": _sb(128, f32), "rm": _sb(128, f32), "hold": _sb(128, f32), "ne": _sb(128, f32),
+    "mk": _sb(128, f32), "rm2": _sb(128, f32), "PDs": _sb(128, f32), "ti": _sb(16, i32), "tj": _sb(8, i32), "tk": _sb(8, i32), "tl": _sb(8, i32),
+    "bi": _sb(16, i32), "pos": _sb(8, u16), "posm": _sb(8, u16),
+    "bl2": _sb(8, u16), "bl4": _sb(8, u16), "key16": _sb(8, u16), "off16": _sb(8, u16), "ho16": _sb(8, u16), "a16": _sb(8, u16),
+    "tf": _sb(16, f32), "tg": _sb(8, f32), "th": _sb(8, f32), "z": _sb(128, bf), "xx": _sb(128, bf), "x1": _sb(128, bf), "TT": _sb(128, bf),
+    "yj": _sb(128, bf), "wq": _sb(128, bf), "ff": _sb(128, bf),
+    "sel": _sb(128, f32), "selm": _sb(128, f32), "nm": _sb(128, f32), "nm3": _sb(128, f32), "tt": _sb(128, f32), "ks": _sb(128, f32),
+    "Kb": _sb(128, f32), "KR": _sb(128, f32),
+    "DG": _sb(256, f32), "DK": _sb(256, f32), "LT": _sb(128, f32), "U": _sb(128, f32), "K2": _sb(256, f32), "DC": _sb(256, f32),
+    "ZC": _sb(256, f32), "K4": _sb(512, f32), "TC": _sb(512, f32), "NC": _sb(512, f32), "q1": _sb(128, f32), "q2": _sb(128, bf),
+    "q3": _sb(128, bf), "h1": _sb(128, f32), "h2": _sb(128, f32), "nb": _sb(128, f32), "t1": _sb(128, f32),
+    "exG": _sb(8, bf), "par": _sb(8, bf), "aG": _sb(8, bf),
+    "vG": _sb(8, f32), "ar": _sb(128, f32), "LG": _sb(NL * 136, f32), "HL": _sb(NL * 136, f32),
+    "PXS": ("dram", [8, 128, 512], bf), "PXL": ("dram", [8, 128, 512], bf), "CS": ("dram", [8, 128, 148], u16), "CL": ("dram", [8, 128, 148], u16),
+    "LS": ("dram", [NL * 8, 128, 17], f32), "LL": ("dram", [NL * 8, 128, 17], f32), "ZS": ("dram", [8, 128, 16], bf), "ZL": ("dram", [8, 128, 16], bf),
+    "VS": ("dram", [8, 128, 2], f32), "VL": ("dram", [8, 128, 2], f32),
+}
+for _m in PS:
+    SCRATCH[_m] = ("psum", [128, 512], f32)
+SEMAPHORES = (["qv", "qa", "qp", "qg", "ls", "dce", "dsm", "dsw", "dcs", "ac", "dwu", "dtb", "dhb", "dvs", "dvo", "av", "dzs", "az", "dout", "dyx"]
+              + ["xs%d" % k for k in range(3)] + ["ax%d" % k for k in range(8)]
+              + ["%s%d" % (p, k) for p in ("lt", "la", "lh") for k in range(NL)])
+
+
+def _mask(es):
+    m = 0
+    for e in es:
+        m |= 1 << e
+    return m
+
+
+def _calls(src, cores, topo):
+    me = cores.index(src)
+    kinds = {"on": [], "mate": [], "plane": [], "far": []}
+    for k in range(1, N):
+        r = (me + k) % N
+        a, b = topo.chip(src), topo.chip(cores[r])
+        kinds["on" if a == b else "mate" if topo.mates(a, b) else "plane" if topo.same_plane(a, b) else "far"].append(r)
+    for k in ("mate", "plane", "far"):
+        kinds[k].sort(key=lambda r: topo.die(cores[r]) != topo.die(src))
+    off = topo.engines(src, cores[kinds["far"][0]])
+    on = [e for e in topo.engines(src, cores[kinds["on"][0]]) if e not in off]
+    h = len(off) // 2
+    lo, hi = off[:h], off[h:]
+    calls = [[(kinds["far"][0], lo), (kinds["far"][1], hi), (kinds["on"][0], on)],
+             [(kinds["mate"][0], lo), (kinds["plane"][0], hi)], [(kinds["mate"][1], lo), (kinds["plane"][1], hi)]]
+    outs = kinds["far"] + kinds["plane"] + kinds["mate"]
+    single = [(r, [off[i]]) for i, r in enumerate(outs)] + [(kinds["on"][0], [on[0]])]
+    return calls, single
+
+
+def _order(ops):
+    n = len(ops)
+    if n not in KEPT:
+        pred = [sorted(o["deps"]) for o in ops]
+        succ = [[] for _ in ops]
+        for i in range(n):
+            for d in pred[i]:
+                succ[d].append(i)
+        prio = [0.0] * n
+        for i in range(n - 1, -1, -1):
+            prio[i] = ops[i]["lat"] + max([prio[s] + HOP for s in succ[i]] + [0.0])
+        best = None
+        for _ in range(PASSES):
+            out, fin = _pass(ops, pred, succ, prio, False)
+            if best is None or max(fin) < best[0]:
+                best = (max(fin), out)
+            prio = _pass(ops, succ, pred, fin, True)[1]
+        KEPT[n] = best[1]
+    return KEPT[n]
+
+
+def _pass(ops, pred, succ, prio, back):
+    n = len(ops)
+    left = [len(p) for p in pred]
+    ready = {i: 0.0 for i in range(n) if not left[i]}
+    at, fin, free, out = [0.0] * n, [0.0] * n, {}, []
+    while ready:
+        best = min(ready, key=lambda i: max(ready[i], free.get(ops[i]["q"], 0.0)) + ops[i]["hold"])
+        q = ops[best]["q"]
+        end = max(ready[best], free.get(q, 0.0)) + ops[best]["hold"]
+        i = max((j for j in ready if ops[j]["q"] == q and (ready[j] < end or j == best)), key=lambda j: (prio[j], -j))
+        st = max(ready.pop(i), free.get(q, 0.0))
+        free[q] = st + ops[i]["hold"]
+        fin[i] = st + (ops[i]["hold"] if back else ops[i]["lat"])
+        out.append(i)
+        for s in succ[i]:
+            a, b = (s, i) if back else (i, s)
+            gap = 0.0 if b in ops[a]["soft"] else ops[a]["lat"] - ops[a]["hold"] + HOP
+            at[s] = max(at[s], st + ops[i]["hold"] + gap)
+            left[s] -= 1
+            if not left[s]:
+                ready[s] = at[s]
+    return out, fin
+
+
+def rank_program(g, core, T, topo):
+    rank = T.rank_of(core)
+    if rank is None:
+        return
+    cores = list(T.cores)
+    Q = {"v": g.vector, "a": g.scalar, "p": g.tensor, "g": g, "s": g.sync}
+    V, S_, P = g.vector, g.scalar, g.tensor
+    ops, hist, bysem = [], {}, {}
+
+    def r(name, lo=0, hi=None, st=1):
+        hi = SCRATCH[name][1][1] if hi is None else hi
+        return (T[name][:, lo:hi:st] if st != 1 else T[name][:, lo:hi], name, lo, hi, len(range(lo, hi, st)))
+
+    def ind(win, off):
+        return (win[0].indirect(off[0]), win[1], win[2], win[3], 16 * off[4], off)
+
+    def dr(name, lo, hi):
+        return (None, name, lo, hi, 0)
+
+    def op(q, fn, rd, wr, hold, lat=None, sem=None, pre=(), after=()):
+        me_ = len(ops)
+        acc = []
+        for x, w in [(x, False) for x in rd] + [(x, True) for x in wr]:
+            if len(x) > 5:
+                acc.append((x[5][1], x[5][2], x[5][3], False))
+            acc.append((x[1], x[2], x[3], w))
+        deps, soft = set(), set(after)
+        for name, lo, hi, w in acc:
+            for e in hist.get(name, []):
+                hit = lo < e[1] and e[0] < hi and (w or e[2])
+                if name in PS and ops[e[3]]["q"] == q == "p":
+                    soft.add(e[3])
+                elif hit or (name in PS and ops[e[3]]["q"] != q):
+                    deps.update(bysem.get(ops[e[3]]["sem"], [e[3]]))
+        if sem:
+            deps -= set(bysem.get(sem, []))
+            bysem.setdefault(sem, []).append(me_)
+        soft -= deps
+        for d in soft:
+            ops[d]["soft"].add(me_)
+        ops.append({"q": q, "fn": fn, "deps": deps | soft, "wait": deps, "soft": set(), "hold": hold, "lat": lat or hold, "sem": sem, "pre": pre})
+        for name, lo, hi, w in acc:
+            h = hist.get(name, [])
+            if name in PS:
+                if q == "p":
+                    h = []
+                elif h and ops[h[-1][3]]["q"] != q:
+                    h = [e for e in h if ops[e[3]]["q"] == ops[h[-1][3]]["q"]]
+            elif w:
+                h = [e for e in h if not (lo <= e[0] and e[1] <= hi) or (sem and ops[e[3]]["sem"] == sem)]
+            h.append((lo, hi, w, me_))
+            hist[name] = h
+        return me_
+
+    def vcost(o, ins):
+        if len(o) > 5:
+            return 0.05 + 3.8 * o[4] * CYC
+        if any(len(x) > 5 for x in ins):
+            return 0.05 + 1.56 * o[4] * CYC
+        two = all(SCRATCH[x[1]][2] in (bf, u16) for x in [o] + ins)
+        return 0.03 + max(64, o[4] * (0.5 if two else 1)) * CYC
+
+    def cp(o, i):
+        op("v", lambda: V.tensor_copy(o[0], i[0]), [i], [o], vcost(o, [i]))
+
+    def tt(o, a, b, f):
+        op("v", lambda: V.tensor_tensor(o[0], a[0], b[0], f), [a, b], [o], vcost(o, [a, b]))
+
+    def ts(o, a, s1, f1, s2=None, f2=None):
+        cols = [s for s in (s1, s2) if isinstance(s, tuple)]
+        x1 = s1[0] if isinstance(s1, tuple) else s1
+        x2 = s2[0] if isinstance(s2, tuple) else s2
+        if f2 is None:
+            op("v", lambda: V.tensor_scalar(o[0], a[0], x1, None, f1), [a] + cols, [o], vcost(o, [a]))
+        else:
+            op("v", lambda: V.tensor_scalar(o[0], a[0], x1, x2, f1, f2), [a] + cols, [o], vcost(o, [a]))
+
+    def scan(o, d0, d1, init, f0, f1):
+        op("v", lambda: V.tensor_tensor_scan(o[0], d0[0], d1[0], init, f0, f1), [d0, d1], [o], vcost(o, [d0, d1]))
+
+    def ms(o, c):
+        op("v", lambda: V.memset(o[0], c), [], [o], vcost(o, []))
+
+    def act(o, i, f=F.Identity, bias=0.0, scale=1.0):
+        cols = [bias] if isinstance(bias, tuple) else []
+        b = bias[0] if cols else bias
+        op("a", lambda: S_.activation(o[0], i[0], f, bias=b, scale=scale), [i] + cols, [o], 0.1 + o[4] * (1.56 if len(i) > 5 else 1) * CYC)
+
+    def mm(o, l, rh, start, stop):
+        c = max(64, rh[4]) * (4 if SCRATCH[l[1]][2] == f32 else 1) * PCYC
+        op("p", lambda: P.matmul(o[0], l[0], rh[0], start, stop), [l, rh], [o], c, c + 0.1)
+
+    def mms(o, pairs):
+        for k, (l, rh) in enumerate(pairs):
+            mm(o, l, rh, k == 0, k == len(pairs) - 1)
+
+    def dma(q, o, i, sem, rd=(), wr=(), lat=2.2, pre=(), after=(), **kw):
+        return op(q, lambda: Q[q].dma_start(o, i, **kw), list(rd), list(wr), 1.0 if q == "g" else 0.1, lat, sem, pre, after)
+
+    sent = [0]
+
+    def remote(plan, src, dst, sem, rd, hold=4.0, after=()):
+        tr = []
+        for d, es in plan:
+            rid, pid, _ = topo.addr(cores[d])
+            tr.append(RemoteDMATransfer(dst_ids=[DstId(rid=rid, pnc=pid)], dma_engine_mask=_mask(es), remote_sem=T.sem[sem],
+                                        src=src(d), dst=dst))
+            sent[0] += len(es)
+        a = op("g", lambda: g.remote_dma_fused(tr, local_sem=T.sem.ls), rd, [], 1.0, None, "", (), after)
+        return a, op("link", None, [], [], hold, None, "", (), [a])
+
+    def m(n, lo=0, hi=128, st=1):
+        buf, k = ("MB", MB.index(n)) if n in MB else ("MF", MF.index(n))
+        return r(buf, 128 * k + lo, 128 * k + hi, st)
+
+    rot = [0]
+
+    def bank(w=128, pool=("E0", "E1", "E2", "E3", "A0")):
+        rot[0] += 1
+        return r(pool[rot[0] % len(pool)], 0, w)
+
+    calls, single = _calls(core, cores, topo)
+    me = slice(16 * rank, 16 * rank + 16)
+    XW, CW, AW = r("TB", XO, CO), r("TB", CO, TW), r("TB", 0, TW)
+
+    dma("a", T.CI[:, 0:1024], T.ce[:], "dce", wr=[r("CI", 0, 1024)], lat=3.5)
+    dma("a", T.CI[:, 1024:1032], T.v0[:], "dce", wr=[r("CI", 1024, 1032)])
+    last_s = []
+    for k, cl in enumerate(calls):
+        for d, _ in cl:
+            last_s = [dma("s", T.PXS[d], T.px[16 * d:16 * d + 16, :], "xs%d" % k, wr=[dr("PXS", k, k + 1)], after=last_s)]
+    dma("a", T.SH[:, 0:128], T.z0[:], "dsm", wr=[r("SH", 0, 128)])
+    dma("a", T.SH[:, 128:144], T.kap[:], "dsm", wr=[r("SH", 128, 144)])
+    dma("g", T.SH[:, 160:161], T.wu[:], "dsw", wr=[r("SH", 160, 161)], allow_slow_non_contiguous=True)
+    cp(r("SF", 0, 144), r("SH", 0, 144))
+    cp(r("SF", 144, 145), r("SH", 160, 161))
+    op("g", lambda: g.iota(T.PI[:, 0:1], [[0, 1]], 0, 1), [], [r("PI", 0, 1)], 0.15)
+    op("g", lambda: g.iota(T.CP[:], [[1, 128]], 0, -1, allow_small_or_imprecise_dtypes=True), [], [r("CP")], 0.4)
+    op("g", lambda: g.iota(T.IOT[:, 0:128], [[1, 128]], 0, 0, allow_small_or_imprecise_dtypes=True), [], [r("IOT", 0, 128)], 0.4)
+    ms(r("HU", 1168, 1184), 0)
+    cp(r("HU", 0, 1032), r("CI"))
+    cp(r("HU", 1032, 1177), r("SF", 0, 145))
+    dma("a", T.CS[:], T.HU[:], "dcs", rd=[r("HU")], wr=[dr("CS", 0, 1)], lat=3.0)
+    dma("a", T.CL[rank], T.HU[me, :], "dcs", rd=[r("HU")], wr=[dr("CL", 0, 1)])
+    ax = "ax%d" % rank
+    c0, l0 = remote(calls[0], lambda d: T.PXS[d], T.PXL[rank], ax, [dr("PXS", 0, 1)], 5.0)
+    c1, l1 = remote(calls[1], lambda d: T.PXS[d], T.PXL[rank], ax, [dr("PXS", 1, 2)], 3.5, [c0])
+    cc, lc = remote(single, lambda d: T.CS[d], T.CL[rank], "ac", [dr("CS", 0, 1)], 2.0, [c1])
+    c2, l2 = remote(calls[2], lambda d: T.PXS[d], T.PXL[rank], ax, [dr("PXS", 2, 3)], 3.5, [cc])
+    dma("s", T.WU[:], T.CL[:], "dwu", rd=[dr("CL", 0, 1)], wr=[r("WU")], lat=3.0, pre=[("ac", N - 1)], after=[lc])
+    lg_ = dma("g", T.TB[me, XO:CO], T.px[me, :], "dtb", wr=[XW], after=[c2])
+    for k in range(3):
+        for s in range(N):
+            if s != rank:
+                for d, es in _calls(cores[s], cores, topo)[0][k]:
+                    if d == rank:
+                        lg_ = dma("g", T.TB[16 * s:16 * s + 16, XO:CO], T.PXL[s], "dtb", wr=[XW], lat=3.0, pre=[("ax%d" % s, len(es))],
+                                  after=[lg_, (l0, l1, l2)[k]])
+    dma("g", T.HB[:, XO:CO], T.px[:], "dhb", wr=[r("HB", XO, CO)], lat=9.0, after=[lg_])
+
+    ts(r("PI", 2, 3), r("PI", 0, 1), 15, A.bitwise_and)
+    ts(r("PI", 4, 5), r("PI", 0, 1), 4, A.arith_shift_right)
+    acol, gcol = r("COL", 0, 1), r("COL", 1, 2)
+    cp(acol, r("PI", 2, 3))
+    cp(gcol, r("PI", 4, 5))
+    ts(m("I32"), r("CP"), 0.0, A.is_equal)
+    cp(m("I"), m("I32"))
+    ts(r("G8", 0, 8), r("IOT", 0, 8), gcol, A.is_equal)
+    ts(r("OH", 0, 16), r("IOT", 0, 16), acol, A.is_equal)
+    for w in (128, 256, 512):
+        act(r("IOT", w, 2 * w), r("IOT", 0, w), bias=float(w))
+
+    def roll(dst, src, k):
+        act(m(dst, k, 128), m(src, 0, 128 - k))
+        act(m(dst, 0, k), m(src, 128 - k, 128))
+    roll("S", "I", 16)
+    roll("SB", "I", 112)
+    for k in range(8):
+        act(m("PM1", k, 128, 8), m("I", 16 * k, 16 * k + 16))
+    for k in range(16):
+        act(r("EP", k, 2048, 16), m("PM1"))
+    w = 16
+    while w < 2048:
+        cp(r("OH", w, 2 * w), r("OH", 0, w))
+        w *= 2
+    for k in range(16):
+        cp(m("BO32", k, 128, 16), r("G8", 0, 8))
+    roll("BS32", "BO32", 16)
+    act(m("BSb"), m("BS32"))
+    act(r("G8", 9, 16), r("G8", 0, 7))
+    act(r("G8", 8, 9), r("G8", 7, 8))
+    for nme, src, sc in (("S2", "S", 2.0), ("nI", "I", -1.0), ("nI2", "I", -2.0), ("I4", "I", -4096.0), ("I1", "I", -1024.0), ("nI32", "I32", -1.0)):
+        act(m(nme), m(src), scale=sc)
+    ms(r("WD"), 0.0)
+    for k in range(16):
+        ts(r("WD", 128 * k + k, 128 * k + 128, 16), r("G8", 0, 8), 2048.0, A.mult)
+    ts(r("MASK"), r("OH", 0, 256), -2097152.0, A.mult, 2097152.0, A.add)
+    ts(r("COL", 2, 3), acol, 128.0, A.mult)
+    ts(m("POS"), r("IOT", 0, 128), r("COL", 2, 3), A.add)
+    ms(m("CS"), 8388608.0 + 2047.0)
+    ms(m("CH"), -2047.5)
+    for nme, v0, vs, at in (("RB", 0.0, BIG, 0), ("RR", 0.0, BIG, 15), ("R0", 1.0, 0.0, 0)):
+        ms(r(nme), v0)
+        ms(r(nme, at, None, 16), vs)
+    ms(r("RC"), -BIG)
+    lane, l64, l4, th = r("GL", 0, 8), r("GL", 8, 16), r("GL", 16, 24), r("GL", 24, 32)
+    ts(lane, r("IOT", 0, 128, 16), acol, A.add)
+    ts(l64, lane, 64.0, A.mult)
+    ts(l4, lane, 4.0, A.mult)
+    ts(th, lane, 64.0, A.mult, 13.0, A.add)
+    ts(r("COL", 4, 5), acol, 8.0, A.mult, 27.0, A.add)
+    ts(r("COL", 5, 6), r("COL", 4, 5), acol, A.mult, 18.0, A.add)
+    ts(r("FL", 0, 1), r("COL", 5, 6), 599.0, A.min)
+    ms(r("CMP"), 1.0)
+    ms(r("CD"), 0.0)
+    for c in range(8):
+        ms(r("CD", SEG[c], SEG[c] + 1), 1.0)
+        ms(r("CD", SEG[c] + 18 + 16 * c, SEG[c] + 19 + 16 * c), 2.0)
+        ts(r("CD", SEG[c] + 1 + 16 * c, SEG[c] + 17 + 16 * c), r("OH", 0, 16), -2.0, A.mult)
+    for nme in ("DK", "TC", "NC", "par", "aG"):
+        ms(r(nme), 0.0)
+    ms(r("TB", 0, XO), 0.0)
+    ms(r("HB", 0, XO), 0.0)
+    ms(r("K4"), 0.0)
+    cp(r("K4", 2, 512, 4), r("IOT", 0, 128))
+    cp(r("K4", 3, 512, 4), r("IOT", 0, 128))
+
+    cp(r("TB", TW, SM), r("WU", 1024, 1184))
+    cp(r("vl", 0, 8), r("TB", TW, TW + 8))
+    cp(r("z"), r("TB", TW + 8, TW + 136))
+    cp(r("SMB", 0, 17), r("TB", TW + 136, TW + 153))
+    cp(CW, r("WU", 0, 1024))
+    z, x, x1, f = r("z"), r("xx"), r("x1"), r("ff")
+    nat, per, oh, Y = r("vl", 0, 8), r("vl", 8, 16), r("OH"), r("Y")
+    AX = ("A0", "PX")
+
+    def turn(src, sh):
+        b = r("A0", 0, 128)
+        mm(b, src, sh, True, True)
+        act(r("TT"), b, scale=-1.0)
+
+    def permuted(o, l, src, stop):
+        for k in range(8):
+            mm(r(o[1], o[2] + k, o[2] + 128, 8), l, r(src, 16 * k, 16 * k + 16), False, stop and k == 7)
+
+    def spread(l, src):
+        mm(r("PM", 0, 256), m("I"), r("MASK"), True, False)
+        mm(r("PM", 0, 128), l, r(src), False, False)
+        permuted(r("PM", 128, 256), l, src, True)
+        scan(r("DG"), r("RB"), r("PM", 0, 256), 0.0, A.add, A.min)
+
+    act(r("VR"), ind(r("IOT"), nat))
+    spread(m("I32"), "VR")
+    cp(per, r("DG", 143, 256, 16))
+    b = bank(17)
+    mm(b, m("SB"), r("SMB", 0, 17), True, True)
+    act(r("KS", 0, 17), b)
+    ts(m("WUm"), m("BSb"), r("KS", 16, 17), A.mult)
+    for k in range(8):
+        ts(m("KP", 16 * k, 16 * k + 16), r("KS", 0, 16), r("G8", 8 + k, 9 + k), A.mult)
+    turn(z, m("I"))
+
+    def probe(func, scale, sums):
+        mm(r("PD", 0, 128), m("I32"), m("POS"), True, False)
+        if sums:
+            mm(r("PX", 0, 128), m("I32"), m("CS"), True, False)
+        for lo, hi, e in CHUNKS:
+            b = r(e, 0, hi - lo)
+            src = ind(XW, r("L16", lo // 16, hi // 16))
+            (act if lo == 0 else cp)(r("Y", lo, hi), src)
+            mms(b, [(r("TT"), r("EP", lo, hi)), (m("I"), r("Y", lo, hi))])
+            act(r("AB", lo, hi), b, func, scale=scale)
+            for a in range(lo // 128, hi // 128):
+                mm(r("PD", 0, 128), r("WD", 128 * a, 128 * a + 128), r("AB", 128 * a, 128 * a + 128), False, a == 15)
+                if sums:
+                    mm(r("PX", 0, 128), r("WD", 128 * a, 128 * a + 128), r("Y", 128 * a, 128 * a + 128), False, False)
+        scan(r("rm"), r("RB", 0, 128), r("PD", 0, 128), 0.0, A.add, A.min)
+
+    def decode(out, src, t0, t1, flip=False):
+        cp(r(t0, 0, 8), r(src, 15, 128, 16))
+        ts(r(t1), r(t0, 0, 8), 2047, A.bitwise_and)
+        if flip:
+            ts(out, r(t1), -1.0, A.mult, 2047.0, A.add)
+        else:
+            cp(out, r(t1))
+
+    def send_log(s):
+        lg = r("LG", 136 * s, 136 * s + 136)
+        sem = "lt%d" % s
+        dma("s", T.LS[8 * s:8 * s + 8], lg[0], sem, rd=[lg], wr=[dr("LS", s, s + 1)])
+        dma("s", T.LL[8 * s + rank], T.LG[me, 136 * s:136 * s + 136], sem, rd=[lg], wr=[dr("LL", s, s + 1)])
+        _, l = remote(single, lambda d: T.LS[8 * s + d], T.LL[8 * s + rank], "la%d" % s, [dr("LS", s, s + 1)], 3.5)
+        hl = r("HL", 136 * s, 136 * s + 136)
+        late = [l] if s >= NL - 2 else [op("link2", None, [], [], 3.0, None, "", (), [l])]
+        dma("s", hl[0], T.LL[8 * s:8 * s + 8], "lh%d" % s, rd=[dr("LL", s, s + 1)], wr=[hl], pre=[("la%d" % s, N - 1)], after=late)
+        for k in range(4 * (s == 0)):
+            cp(r("HB", CO + 256 * k, CO + 256 * k + 256), r("CI", 256 * k, 256 * k + 256))
+        cp(r("ho16"), r("HL", 136 * s + 128, 136 * s + 136))
+        cp(ind(r("HB"), r("ho16")), r("HL", 136 * s, 136 * s + 128))
+
+    def keys():
+        mm(r("PM", 0, 128), m("I"), r("MASK", 0, 128), True, False)
+        mm(r("PM", 0, 128), m("BO32"), r("ks"), False, True)
+        b = bank()
+        mm(b, m("BO32"), r("ks"), True, True)
+        act(r("KR"), b)
+        scan(r("DK", 0, 128), r("RB", 0, 128), r("PM", 0, 128), 0.0, A.add, A.min)
+        for c in range(7, -1, -1):
+            o, i, own = r("CMP", SEG[c] + 2, SEG[c] + 18 + 16 * c), r("KR", 0, 16 * c + 16), r("DK", 16 * c + 15, 16 * c + 16)
+            if c in VCMP:
+                ts(o, i, own, A.not_equal)
+            else:
+                act(o, i, F.Abs, bias=own, scale=-1.0)
+
+    def winners(s):
+        scan(r("WO"), r("CMP"), r("CD"), 1.0, A.min, A.add)
+        tt(r("tf"), ind(r("WO"), r("FL", 0, 1)), r("DK", 15, 256, 16), A.mult)
+        o = r("LG", 136 * s + 128, 136 * s + 136)
+        tt(o, r("tf", 0, 8), lane, A.max)
+        if s < NL - 1:
+            cp(r("off16"), o)
+
+    def rev(n):
+        return (T[n][:, 127::-1], n, 0, 128, 128)
+
+    k0, k4 = r("K2", 0, 256, 2), r("K4", 0, 512, 4)
+    for t in range(RO):
+        last = t == RO - 1
+        cp(r("L16"), ind(CW, per))
+        act(r("Lf"), ind(CW, nat))
+        b = bank(8, AX)
+        mms(b, [(m("S"), r("par")), (m("I32"), l64)])
+        act(r("RC", 0, 128, 16), b)
+        probe(F.Relu, -1.0, False)
+        decode(r("pos"), "rm", "ti", "tj")
+        cp(x, ind(Y, r("pos")))
+        tt(r("sel"), ind(oh, r("pos")), r("Lf"), A.mult)
+        spread(m("WUm"), "xx")
+        turn(x, m("S"))
+        cp(r("ti"), r("DG", 15, 256, 16))
+        ts(r("bi"), r("ti"), 1023, A.bitwise_and)
+        cp(r("vl"), r("bi"))
+        cp(r("L16"), ind(CW, per))
+        b = r("A0", 0, 128)
+        mm(b, m("S"), x, True, True)
+        act(x1, b)
+        act(k0, ind(CW, nat), bias=float(XO))
+        act(r("K2", 1, 256, 2), ind(r("IOT"), nat), bias=float(CO))
+        mms(b, [(m("BS32"), r("sel")), (m("nI32"), k0)])
+        act(r("nm"), b, bias=float(XO))
+        probe(F.Abs, 1.0, True)
+        act(r("LT"), r("PD", 0, 128), F.Sign, bias=-(240 * 2048 - 0.5))
+        act(r("PDs"), r("PD", 0, 128))
+        mm(r("PX", 0, 128), m("nI32"), r("PDs"), False, True)
+        decode(r("pos"), "rm", "ti", "tj")
+        scan(r("U"), r("RC"), r("LT"), -BIG, A.max, A.add)
+        ts(r("bl2"), r("U", 15, 128, 16), 3.0, A.add, 1.0 / 32, A.mult)
+        act(r("Kb"), ind(r("K2"), r("bl2")))
+        act(r("yj"), ind(Y, r("pos")))
+        scan(rev("hold"), rev("RR"), rev("rm"), 0.0, A.add, A.min)
+        tt(r("ne"), r("PDs"), r("hold"), A.not_equal)
+        tt(r("mk"), r("PX", 0, 128), r("ne"), A.mult)
+        scan(r("rm2"), r("R0"), r("mk"), 0.0, A.mult, A.max)
+        decode(r("posm"), "rm2", "tk", "tl", True)
+        tt(f, ind(Y, r("posm")), x1, A.max)
+        tt(r("ks"), ind(oh, r("pos")), r("Kb"), A.mult)
+        bq = r("PX", 0, 128)
+        mm(bq, m("I32"), m("CH"), True, False)
+        permuted(bq, m("KP"), "ff", True)
+        act(r("q1"), bq, bias=MG, scale=1.0 / 4096)
+        act(r("q2"), r("q1"), bias=-MG)
+        keys()
+        tt(r("tt"), ind(oh, r("pos")), r("nm"), A.mult)
+        b, b2, b3 = r("PD", 0, 128), r("PD", 128, 256), r("PD", 256, 384)
+        mms(b, [(m("I"), x1), (m("I"), r("yj"))])
+        mms(b3, [(m("S"), z), (m("nI"), r("yj"))])
+        mms(b2, [(m("I32"), k0), (m("I32"), r("tt"))])
+        act(r("DC", 0, 256, 2), b, bias=MG, scale=0.4995)
+        act(r("DC", 1, 256, 2), b2, bias=MG - XO)
+        act(r("h1"), b3, F.Abs)
+        act(r("ZC", 0, 256, 2), r("h1"), bias=MG)
+        lg = r("LG", 136 * 2 * t, 136 * 2 * t + 128)
+        act(lg, ind(r("DC"), r("bl2")), bias=-MG)
+        winners(2 * t)
+        turn(f, m("S"))
+        mm(r("PM", 0, 128), m("I4"), r("q2"), True, False)
+        permuted(r("PM", 0, 128), m("KP"), "ff", True)
+        cp(r("L16"), r("PM", 0, 128))
+        cp(ind(AW, r("off16")), lg)
+        send_log(2 * t)
+        tt(r("exG"), r("U", 15, 128, 16), th, A.is_lt)
+        tt(r("selm"), ind(oh, r("posm")), k0, A.mult)
+        if last:
+            cp(r("vG"), r("bi", 0, 8))
+        b = r("PX", 0, 128)
+        mm(b, m("KP"), f, True, False)
+        for k in range(8):
+            mm(r("PX", 16 * k, 16 * k + 16), m("I4"), r("q2", k, 128, 8), False, k == 7)
+        act(k4, b, bias=float(XO))
+        act(r("q3"), k4, bias=192 - 639.5 / 1024, scale=1.0 / 1024)
+        b = r("A0", 0, 128)
+        mm(b, m("BS32"), r("selm"), True, True)
+        act(r("nm3"), b, bias=-float(XO))
+        b = r("PX", 0, 128)
+        mms(b, [(m("I32"), k4), (m("I1"), r("q3"))])
+        act(r("K4", 1, 512, 4), b, bias=196608.0 + CO - XO)
+        l4e = r("PM", 0, 8)
+        mms(l4e, [(m("I32"), l4), (m("S2"), r("exG"))])
+        mms(r("A0", 0, 8), [(m("S"), r("par")), (m("nI2"), r("exG"))])
+        mms(r("A0", 8, 16), [(m("S"), r("aG")), (m("I"), r("exG"))])
+        act(r("par"), r("A0", 0, 8), F.Abs)
+        act(r("aG"), r("A0", 8, 16))
+        if last:
+            cp(r("a16"), r("aG"))
+            act(r("ar"), ind(r("IOT"), r("a16")))
+            dma("s", T.VS[:, 0:64, :], T.vG[:], "dvs", rd=[r("vG")], wr=[dr("VS", 0, 1)])
+            dma("s", T.VS[:, 64:128, :], T.ar[0:128:16, :], "dvs", rd=[r("ar")], wr=[dr("VS", 0, 1)])
+            _, l = remote(single, lambda d: T.VS[d], T.VL[rank], "av", [dr("VS", 0, 1)])
+            dma("s", T.VL[rank], T.VS[rank], "dvo", rd=[dr("VS", 0, 1)], wr=[dr("VL", 0, 1)])
+            dma("s", T.yv[:], T.VL[:, 0:64, :], "dout", rd=[dr("VL", 0, 1)], pre=[("av", N - 1)], after=[l])
+            dma("s", T.ya[:], T.VL[:, 64:128, :], "dout", rd=[dr("VL", 0, 1)], pre=[("av", N - 1)], after=[l])
+        probe(F.Abs, 1.0, False)
+        ts(r("th"), r("rm", 15, 128, 16), 640.0 * 2048, A.is_ge)
+        tt(r("tg"), l4e, r("th"), A.add)
+        cp(r("bl4"), r("tg"))
+        act(r("Kb"), ind(r("K4"), r("bl4")))
+        decode(r("pos"), "rm", "ti", "tj")
+        act(r("wq"), ind(Y, r("pos")))
+        tt(r("ks"), ind(oh, r("pos")), r("Kb"), A.mult)
+        keys()
+        tt(r("TC", 1, 512, 4), ind(oh, r("pos")), r("nm3"), A.mult)
+        bz, bh = r("PX", 0, 128), r("PD", 0, 128)
+        mms(bh, [(m("S"), f), (m("I"), r("wq"))])
+        mms(bz, [(m("S"), z), (m("SB"), r("wq"))])
+        act(r("NC", 1, 512, 4), ind(oh, r("pos")), bias=1.0, scale=-1.0)
+        cp(r("key16"), r("DK", 15, 128, 16))
+        act(r("nb"), ind(r("NC"), r("bl4")))
+        act(r("h2"), bh, bias=MG, scale=0.4995)
+        act(r("TC", 0, 512, 4), r("h2"), bias=-MG)
+        act(r("t1"), ind(r("TC"), r("bl4")))
+        winners(2 * t + 1)
+        tt(r("tt"), ind(AW, r("key16")), r("nb"), A.mult)
+        lg = r("LG", 136 * (2 * t + 1), 136 * (2 * t + 1) + 128)
+        act(r("ZC", 1, 256, 2), bz, bias=MG, scale=0.4995)
+        act(z, ind(r("ZC"), r("bl2")), bias=-MG)
+        if last:
+            tt(lg, r("tt"), r("t1"), A.add)
+        else:
+            tt(ind(AW, r("off16")), r("tt"), r("t1"), A.add)
+            turn(z, m("I"))
+            b = r("PM", 0, 128)
+            mms(b, [(m("I32"), r("tt")), (m("I32"), r("t1"))])
+            act(lg, b)
+        send_log(2 * t + 1)
+
+    dma("a", T.ZS[:], T.z[:], "dzs", rd=[z], wr=[dr("ZS", 0, 1)])
+    dma("a", T.ZL[rank], T.z[me, :], "dzs", rd=[z], wr=[dr("ZL", 0, 1)])
+    _, l = remote(single, lambda d: T.ZS[d], T.ZL[rank], "az", [dr("ZS", 0, 1)], 0.5)
+    dma("a", T.yz[:], T.ZL[:], "dout", rd=[dr("ZL", 0, 1)], pre=[("az", N - 1)], after=[l])
+    dma("g", T.yx[:], T.HB[:, XO:CO], "dyx", rd=[r("HB")], lat=6.0)
+    dma("s", T.yc[:], T.HB[:, CO:TW], "dout", rd=[r("HB")], lat=4.0)
+
+    cnt, waited, done = {}, {}, {}
+
+    def wait(q, sem, val):
+        if waited.get((q, sem), 0) < val:
+            Q[q].wait_ge(T.sem[sem], val)
+            waited[(q, sem)] = val
+
+    needed = set()
+    for o in ops:
+        needed |= o["wait"]
+    for i in _order(ops):
+        o = ops[i]
+        if o["fn"] is None:
+            continue
+        need = dict(o["pre"])
+        for d in o["wait"]:
+            s, val = done[d]
+            need[s] = max(need.get(s, 0), val)
+        for s in sorted(need):
+            wait(o["q"], s, need[s])
+        ins = o["fn"]()
+        if o["sem"]:
+            cnt[o["sem"]] = cnt.get(o["sem"], 0) + 16
+            ins.then_inc(T.sem[o["sem"]], 16)
+            done[i] = (o["sem"], 16 * len(bysem[o["sem"]]))
+        elif o["sem"] is None and i in needed:
+            s = "q" + o["q"]
+            cnt[s] = cnt.get(s, 0) + 1
+            ins.then_inc(T.sem[s], 1)
+            done[i] = (s, cnt[s])
+    cnt["ls"] = sent[0]
+    for s in sorted(cnt):
+        wait("g", s, cnt[s])

@@ -10,13 +10,14 @@ BIG = 16777216.0
 SEG = [8 * c * (c + 1) + 3 * c for c in range(8)]
 NL = 2 * RO
 f32, bf, i32, u16 = "float32", "bfloat16", "int32", "uint16"
-MB = ("I", "S", "SB", "S2", "nI", "nI2", "I4", "I1", "BSb", "WUm", "KP", "PM1")
-MF = ("I32", "nI32", "BO32", "BS32", "POS", "CS", "CH")
+MB = ("I", "S", "SB", "S2", "nI", "nI2", "I4", "I1", "BSb", "WUm", "KP", "PM1", "POS", "CH")
+MF = ("I32", "BO32", "BS32")
 PS = ("E0", "E1", "E2", "E3", "PD", "PX", "PM", "A0")
-CYC, PCYC, HOP = 1.04e-3, 0.52e-3, 0.06
+CYC, PCYC, HOP = 0.92e-3, 0.55e-3, 0.11
 VCMP = (7, 6, 5, 4)
 PASSES = 8
 KEPT = {}
+TRIES = 900
 CHUNKS = ((0, 256, "E3"), (256, 768, "E0"), (768, 1280, "E1"), (1280, 1664, "E2"), (1664, 1920, "E3"), (1920, 2048, "E0"))
 
 
@@ -25,7 +26,7 @@ def _sb(w, d):
 
 
 SCRATCH = {
-    "TB": _sb(SM, f32), "HB": _sb(TW, f32), "HU": _sb(1184, u16), "WU": _sb(1184, u16), "CI": _sb(1032, i32), "SF": _sb(160, f32), "SH": _sb(176, bf),
+    "TB": _sb(SM, f32), "HB": _sb(TW, f32), "HU": _sb(1184, u16), "WU": _sb(1184, u16), "CI": _sb(1032, i32), "SF": _sb(160, f32), "SH": _sb(176, bf), "EX": _sb(2048, bf), "GB": _sb(16, bf), "fr": _sb(128, bf),
     "Y": _sb(2048, bf), "AB": _sb(2048, bf), "EP": _sb(2048, bf), "OH": _sb(2048, bf), "WD": _sb(2048, bf),
     "MB": _sb(128 * len(MB), bf), "MF": _sb(128 * len(MF), f32),
     "IOT": _sb(1024, f32), "CP": _sb(128, f32), "PI": _sb(8, i32), "COL": _sb(16, f32), "G8": _sb(16, f32),
@@ -98,8 +99,20 @@ def _order(ops):
         for _ in range(PASSES):
             out, fin = _pass(ops, pred, succ, prio, False)
             if best is None or max(fin) < best[0]:
-                best = (max(fin), out)
+                best = (max(fin), out, prio)
             prio = _pass(ops, succ, pred, fin, True)[1]
+        labs = sorted(set(o["lab"] for o in ops if o["lab"][0]))
+        bias, seed = {}, 12345
+        for _ in range(TRIES):
+            new = dict(bias)
+            for _k in range(3):
+                seed = (seed * 1103515245 + 12345) % 2147483648
+                lab = labs[(seed >> 8) % len(labs)]
+                seed = (seed * 1103515245 + 12345) % 2147483648
+                new[lab] = new.get(lab, 0.0) + ((seed >> 8) % 1000 - 500) / 400.0
+            out, fin = _pass(ops, pred, succ, [best[2][i] + new.get(ops[i]["lab"], 0.0) for i in range(n)], False)
+            if max(fin) < best[0]:
+                best, bias = (max(fin), out, best[2]), new
         KEPT[n] = best[1]
     return KEPT[n]
 
@@ -135,7 +148,7 @@ def rank_program(g, core, T, topo):
     cores = list(T.cores)
     Q = {"v": g.vector, "a": g.scalar, "p": g.tensor, "g": g, "s": g.sync}
     V, S_, P = g.vector, g.scalar, g.tensor
-    ops, hist, bysem = [], {}, {}
+    ops, hist, bysem, part = [], {}, {}, [0]
 
     def r(name, lo=0, hi=None, st=1):
         hi = SCRATCH[name][1][1] if hi is None else hi
@@ -152,12 +165,12 @@ def rank_program(g, core, T, topo):
         acc = []
         for x, w in [(x, False) for x in rd] + [(x, True) for x in wr]:
             if len(x) > 5:
-                acc.append((x[5][1], x[5][2], x[5][3], False))
-            acc.append((x[1], x[2], x[3], w))
+                acc.append((x[5][1], x[5][2], x[5][3], False, 1))
+            acc.append((x[1], x[2], x[3], w, -(-(x[3] - x[2]) // x[4]) if len(x) == 5 and x[4] > 1 else 1))
         deps, soft = set(), set(after)
-        for name, lo, hi, w in acc:
+        for name, lo, hi, w, st in acc:
             for e in hist.get(name, []):
-                hit = lo < e[1] and e[0] < hi and (w or e[2])
+                hit = lo < e[1] and e[0] < hi and (w or e[2]) and not (st > 1 and st == e[4] and (lo - e[0]) % st)
                 if name in PS and ops[e[3]]["q"] == q == "p":
                     soft.add(e[3])
                 elif hit or (name in PS and ops[e[3]]["q"] != q):
@@ -168,17 +181,18 @@ def rank_program(g, core, T, topo):
         soft -= deps
         for d in soft:
             ops[d]["soft"].add(me_)
-        ops.append({"q": q, "fn": fn, "deps": deps | soft, "wait": deps, "soft": set(), "hold": hold, "lat": lat or hold, "sem": sem, "pre": pre})
-        for name, lo, hi, w in acc:
+        ops.append({"q": q, "fn": fn, "deps": deps | soft, "wait": deps, "soft": set(), "hold": hold, "lat": lat or hold, "sem": sem, "pre": pre,
+                    "lab": (part[0], q, wr[0][1] if wr else "")})
+        for name, lo, hi, w, st in acc:
             h = hist.get(name, [])
             if name in PS:
                 if q == "p":
                     h = []
                 elif h and ops[h[-1][3]]["q"] != q:
                     h = [e for e in h if ops[e[3]]["q"] == ops[h[-1][3]]["q"]]
-            elif w:
+            elif w and st == 1:
                 h = [e for e in h if not (lo <= e[0] and e[1] <= hi) or (sem and ops[e[3]]["sem"] == sem)]
-            h.append((lo, hi, w, me_))
+            h.append((lo, hi, w, me_, st))
             hist[name] = h
         return me_
 
@@ -275,10 +289,11 @@ def rank_program(g, core, T, topo):
     ax = "ax%d" % rank
     c0, l0 = remote(calls[0], lambda d: T.PXS[d], T.PXL[rank], ax, [dr("PXS", 0, 1)], 5.0)
     c1, l1 = remote(calls[1], lambda d: T.PXS[d], T.PXL[rank], ax, [dr("PXS", 1, 2)], 3.5, [c0])
-    cc, lc = remote(single, lambda d: T.CS[d], T.CL[rank], "ac", [dr("CS", 0, 1)], 2.0, [c1])
+    own = dma("g", T.TB[me, XO:CO], T.px[me, :], "dtb", wr=[XW], after=[c1])
+    cc, lc = remote(single, lambda d: T.CS[d], T.CL[rank], "ac", [dr("CS", 0, 1)], 2.0, [own])
     c2, l2 = remote(calls[2], lambda d: T.PXS[d], T.PXL[rank], ax, [dr("PXS", 2, 3)], 3.5, [cc])
     dma("s", T.WU[:], T.CL[:], "dwu", rd=[dr("CL", 0, 1)], wr=[r("WU")], lat=3.0, pre=[("ac", N - 1)], after=[lc])
-    lg_ = dma("g", T.TB[me, XO:CO], T.px[me, :], "dtb", wr=[XW], after=[c2])
+    lg_ = c2
     for k in range(3):
         for s in range(N):
             if s != rank:
@@ -319,21 +334,23 @@ def rank_program(g, core, T, topo):
     act(m("BSb"), m("BS32"))
     act(r("G8", 9, 16), r("G8", 0, 7))
     act(r("G8", 8, 9), r("G8", 7, 8))
-    for nme, src, sc in (("S2", "S", 2.0), ("nI", "I", -1.0), ("nI2", "I", -2.0), ("I4", "I", -4096.0), ("I1", "I", -1024.0), ("nI32", "I32", -1.0)):
+    for nme, src, sc in (("S2", "S", 2.0), ("nI", "I", -1.0), ("nI2", "I", -2.0), ("I4", "I", -4096.0), ("I1", "I", -1024.0)):
         act(m(nme), m(src), scale=sc)
     ms(r("WD"), 0.0)
     for k in range(16):
         ts(r("WD", 128 * k + k, 128 * k + 128, 16), r("G8", 0, 8), 2048.0, A.mult)
     ts(r("MASK"), r("OH", 0, 256), -2097152.0, A.mult, 2097152.0, A.add)
     ts(r("COL", 2, 3), acol, 128.0, A.mult)
-    ts(m("POS"), r("IOT", 0, 128), r("COL", 2, 3), A.add)
-    ms(m("CS"), 8388608.0 + 2047.0)
-    ms(m("CH"), -2047.5)
+    ts(r("COL", 3, 4), acol, 128.0, A.mult, 2047.0, A.add)
+    cp(m("POS"), r("IOT", 0, 128))
+    ts(r("COL", 6, 7), r("OH", 0, 1), -2048.0, A.mult)
+    ts(r("COL", 7, 8), r("OH", 1, 2), 0.5, A.mult, r("COL", 6, 7), A.add)
+    ts(m("CH"), r("IOT", 0, 128), 0.0, A.mult, r("COL", 7, 8), A.add)
     for nme, v0, vs, at in (("RB", 0.0, BIG, 0), ("RR", 0.0, BIG, 15), ("R0", 1.0, 0.0, 0)):
         ms(r(nme), v0)
         ms(r(nme, at, None, 16), vs)
     ms(r("RC"), -BIG)
-    lane, l64, l4, th = r("GL", 0, 8), r("GL", 8, 16), r("GL", 16, 24), r("GL", 24, 32)
+    lane, l64, l4, th = r("GL", 0, 8), r("GB", 0, 8), r("GB", 8, 16), r("GL", 24, 32)
     ts(lane, r("IOT", 0, 128, 16), acol, A.add)
     ts(l64, lane, 64.0, A.mult)
     ts(l4, lane, 4.0, A.mult)
@@ -344,16 +361,15 @@ def rank_program(g, core, T, topo):
     ms(r("CMP"), 1.0)
     ms(r("CD"), 0.0)
     for c in range(8):
-        ms(r("CD", SEG[c], SEG[c] + 1), 1.0)
-        ms(r("CD", SEG[c] + 18 + 16 * c, SEG[c] + 19 + 16 * c), 2.0)
+        act(r("CD", SEG[c], SEG[c] + 1), r("IOT", 1, 2))
+        act(r("CD", SEG[c] + 18 + 16 * c, SEG[c] + 19 + 16 * c), r("IOT", 2, 3))
         ts(r("CD", SEG[c] + 1 + 16 * c, SEG[c] + 17 + 16 * c), r("OH", 0, 16), -2.0, A.mult)
-    for nme in ("DK", "TC", "NC", "par", "aG"):
-        ms(r(nme), 0.0)
+    for nme in ("DK", "TC", "NC", "K4", "par", "aG"):
+        act(r(nme), r("IOT", 0, SCRATCH[nme][1][1]), scale=0.0)
     ms(r("TB", 0, XO), 0.0)
     ms(r("HB", 0, XO), 0.0)
-    ms(r("K4"), 0.0)
-    cp(r("K4", 2, 512, 4), r("IOT", 0, 128))
-    cp(r("K4", 3, 512, 4), r("IOT", 0, 128))
+    act(r("K4", 2, 512, 4), r("IOT", 0, 128))
+    act(r("K4", 3, 512, 4), r("IOT", 0, 128))
 
     cp(r("TB", TW, SM), r("WU", 1024, 1184))
     cp(r("vl", 0, 8), r("TB", TW, TW + 8))
@@ -391,28 +407,33 @@ def rank_program(g, core, T, topo):
     turn(z, m("I"))
 
     def probe(func, scale, sums):
-        mm(r("PD", 0, 128), m("I32"), m("POS"), True, False)
-        if sums:
-            mm(r("PX", 0, 128), m("I32"), m("CS"), True, False)
+        mm(r("PD", 0, 128), m("I"), m("POS"), True, False)
         for lo, hi, e in CHUNKS:
             b = r(e, 0, hi - lo)
             src = ind(XW, r("L16", lo // 16, hi // 16))
             (act if lo == 0 else cp)(r("Y", lo, hi), src)
             mms(b, [(r("TT"), r("EP", lo, hi)), (m("I"), r("Y", lo, hi))])
-            act(r("AB", lo, hi), b, func, scale=scale)
+            if hi < 2048:
+                act(r("AB", lo, hi), b, func, scale=scale)
+            else:
+                ts(r("AB", lo, hi), b, -1.0, A.mult, 0.0, A.max)
+                if scale > 0:
+                    ts(r("EX", lo, hi), b, 0.0, A.max)
+                    for a in range(lo // 128, hi // 128):
+                        mm(r("PD", 0, 128), r("WD", 128 * a, 128 * a + 128), r("EX", 128 * a, 128 * a + 128), False, False)
             for a in range(lo // 128, hi // 128):
                 mm(r("PD", 0, 128), r("WD", 128 * a, 128 * a + 128), r("AB", 128 * a, 128 * a + 128), False, a == 15)
                 if sums:
-                    mm(r("PX", 0, 128), r("WD", 128 * a, 128 * a + 128), r("Y", 128 * a, 128 * a + 128), False, False)
+                    mm(r("PX", 0, 128), r("WD", 128 * a, 128 * a + 128), r("Y", 128 * a, 128 * a + 128), a == 0, False)
         scan(r("rm"), r("RB", 0, 128), r("PD", 0, 128), 0.0, A.add, A.min)
 
     def decode(out, src, t0, t1, flip=False):
         cp(r(t0, 0, 8), r(src, 15, 128, 16))
         ts(r(t1), r(t0, 0, 8), 2047, A.bitwise_and)
         if flip:
-            ts(out, r(t1), -1.0, A.mult, 2047.0, A.add)
+            ts(out, r(t1), -1.0, A.mult, r("COL", 3, 4), A.add)
         else:
-            cp(out, r(t1))
+            ts(out, r(t1), r("COL", 2, 3), A.add)
 
     def send_log(s):
         lg = r("LG", 136 * s, 136 * s + 136)
@@ -424,7 +445,8 @@ def rank_program(g, core, T, topo):
         late = [l] if s >= NL - 2 else [op("link2", None, [], [], 3.0, None, "", (), [l])]
         dma("s", hl[0], T.LL[8 * s:8 * s + 8], "lh%d" % s, rd=[dr("LL", s, s + 1)], wr=[hl], pre=[("la%d" % s, N - 1)], after=late)
         for k in range(4 * (s == 0)):
-            cp(r("HB", CO + 256 * k, CO + 256 * k + 256), r("CI", 256 * k, 256 * k + 256))
+            o, i = r("HB", CO + 256 * k, CO + 256 * k + 256), r("CI", 256 * k, 256 * k + 256)
+            op("v", lambda o=o, i=i: V.tensor_copy(o[0], i[0]), [i, r("posm")], [o], vcost(o, [i]))
         cp(r("ho16"), r("HL", 136 * s + 128, 136 * s + 136))
         cp(ind(r("HB"), r("ho16")), r("HL", 136 * s, 136 * s + 128))
 
@@ -456,15 +478,17 @@ def rank_program(g, core, T, topo):
     k0, k4 = r("K2", 0, 256, 2), r("K4", 0, 512, 4)
     for t in range(RO):
         last = t == RO - 1
+        part[0] = 1
         cp(r("L16"), ind(CW, per))
-        act(r("Lf"), ind(CW, nat))
+        act(r("Lf"), ind(CW, nat), bias=float(XO))
         b = bank(8, AX)
-        mms(b, [(m("S"), r("par")), (m("I32"), l64)])
+        mms(b, [(m("S"), r("par")), (m("I"), l64)])
         act(r("RC", 0, 128, 16), b)
         probe(F.Relu, -1.0, False)
         decode(r("pos"), "rm", "ti", "tj")
         cp(x, ind(Y, r("pos")))
         tt(r("sel"), ind(oh, r("pos")), r("Lf"), A.mult)
+        part[0] = 2
         spread(m("WUm"), "xx")
         turn(x, m("S"))
         cp(r("ti"), r("DG", 15, 256, 16))
@@ -476,41 +500,42 @@ def rank_program(g, core, T, topo):
         act(x1, b)
         act(k0, ind(CW, nat), bias=float(XO))
         act(r("K2", 1, 256, 2), ind(r("IOT"), nat), bias=float(CO))
-        mms(b, [(m("BS32"), r("sel")), (m("nI32"), k0)])
-        act(r("nm"), b, bias=float(XO))
+        mm(b, m("BS32"), r("sel"), True, True)
+        tt(r("nm"), b, k0, A.subtract)
         probe(F.Abs, 1.0, True)
+        part[0] = 5
         act(r("LT"), r("PD", 0, 128), F.Sign, bias=-(240 * 2048 - 0.5))
-        act(r("PDs"), r("PD", 0, 128))
-        mm(r("PX", 0, 128), m("nI32"), r("PDs"), False, True)
+        act(r("PDs"), r("PD", 0, 128), bias=8388608.0 + 2047.0, scale=-1.0)
+        mm(r("PX", 0, 128), m("I32"), r("PDs"), False, True)
         decode(r("pos"), "rm", "ti", "tj")
         scan(r("U"), r("RC"), r("LT"), -BIG, A.max, A.add)
         ts(r("bl2"), r("U", 15, 128, 16), 3.0, A.add, 1.0 / 32, A.mult)
         act(r("Kb"), ind(r("K2"), r("bl2")))
         act(r("yj"), ind(Y, r("pos")))
         scan(rev("hold"), rev("RR"), rev("rm"), 0.0, A.add, A.min)
-        tt(r("ne"), r("PDs"), r("hold"), A.not_equal)
+        tt(r("ne"), r("PD", 0, 128), r("hold"), A.not_equal)
         tt(r("mk"), r("PX", 0, 128), r("ne"), A.mult)
         scan(r("rm2"), r("R0"), r("mk"), 0.0, A.mult, A.max)
         decode(r("posm"), "rm2", "tk", "tl", True)
         tt(f, ind(Y, r("posm")), x1, A.max)
         tt(r("ks"), ind(oh, r("pos")), r("Kb"), A.mult)
         bq = r("PX", 0, 128)
-        mm(bq, m("I32"), m("CH"), True, False)
+        mm(bq, m("BSb"), m("CH"), True, False)
         permuted(bq, m("KP"), "ff", True)
         act(r("q1"), bq, bias=MG, scale=1.0 / 4096)
         act(r("q2"), r("q1"), bias=-MG)
         keys()
         tt(r("tt"), ind(oh, r("pos")), r("nm"), A.mult)
-        b, b2, b3 = r("PD", 0, 128), r("PD", 128, 256), r("PD", 256, 384)
+        b, b3 = r("PD", 0, 128), r("PD", 256, 384)
         mms(b, [(m("I"), x1), (m("I"), r("yj"))])
         mms(b3, [(m("S"), z), (m("nI"), r("yj"))])
-        mms(b2, [(m("I32"), k0), (m("I32"), r("tt"))])
-        act(r("DC", 0, 256, 2), b, bias=MG, scale=0.4995)
-        act(r("DC", 1, 256, 2), b2, bias=MG - XO)
+        act(r("h2"), b, bias=MG, scale=0.4995)
+        act(r("DC", 0, 256, 2), r("h2"), bias=XO - MG)
+        tt(r("DC", 1, 256, 2), k0, r("tt"), A.add)
         act(r("h1"), b3, F.Abs)
         act(r("ZC", 0, 256, 2), r("h1"), bias=MG)
         lg = r("LG", 136 * 2 * t, 136 * 2 * t + 128)
-        act(lg, ind(r("DC"), r("bl2")), bias=-MG)
+        act(lg, ind(r("DC"), r("bl2")), bias=-float(XO))
         winners(2 * t)
         turn(f, m("S"))
         mm(r("PM", 0, 128), m("I4"), r("q2"), True, False)
@@ -522,6 +547,7 @@ def rank_program(g, core, T, topo):
         tt(r("selm"), ind(oh, r("posm")), k0, A.mult)
         if last:
             cp(r("vG"), r("bi", 0, 8))
+        part[0] = 3
         b = r("PX", 0, 128)
         mm(b, m("KP"), f, True, False)
         for k in range(8):
@@ -535,7 +561,7 @@ def rank_program(g, core, T, topo):
         mms(b, [(m("I32"), k4), (m("I1"), r("q3"))])
         act(r("K4", 1, 512, 4), b, bias=196608.0 + CO - XO)
         l4e = r("PM", 0, 8)
-        mms(l4e, [(m("I32"), l4), (m("S2"), r("exG"))])
+        mms(l4e, [(m("I"), l4), (m("S2"), r("exG"))])
         mms(r("A0", 0, 8), [(m("S"), r("par")), (m("nI2"), r("exG"))])
         mms(r("A0", 8, 16), [(m("S"), r("aG")), (m("I"), r("exG"))])
         act(r("par"), r("A0", 0, 8), F.Abs)
@@ -550,6 +576,7 @@ def rank_program(g, core, T, topo):
             dma("s", T.yv[:], T.VL[:, 0:64, :], "dout", rd=[dr("VL", 0, 1)], pre=[("av", N - 1)], after=[l])
             dma("s", T.ya[:], T.VL[:, 64:128, :], "dout", rd=[dr("VL", 0, 1)], pre=[("av", N - 1)], after=[l])
         probe(F.Abs, 1.0, False)
+        part[0] = 4
         ts(r("th"), r("rm", 15, 128, 16), 640.0 * 2048, A.is_ge)
         tt(r("tg"), l4e, r("th"), A.add)
         cp(r("bl4"), r("tg"))
@@ -578,9 +605,7 @@ def rank_program(g, core, T, topo):
         else:
             tt(ind(AW, r("off16")), r("tt"), r("t1"), A.add)
             turn(z, m("I"))
-            b = r("PM", 0, 128)
-            mms(b, [(m("I32"), r("tt")), (m("I32"), r("t1"))])
-            act(lg, b)
+            tt(lg, r("tt"), r("t1"), A.add)
         send_log(2 * t + 1)
 
     dma("a", T.ZS[:], T.z[:], "dzs", rd=[z], wr=[dr("ZS", 0, 1)])

@@ -4,21 +4,26 @@ from concourse.mybir import AluOpType, ActivationFunctionType
 A = AluOpType
 F = ActivationFunctionType
 N, RO = 8, 5
-XO, CO, TW, SM = 128, 4224, 5248, 5408
+XO, ZP, CO, TW, SM = 128, 4224, 4232, 5256, 5416
 MG = 12582912.0
-BIG = 16777216.0
+BIG = 268435456.0
+KS_ = 8192.0
 SEG = [8 * c * (c + 1) + 3 * c for c in range(8)]
 NL = 2 * RO
+LW = 272
 f32, bf, i32, u16 = "float32", "bfloat16", "int32", "uint16"
-MB = ("I", "S", "SB", "S2", "nI", "nI2", "I4", "I1", "BSb", "WUm", "KP", "PM1", "POS", "CH")
-MF = ("I32", "BO32", "BS32")
+MB = ("I", "S", "SB", "S2", "nI", "nI2", "BSb", "WUm", "KP", "PM1", "POS", "Z", "POS2")
+MF = ("I32", "BO32", "BS32", "BOK", "nI32")
 PS = ("E0", "E1", "E2", "E3", "PD", "PX", "PM", "A0")
-CYC, PCYC, HOP = 0.92e-3, 0.55e-3, 0.11
-VCMP = (7, 6, 5, 4)
+CYC, PCYC, HOP = 0.95e-3, 0.5e-3, 0.09
+VCMP = ((7, 6), (7, 6, 5))
 PASSES = 8
 KEPT = {}
-TRIES = 900
-CHUNKS = ((0, 256, "E3"), (256, 768, "E0"), (768, 1280, "E1"), (1280, 1664, "E2"), (1664, 1920, "E3"), (1920, 2048, "E0"))
+TRIES, REACH, SLACK, MEAN = 24000, 1.0, 0.03, 0.1
+MARK = (1, "v", "rm", 0)
+CHUNKS = ((0, 512, "E3", "a", "a"), (512, 896, "E0", "v", "a"), (896, 1408, "E1", "v", "a"), (1408, 1792, "E2", "v", "a"),
+          (1792, 2048, "E0", "v", "v"))
+TAIL = min(c[0] for c in CHUNKS if c[4] == "v")
 
 
 def _sb(w, d):
@@ -26,28 +31,28 @@ def _sb(w, d):
 
 
 SCRATCH = {
-    "TB": _sb(SM, f32), "HB": _sb(TW, f32), "HU": _sb(1184, u16), "WU": _sb(1184, u16), "CI": _sb(1032, i32), "SF": _sb(160, f32), "SH": _sb(176, bf), "EX": _sb(2048, bf), "GB": _sb(16, bf), "fr": _sb(128, bf),
+    "TB": _sb(SM, f32), "HB": _sb(TW, f32), "HU": _sb(1184, u16), "WU": _sb(1184, u16), "CI": _sb(1032, i32), "SF": _sb(160, f32), "SH": _sb(176, bf),
+    "EX": _sb(2048, bf), "GB": _sb(8, bf), "EN": _sb(2048, bf), "WN": _sb(2048, bf), "W2": _sb(2048, bf), "SENT": _sb(136, bf),
     "Y": _sb(2048, bf), "AB": _sb(2048, bf), "EP": _sb(2048, bf), "OH": _sb(2048, bf), "WD": _sb(2048, bf),
     "MB": _sb(128 * len(MB), bf), "MF": _sb(128 * len(MF), f32),
     "IOT": _sb(1024, f32), "CP": _sb(128, f32), "PI": _sb(8, i32), "COL": _sb(16, f32), "G8": _sb(16, f32),
     "MASK": _sb(256, bf), "RB": _sb(256, f32), "RR": _sb(128, f32), "R0": _sb(128, f32), "RC": _sb(128, f32),
     "GL": _sb(32, f32), "FL": _sb(2, u16), "CMP": _sb(600, bf), "CD": _sb(600, bf), "WO": _sb(600, bf),
-    "SMB": _sb(32, bf), "KS": _sb(32, f32), "VR": _sb(128, f32),
+    "SMB": _sb(32, bf), "KS": _sb(32, f32), "VR": _sb(128, f32), "L128": _sb(8, bf),
     "vl": _sb(16, u16), "L16": _sb(128, u16), "Lf": _sb(128, f32), "rm": _sb(128, f32), "hold": _sb(128, f32), "ne": _sb(128, f32),
     "mk": _sb(128, f32), "rm2": _sb(128, f32), "PDs": _sb(128, f32), "ti": _sb(16, i32), "tj": _sb(8, i32), "tk": _sb(8, i32), "tl": _sb(8, i32),
     "bi": _sb(16, i32), "pos": _sb(8, u16), "posm": _sb(8, u16),
-    "bl2": _sb(8, u16), "bl4": _sb(8, u16), "key16": _sb(8, u16), "off16": _sb(8, u16), "ho16": _sb(8, u16), "a16": _sb(8, u16),
-    "tf": _sb(16, f32), "tg": _sb(8, f32), "th": _sb(8, f32), "z": _sb(128, bf), "xx": _sb(128, bf), "x1": _sb(128, bf), "TT": _sb(128, bf),
+    "blA": _sb(8, u16), "blB": _sb(8, u16), "bl4": _sb(8, u16), "key16": _sb(8, u16), "off16": _sb(8, u16), "ho16": _sb(8, u16), "a16": _sb(8, u16),
+    "tg": _sb(8, f32), "th": _sb(8, f32), "z": _sb(128, bf), "xx": _sb(128, bf), "x1": _sb(128, bf), "TT": _sb(128, bf),
     "yj": _sb(128, bf), "wq": _sb(128, bf), "ff": _sb(128, bf),
-    "sel": _sb(128, f32), "selm": _sb(128, f32), "nm": _sb(128, f32), "nm3": _sb(128, f32), "tt": _sb(128, f32), "ks": _sb(128, f32),
-    "Kb": _sb(128, f32), "KR": _sb(128, f32),
-    "DG": _sb(256, f32), "DK": _sb(256, f32), "LT": _sb(128, f32), "U": _sb(128, f32), "K2": _sb(256, f32), "DC": _sb(256, f32),
-    "ZC": _sb(256, f32), "K4": _sb(512, f32), "TC": _sb(512, f32), "NC": _sb(512, f32), "q1": _sb(128, f32), "q2": _sb(128, bf),
-    "q3": _sb(128, bf), "h1": _sb(128, f32), "h2": _sb(128, f32), "nb": _sb(128, f32), "t1": _sb(128, f32),
-    "exG": _sb(8, bf), "par": _sb(8, bf), "aG": _sb(8, bf),
-    "vG": _sb(8, f32), "ar": _sb(128, f32), "LG": _sb(NL * 136, f32), "HL": _sb(NL * 136, f32),
+    "sel": _sb(128, f32), "selm": _sb(128, f32), "nmz": _sb(128, f32), "nm3": _sb(128, f32), "ks": _sb(128, f32), "noh": _sb(128, f32),
+    "Kb": _sb(128, f32), "DKp": _sb(16, f32),
+    "DG": _sb(256, f32), "DK": _sb(256, f32), "LT": _sb(128, f32), "U": _sb(128, f32), "K3": _sb(512, f32), "NM": _sb(512, f32),
+    "ZC": _sb(512, f32), "K4": _sb(512, f32), "TC": _sb(512, f32), "hi": _sb(128, i32), "ci": _sb(128, i32),
+    "LP": _sb(8, u16), "exG": _sb(8, bf), "PA": _sb(16, bf),
+    "vG": _sb(8, f32), "ar": _sb(128, f32), "LG": _sb(NL * LW, f32), "HL": _sb(NL * LW, f32),
     "PXS": ("dram", [8, 128, 512], bf), "PXL": ("dram", [8, 128, 512], bf), "CS": ("dram", [8, 128, 148], u16), "CL": ("dram", [8, 128, 148], u16),
-    "LS": ("dram", [NL * 8, 128, 17], f32), "LL": ("dram", [NL * 8, 128, 17], f32), "ZS": ("dram", [8, 128, 16], bf), "ZL": ("dram", [8, 128, 16], bf),
+    "LS": ("dram", [NL * 8, 128, LW // 8], f32), "LL": ("dram", [NL * 8, 128, LW // 8], f32), "ZS": ("dram", [8, 128, 16], bf), "ZL": ("dram", [8, 128, 16], bf),
     "VS": ("dram", [8, 128, 2], f32), "VL": ("dram", [8, 128, 2], f32),
 }
 for _m in PS:
@@ -101,20 +106,163 @@ def _order(ops):
             if best is None or max(fin) < best[0]:
                 best = (max(fin), out, prio)
             prio = _pass(ops, succ, pred, fin, True)[1]
-        labs = sorted(set(o["lab"] for o in ops if o["lab"][0]))
-        bias, seed = {}, 12345
-        for _ in range(TRIES):
-            new = dict(bias)
-            for _k in range(3):
-                seed = (seed * 1103515245 + 12345) % 2147483648
-                lab = labs[(seed >> 8) % len(labs)]
-                seed = (seed * 1103515245 + 12345) % 2147483648
-                new[lab] = new.get(lab, 0.0) + ((seed >> 8) % 1000 - 500) / 400.0
-            out, fin = _pass(ops, pred, succ, [best[2][i] + new.get(ops[i]["lab"], 0.0) for i in range(n)], False)
-            if max(fin) < best[0]:
-                best, bias = (max(fin), out, best[2]), new
-        KEPT[n] = best[1]
+        order = best[1]
+        mid = [i for i in order if ops[i]["t"] in (1, 2, 3)]
+        order = _alike(ops, pred, succ, order, _improve(ops, pred, succ, mid, TRIES, True))
+        head = [i for i in order if ops[i]["t"] in (-1, 0)]
+        tail = [i for i in order if ops[i]["t"] in (RO - 1, RO)]
+        for sub in (head, tail):
+            new = iter(_improve(ops, pred, succ, sub, TRIES // 4, False))
+            inside = set(sub)
+            order = _valid(pred, succ, [next(new) if i in inside else i for i in order])
+        KEPT[n] = order
     return KEPT[n]
+
+
+def _valid(pred, succ, order):
+    place = {i: k for k, i in enumerate(order)}
+    left, out, seen = [len(p) for p in pred], [], set()
+    for i in order:
+        stack = [i]
+        while stack:
+            j = stack[-1]
+            wait = [d for d in pred[j] if d not in seen]
+            if j in seen:
+                stack.pop()
+            elif wait:
+                stack.extend(sorted(wait, key=lambda d: -place[d]))
+            else:
+                seen.add(j)
+                out.append(stack.pop())
+    return out
+
+
+def _alike(ops, pred, succ, order, mid):
+    st = _times(ops, mid)[1]
+    ph = {ops[i]["lab"]: st[i] for i in mid if ops[i]["t"] == 2}
+    span = (st[[i for i in mid if ops[i]["t"] == 3 and ops[i]["lab"] == MARK][0]] - ph[MARK])
+    st = _times(ops, order)[1]
+    t0 = st[[i for i in order if ops[i]["t"] == 0 and ops[i]["lab"] == MARK][0]] - ph[MARK]
+    key = {}
+    for i in range(len(ops)):
+        o = ops[i]
+        if o["t"] >= 0 and o["lab"] in ph:
+            key[i] = t0 + o["t"] * span + ph[o["lab"]]
+        elif o["t"] <= 0:
+            key[i] = st[i]
+        else:
+            key[i] = max(key[d] + ops[d]["lat"] for d in pred[i])
+    return _valid(pred, succ, sorted(range(len(ops)), key=lambda i: key[i]))
+
+
+def _times(ops, order):
+    free, fin, end, st = {}, {}, {}, {}
+    for i in order:
+        o = ops[i]
+        t = free.get(o["q"], 0.0)
+        for d in o["deps"]:
+            if d in fin:
+                t = max(t, fin[d] + HOP if d in o["wait"] else end[d])
+        st[i] = t
+        free[o["q"]] = end[i] = t + o["hold"]
+        fin[i] = t + o["lat"]
+    return max(fin.values()), st
+
+
+def _improve(ops, pred, succ, order, tries, alike):
+    n = len(order)
+    at = {i: k for k, i in enumerate(order)}
+    qs = sorted(set(ops[i]["q"] for i in order))
+    rows = [(qs.index(ops[i]["q"]), ops[i]["hold"], ops[i]["lat"] + HOP, [at[d] for d in ops[i]["wait"] if d in at],
+             [at[d] for d in ops[i]["deps"] if d in at and d not in ops[i]["wait"]]) for i in order]
+    pr = [w + s for _, _, _, w, s in rows]
+    su = [[at[d] for d in succ[i] if d in at] for i in order]
+    same = {}
+    for k, i in enumerate(order):
+        same.setdefault(ops[i]["lab"] if alike else k, []).append(k)
+    labs = [v for v in same.values() if ops[order[v[0]]]["fn"]]
+
+    def run(seq):
+        free, fin, end, why, prev = [0.0] * len(qs), [0.0] * n, [0.0] * n, [-1] * n, [-1] * len(qs)
+        for k in seq:
+            q, hold, lat, w, s = rows[k]
+            t, y = free[q], prev[q]
+            for d in w:
+                if fin[d] > t:
+                    t, y = fin[d], d
+            for d in s:
+                if end[d] > t:
+                    t, y = end[d], d
+            free[q] = end[k] = t + hold
+            fin[k] = t + lat
+            why[k], prev[q] = y, k
+        return max(fin) + MEAN * sum(fin) / n, end, why, fin
+
+    rnd = [ops[i]["t"] for i in order]
+    ref = [([j for j in same[ops[i]["lab"]] if rnd[j] == 2] + [k])[0] if alike else k for k, i in enumerate(order)]
+    mates = [same[ops[i]["lab"] if alike else k] for k, i in enumerate(order)]
+
+    def places(seq, end):
+        key = [0.0] * n
+        for p, k in enumerate(seq):
+            key[k] = end[k] - rows[k][1] + 1e-8 * p
+        if alike:
+            span = key[same[MARK][2]] - key[same[MARK][1]]
+            key = [key[ref[k]] + span * (rnd[k] - rnd[ref[k]]) for k in range(n)]
+        return key
+
+    def links(res):
+        k, out = res[3].index(max(res[3])), []
+        while res[2][k] >= 0:
+            y = res[2][k]
+            if rows[y][0] == rows[k][0] and y not in pr[k]:
+                out.append((y, k))
+            k = y
+        return out
+
+    key = places(range(n), run(range(n))[1])
+    seq = _valid(pr, su, sorted(range(n), key=lambda k: key[k]))
+    srt = sorted(key)
+    for p, k in enumerate(seq):
+        key[k] = srt[p] + 1e-8 * p
+    res = run(seq)
+    cur, chain = res[0], links(res)
+    best, kept, seed = cur, list(key), 12345
+    for it in range(tries):
+        seed = (seed * 1103515245 + 12345) % 2147483648
+        kind = (seed >> 8) % 4
+        seed = (seed * 1103515245 + 12345) % 2147483648
+        if kind < 2 and chain:
+            u, w = chain[(seed >> 8) % len(chain)]
+            v = mates[(w, u)[kind]]
+        else:
+            v = labs[(seed >> 8) % len(labs)]
+        lo = max([key[d] - key[k] for k in v for d in pr[k]] + [-REACH])
+        hi = min([key[d] - key[k] for k in v for d in su[k]] + [REACH])
+        if kind == 0 and chain:
+            hi = key[u] - key[w]
+        elif kind == 1 and chain:
+            lo = key[w] - key[u]
+        if lo >= hi:
+            continue
+        seed = (seed * 1103515245 + 12345) % 2147483648
+        step = ((seed >> 8) % 998 + 1) / 1000.0
+        step = hi - (hi - lo) * step ** 3 if kind == 0 else lo + (hi - lo) * step ** (3 if kind == 1 else 1)
+        for k in v:
+            key[k] += step
+        seq = sorted(range(n), key=lambda k: key[k])
+        res = run(seq)
+        if res[0] <= cur + SLACK * (1 - it / tries):
+            cur, chain = res[0], links(res)
+            new = places(seq, res[1])
+            if all(new[d] < new[k] for k in range(n) for d in pr[k]) and run(sorted(range(n), key=lambda k: new[k]))[0] <= cur + 1e-6:
+                key = new
+            if cur < best:
+                best, kept = cur, list(key)
+        else:
+            for k in v:
+                key[k] -= step
+    return [order[k] for k in sorted(range(n), key=lambda k: kept[k])]
 
 
 def _pass(ops, pred, succ, prio, back):
@@ -148,7 +296,7 @@ def rank_program(g, core, T, topo):
     cores = list(T.cores)
     Q = {"v": g.vector, "a": g.scalar, "p": g.tensor, "g": g, "s": g.sync}
     V, S_, P = g.vector, g.scalar, g.tensor
-    ops, hist, bysem, part = [], {}, {}, [0]
+    ops, hist, bysem, part, seen = [], {}, {}, [0, -1], {}
 
     def r(name, lo=0, hi=None, st=1):
         hi = SCRATCH[name][1][1] if hi is None else hi
@@ -160,7 +308,9 @@ def rank_program(g, core, T, topo):
     def dr(name, lo, hi):
         return (None, name, lo, hi, 0)
 
-    def op(q, fn, rd, wr, hold, lat=None, sem=None, pre=(), after=()):
+    banks = {}
+
+    def op(q, fn, rd, wr, hold, lat=None, sem=None, pre=(), after=(), start=False):
         me_ = len(ops)
         acc = []
         for x, w in [(x, False) for x in rd] + [(x, True) for x in wr]:
@@ -169,46 +319,57 @@ def rank_program(g, core, T, topo):
             acc.append((x[1], x[2], x[3], w, -(-(x[3] - x[2]) // x[4]) if len(x) == 5 and x[4] > 1 else 1))
         deps, soft = set(), set(after)
         for name, lo, hi, w, st in acc:
+            if name in PS:
+                bk = banks.setdefault(name, {"pe": [], "np": [], "first": None})
+                if q != "p":
+                    deps.update(bk["pe"] + [e for e in bk["np"] if ops[e]["q"] != q])
+                    bk["np"].append(me_)
+                elif start:
+                    deps.update(bk["np"])
+                    soft.update(bk["pe"])
+                    banks[name] = {"pe": ([] if bk["np"] else bk["pe"]) + [me_], "np": [], "first": me_}
+                else:
+                    deps.update(bk["np"])
+                    soft.add(bk["first"])
+                    bk["pe"].append(me_)
+                continue
             for e in hist.get(name, []):
-                hit = lo < e[1] and e[0] < hi and (w or e[2]) and not (st > 1 and st == e[4] and (lo - e[0]) % st)
-                if name in PS and ops[e[3]]["q"] == q == "p":
-                    soft.add(e[3])
-                elif hit or (name in PS and ops[e[3]]["q"] != q):
+                if lo < e[1] and e[0] < hi and (w or e[2]) and not (st > 1 and st == e[4] and (lo - e[0]) % st):
                     deps.update(bysem.get(ops[e[3]]["sem"], [e[3]]))
+        deps.discard(me_)
         if sem:
             deps -= set(bysem.get(sem, []))
             bysem.setdefault(sem, []).append(me_)
         soft -= deps
         for d in soft:
             ops[d]["soft"].add(me_)
+        lab = (part[0], q, wr[0][1] if wr else "")
+        seen[lab, part[1]] = seen.get((lab, part[1]), -1) + 1
         ops.append({"q": q, "fn": fn, "deps": deps | soft, "wait": deps, "soft": set(), "hold": hold, "lat": lat or hold, "sem": sem, "pre": pre,
-                    "lab": (part[0], q, wr[0][1] if wr else "")})
+                    "lab": lab + (seen[lab, part[1]],), "t": part[1], "sum": banks[wr[0][1]]["first"] if q == "p" else None})
         for name, lo, hi, w, st in acc:
             h = hist.get(name, [])
             if name in PS:
-                if q == "p":
-                    h = []
-                elif h and ops[h[-1][3]]["q"] != q:
-                    h = [e for e in h if ops[e[3]]["q"] == ops[h[-1][3]]["q"]]
-            elif w and st == 1:
+                continue
+            if w and st == 1:
                 h = [e for e in h if not (lo <= e[0] and e[1] <= hi) or (sem and ops[e[3]]["sem"] == sem)]
             h.append((lo, hi, w, me_, st))
             hist[name] = h
         return me_
 
-    def vcost(o, ins):
+    def vcost(o, ins, both=1):
         if len(o) > 5:
             return 0.05 + 3.8 * o[4] * CYC
         if any(len(x) > 5 for x in ins):
             return 0.05 + 1.56 * o[4] * CYC
         two = all(SCRATCH[x[1]][2] in (bf, u16) for x in [o] + ins)
-        return 0.03 + max(64, o[4] * (0.5 if two else 1)) * CYC
+        return 0.03 + max(64, o[4] * both * (0.5 if two else 1)) * CYC
 
     def cp(o, i):
         op("v", lambda: V.tensor_copy(o[0], i[0]), [i], [o], vcost(o, [i]))
 
     def tt(o, a, b, f):
-        op("v", lambda: V.tensor_tensor(o[0], a[0], b[0], f), [a, b], [o], vcost(o, [a, b]))
+        op("v", lambda: V.tensor_tensor(o[0], a[0], b[0], f), [a, b], [o], vcost(o, [a, b], 1 if a[1] in PS or b[1] in PS else 2))
 
     def ts(o, a, s1, f1, s2=None, f2=None):
         cols = [s for s in (s1, s2) if isinstance(s, tuple)]
@@ -228,80 +389,80 @@ def rank_program(g, core, T, topo):
     def act(o, i, f=F.Identity, bias=0.0, scale=1.0):
         cols = [bias] if isinstance(bias, tuple) else []
         b = bias[0] if cols else bias
-        op("a", lambda: S_.activation(o[0], i[0], f, bias=b, scale=scale), [i] + cols, [o], 0.1 + o[4] * (1.56 if len(i) > 5 else 1) * CYC)
+        op("a", lambda: S_.activation(o[0], i[0], f, bias=b, scale=scale), [i] + cols, [o], 0.075 + o[4] * (1.56 if len(i) > 5 else 1) * CYC)
 
     def mm(o, l, rh, start, stop):
-        c = max(64, rh[4]) * (4 if SCRATCH[l[1]][2] == f32 else 1) * PCYC
-        op("p", lambda: P.matmul(o[0], l[0], rh[0], start, stop), [l, rh], [o], c, c + 0.1)
+        c = 0.02 + max(64, rh[4]) * (4 if SCRATCH[l[1]][2] == f32 else 1) * PCYC
+        op("p", lambda end: P.matmul(o[0], l[0], rh[0], start, end), [l, rh], [o], c, c + 0.1, start=start)
 
     def mms(o, pairs):
         for k, (l, rh) in enumerate(pairs):
             mm(o, l, rh, k == 0, k == len(pairs) - 1)
 
-    def dma(q, o, i, sem, rd=(), wr=(), lat=2.2, pre=(), after=(), **kw):
-        return op(q, lambda: Q[q].dma_start(o, i, **kw), list(rd), list(wr), 1.0 if q == "g" else 0.1, lat, sem, pre, after)
+    def dma(q, o, i, sem, rd=(), wr=(), lat=2.0, pre=(), after=(), hold=None, **kw):
+        return op(q, lambda: Q[q].dma_start(o, i, **kw), list(rd), list(wr), hold or (0.8 if q == "g" else 0.1), lat, sem, pre, after)
 
     sent = [0]
 
-    def remote(plan, src, dst, sem, rd, hold=4.0, after=()):
+    def remote(plan, src, dst, sem, rd, hold=3.0, after=(), issue=0.7):
         tr = []
         for d, es in plan:
             rid, pid, _ = topo.addr(cores[d])
             tr.append(RemoteDMATransfer(dst_ids=[DstId(rid=rid, pnc=pid)], dma_engine_mask=_mask(es), remote_sem=T.sem[sem],
                                         src=src(d), dst=dst))
             sent[0] += len(es)
-        a = op("g", lambda: g.remote_dma_fused(tr, local_sem=T.sem.ls), rd, [], 1.0, None, "", (), after)
+        a = op("g", lambda: g.remote_dma_fused(tr, local_sem=T.sem.ls), rd, [], issue, None, "", (), after)
         return a, op("link", None, [], [], hold, None, "", (), [a])
 
     def m(n, lo=0, hi=128, st=1):
         buf, k = ("MB", MB.index(n)) if n in MB else ("MF", MF.index(n))
         return r(buf, 128 * k + lo, 128 * k + hi, st)
 
-    rot = [0]
-
-    def bank(w=128, pool=("E0", "E1", "E2", "E3", "A0")):
-        rot[0] += 1
-        return r(pool[rot[0] % len(pool)], 0, w)
-
     calls, single = _calls(core, cores, topo)
     me = slice(16 * rank, 16 * rank + 16)
-    XW, CW, AW = r("TB", XO, CO), r("TB", CO, TW), r("TB", 0, TW)
+    XW, CW, AW, ZW = r("TB", XO, ZP), r("TB", CO, TW), r("TB", 0, TW), r("TB", ZP, TW)
 
-    dma("a", T.CI[:, 0:1024], T.ce[:], "dce", wr=[r("CI", 0, 1024)], lat=3.5)
-    dma("a", T.CI[:, 1024:1032], T.v0[:], "dce", wr=[r("CI", 1024, 1032)])
     last_s = []
     for k, cl in enumerate(calls):
         for d, _ in cl:
             last_s = [dma("s", T.PXS[d], T.px[16 * d:16 * d + 16, :], "xs%d" % k, wr=[dr("PXS", k, k + 1)], after=last_s)]
+        if k == 0:
+            last_s = [dma("s", T.CI[:, 0:1024], T.ce[:], "dce", wr=[r("CI", 0, 1024)], lat=4.5, after=last_s)]
+    dma("a", T.CI[:, 1024:1032], T.v0[:], "dce", wr=[r("CI", 1024, 1032)])
     dma("a", T.SH[:, 0:128], T.z0[:], "dsm", wr=[r("SH", 0, 128)])
     dma("a", T.SH[:, 128:144], T.kap[:], "dsm", wr=[r("SH", 128, 144)])
-    dma("g", T.SH[:, 160:161], T.wu[:], "dsw", wr=[r("SH", 160, 161)], allow_slow_non_contiguous=True)
+    i0 = op("g", lambda: g.iota(T.PI[:, 0:1], [[0, 1]], 0, 1), [], [r("PI", 0, 1)], 0.15)
+    i1 = op("g", lambda: g.iota(T.CP[:], [[1, 128]], 0, -1, allow_small_or_imprecise_dtypes=True), [], [r("CP")], 0.4)
+    i2 = op("g", lambda: g.iota(T.IOT[:, 0:128], [[1, 128]], 0, 0, allow_small_or_imprecise_dtypes=True), [], [r("IOT", 0, 128)], 0.4)
+    ax = "ax%d" % rank
+    c0, l0 = remote(calls[0], lambda d: T.PXS[d], T.PXL[rank], ax, [dr("PXS", 0, 1)], 5.0, [i0, i1, i2], 2.7)
+    c1, l1 = remote(calls[1], lambda d: T.PXS[d], T.PXL[rank], ax, [dr("PXS", 1, 2)], 2.2, [c0])
+    w0 = dma("g", T.SH[:, 160:161], T.wu[:], "dsw", wr=[r("SH", 160, 161)], after=[c1], hold=2.8, lat=4.3, allow_slow_non_contiguous=True)
     cp(r("SF", 0, 144), r("SH", 0, 144))
     cp(r("SF", 144, 145), r("SH", 160, 161))
-    op("g", lambda: g.iota(T.PI[:, 0:1], [[0, 1]], 0, 1), [], [r("PI", 0, 1)], 0.15)
-    op("g", lambda: g.iota(T.CP[:], [[1, 128]], 0, -1, allow_small_or_imprecise_dtypes=True), [], [r("CP")], 0.4)
-    op("g", lambda: g.iota(T.IOT[:, 0:128], [[1, 128]], 0, 0, allow_small_or_imprecise_dtypes=True), [], [r("IOT", 0, 128)], 0.4)
     ms(r("HU", 1168, 1184), 0)
     cp(r("HU", 0, 1032), r("CI"))
     cp(r("HU", 1032, 1177), r("SF", 0, 145))
-    dma("a", T.CS[:], T.HU[:], "dcs", rd=[r("HU")], wr=[dr("CS", 0, 1)], lat=3.0)
+    dma("a", T.CS[:], T.HU[:], "dcs", rd=[r("HU")], wr=[dr("CS", 0, 1)], lat=2.5)
     dma("a", T.CL[rank], T.HU[me, :], "dcs", rd=[r("HU")], wr=[dr("CL", 0, 1)])
-    ax = "ax%d" % rank
-    c0, l0 = remote(calls[0], lambda d: T.PXS[d], T.PXL[rank], ax, [dr("PXS", 0, 1)], 5.0)
-    c1, l1 = remote(calls[1], lambda d: T.PXS[d], T.PXL[rank], ax, [dr("PXS", 1, 2)], 3.5, [c0])
-    own = dma("g", T.TB[me, XO:CO], T.px[me, :], "dtb", wr=[XW], after=[c1])
-    cc, lc = remote(single, lambda d: T.CS[d], T.CL[rank], "ac", [dr("CS", 0, 1)], 2.0, [own])
-    c2, l2 = remote(calls[2], lambda d: T.PXS[d], T.PXL[rank], ax, [dr("PXS", 2, 3)], 3.5, [cc])
-    dma("s", T.WU[:], T.CL[:], "dwu", rd=[dr("CL", 0, 1)], wr=[r("WU")], lat=3.0, pre=[("ac", N - 1)], after=[lc])
-    lg_ = c2
+    own = dma("g", T.TB[me, XO:ZP], T.px[me, :], "dtb", wr=[XW], after=[w0])
+    got = {}
     for k in range(3):
         for s in range(N):
             if s != rank:
                 for d, es in _calls(cores[s], cores, topo)[0][k]:
                     if d == rank:
-                        lg_ = dma("g", T.TB[16 * s:16 * s + 16, XO:CO], T.PXL[s], "dtb", wr=[XW], lat=3.0, pre=[("ax%d" % s, len(es))],
-                                  after=[lg_, (l0, l1, l2)[k]])
-    dma("g", T.HB[:, XO:CO], T.px[:], "dhb", wr=[r("HB", XO, CO)], lat=9.0, after=[lg_])
+                        got.setdefault(k, []).append((s, len(es)))
+
+    def land(k, after):
+        for s, n in got[k]:
+            after = [dma("g", T.TB[16 * s:16 * s + 16, XO:ZP], T.PXL[s], "dtb", wr=[XW], lat=3.0, pre=[("ax%d" % s, n)], after=after)]
+        return after
+    cc, lc = remote(single, lambda d: T.CS[d], T.CL[rank], "ac", [dr("CS", 0, 1)], 2.5, [own])
+    c2, l2 = remote(calls[2], lambda d: T.PXS[d], T.PXL[rank], ax, [dr("PXS", 2, 3)], 2.2, [cc])
+    lg_ = land(2, land(1, land(0, [c2, l0]) + [l1]) + [l2])
+    dma("s", T.WU[:], T.CL[:], "dwu", rd=[dr("CL", 0, 1)], wr=[r("WU")], lat=2.5, pre=[("ac", N - 1)], after=[lc])
+    dma("g", T.HB[:, XO:ZP], T.px[:], "dhb", wr=[r("HB", XO, ZP)], lat=9.0, after=lg_)
 
     ts(r("PI", 2, 3), r("PI", 0, 1), 15, A.bitwise_and)
     ts(r("PI", 4, 5), r("PI", 0, 1), 4, A.arith_shift_right)
@@ -324,52 +485,61 @@ def rank_program(g, core, T, topo):
         act(m("PM1", k, 128, 8), m("I", 16 * k, 16 * k + 16))
     for k in range(16):
         act(r("EP", k, 2048, 16), m("PM1"))
+    ts(r("EN", TAIL, 2048), r("EP", TAIL, 2048), -1.0, A.mult)
     w = 16
     while w < 2048:
         cp(r("OH", w, 2 * w), r("OH", 0, w))
         w *= 2
+    ts(r("W2"), r("OH"), 2 * BIG / 16 - MG, A.mult, MG, A.add)
     for k in range(16):
         cp(m("BO32", k, 128, 16), r("G8", 0, 8))
     roll("BS32", "BO32", 16)
     act(m("BSb"), m("BS32"))
     act(r("G8", 9, 16), r("G8", 0, 7))
     act(r("G8", 8, 9), r("G8", 7, 8))
-    for nme, src, sc in (("S2", "S", 2.0), ("nI", "I", -1.0), ("nI2", "I", -2.0), ("I4", "I", -4096.0), ("I1", "I", -1024.0)):
+    for nme, src, sc in (("S2", "S", 2.0), ("nI", "I", -1.0), ("nI2", "I", -2.0), ("BOK", "BO32", KS_),
+                         ("nI32", "I32", -1.0)):
         act(m(nme), m(src), scale=sc)
     ms(r("WD"), 0.0)
     for k in range(16):
         ts(r("WD", 128 * k + k, 128 * k + 128, 16), r("G8", 0, 8), 2048.0, A.mult)
-    ts(r("MASK"), r("OH", 0, 256), -2097152.0, A.mult, 2097152.0, A.add)
+    ts(r("WN", TAIL, 2048), r("WD", TAIL, 2048), -1.0, A.mult)
+    ts(r("MASK"), r("OH", 0, 256), -BIG / 2, A.mult, BIG / 2, A.add)
     ts(r("COL", 2, 3), acol, 128.0, A.mult)
     ts(r("COL", 3, 4), acol, 128.0, A.mult, 2047.0, A.add)
     cp(m("POS"), r("IOT", 0, 128))
-    ts(r("COL", 6, 7), r("OH", 0, 1), -2048.0, A.mult)
-    ts(r("COL", 7, 8), r("OH", 1, 2), 0.5, A.mult, r("COL", 6, 7), A.add)
-    ts(m("CH"), r("IOT", 0, 128), 0.0, A.mult, r("COL", 7, 8), A.add)
+    ts(r("COL", 8, 9), acol, TAIL // 128 - 0.5, A.is_gt, 8388608.0, A.mult)
+    ts(m("POS2"), r("IOT", 0, 128), 0.0, A.mult, r("COL", 8, 9), A.add)
+    ms(m("Z"), 0.0)
+    ts(r("COL", 6, 7), acol, 8.0, A.mult)
+    ts(r("LP"), r("IOT", 0, 8), r("COL", 6, 7), A.add)
     for nme, v0, vs, at in (("RB", 0.0, BIG, 0), ("RR", 0.0, BIG, 15), ("R0", 1.0, 0.0, 0)):
         ms(r(nme), v0)
         ms(r(nme, at, None, 16), vs)
     ms(r("RC"), -BIG)
-    lane, l64, l4, th = r("GL", 0, 8), r("GB", 0, 8), r("GB", 8, 16), r("GL", 24, 32)
+    ms(r("SENT"), 0.0)
+    ms(r("SENT", 0, 1), ZP * KS_)
+    lane, l128, l4, th = r("GL", 0, 8), r("L128"), r("GB", 0, 8), r("GL", 24, 32)
     ts(lane, r("IOT", 0, 128, 16), acol, A.add)
-    ts(l64, lane, 64.0, A.mult)
+    ts(l128, lane, 128.0, A.mult)
     ts(l4, lane, 4.0, A.mult)
-    ts(th, lane, 64.0, A.mult, 13.0, A.add)
+    ts(th, lane, 128.0, A.mult, 13.0, A.add)
     ts(r("COL", 4, 5), acol, 8.0, A.mult, 27.0, A.add)
     ts(r("COL", 5, 6), r("COL", 4, 5), acol, A.mult, 18.0, A.add)
     ts(r("FL", 0, 1), r("COL", 5, 6), 599.0, A.min)
-    ms(r("CMP"), 1.0)
+    ms(r("CMP"), KS_)
     ms(r("CD"), 0.0)
     for c in range(8):
-        act(r("CD", SEG[c], SEG[c] + 1), r("IOT", 1, 2))
-        act(r("CD", SEG[c] + 18 + 16 * c, SEG[c] + 19 + 16 * c), r("IOT", 2, 3))
-        ts(r("CD", SEG[c] + 1 + 16 * c, SEG[c] + 17 + 16 * c), r("OH", 0, 16), -2.0, A.mult)
-    for nme in ("DK", "TC", "NC", "K4", "par", "aG"):
-        act(r(nme), r("IOT", 0, SCRATCH[nme][1][1]), scale=0.0)
-    ms(r("TB", 0, XO), 0.0)
-    ms(r("HB", 0, XO), 0.0)
-    act(r("K4", 2, 512, 4), r("IOT", 0, 128))
-    act(r("K4", 3, 512, 4), r("IOT", 0, 128))
+        ms(r("CD", SEG[c], SEG[c] + 1), KS_)
+        ts(r("CD", SEG[c] + 1 + 16 * c, SEG[c] + 17 + 16 * c), r("OH", 0, 16), -4 * KS_, A.mult)
+        ms(r("CD", SEG[c] + 17 + 16 * c, SEG[c] + 18 + 16 * c), 4 * KS_)
+        if c:
+            ms(r("CD", SEG[c] + 18 + 16 * c, SEG[c] + 19 + 16 * c), 16.0 * c)
+    for nme, val in (("DK", 0.0), ("TC", MG), ("K4", float(ZP)), ("K3", 0.0), ("NM", 0.0), ("ZC", 0.0), ("PA", 0.0)):
+        act(r(nme), r("IOT", 0, SCRATCH[nme][1][1]), scale=0.0, bias=val)
+    for nme in ("TB", "HB"):
+        ms(r(nme, 0, XO), 0.0)
+        ms(r(nme, ZP, CO), 0.0)
 
     cp(r("TB", TW, SM), r("WU", 1024, 1184))
     cp(r("vl", 0, 8), r("TB", TW, TW + 8))
@@ -378,7 +548,7 @@ def rank_program(g, core, T, topo):
     cp(CW, r("WU", 0, 1024))
     z, x, x1, f = r("z"), r("xx"), r("x1"), r("ff")
     nat, per, oh, Y = r("vl", 0, 8), r("vl", 8, 16), r("OH"), r("Y")
-    AX = ("A0", "PX")
+    par, aG = r("PA", 0, 8), r("PA", 8, 16)
 
     def turn(src, sh):
         b = r("A0", 0, 128)
@@ -398,7 +568,7 @@ def rank_program(g, core, T, topo):
     act(r("VR"), ind(r("IOT"), nat))
     spread(m("I32"), "VR")
     cp(per, r("DG", 143, 256, 16))
-    b = bank(17)
+    b = r("E1", 0, 17)
     mm(b, m("SB"), r("SMB", 0, 17), True, True)
     act(r("KS", 0, 17), b)
     ts(m("WUm"), m("BSb"), r("KS", 16, 17), A.mult)
@@ -406,25 +576,34 @@ def rank_program(g, core, T, topo):
         ts(m("KP", 16 * k, 16 * k + 16), r("KS", 0, 16), r("G8", 8 + k, 9 + k), A.mult)
     turn(z, m("I"))
 
-    def probe(func, scale, sums):
-        mm(r("PD", 0, 128), m("I"), m("POS"), True, False)
-        for lo, hi, e in CHUNKS:
+    def probe(step):
+        pd = r("PD", 0, 128)
+        mm(pd, m("I"), m("POS"), True, False)
+        if step == 1:
+            mm(pd, m("I"), m("POS2"), False, False)
+        for lo, hi, e, ge, te in CHUNKS:
             b = r(e, 0, hi - lo)
             src = ind(XW, r("L16", lo // 16, hi // 16))
-            (act if lo == 0 else cp)(r("Y", lo, hi), src)
-            mms(b, [(r("TT"), r("EP", lo, hi)), (m("I"), r("Y", lo, hi))])
-            if hi < 2048:
-                act(r("AB", lo, hi), b, func, scale=scale)
+            if te == "v":
+                mm(b, r("TT"), r("EN", lo, hi), True, True)
+            (act if ge == "a" else cp)(r("Y", lo, hi), src)
+            if te == "a":
+                mms(b, [(r("TT"), r("EP", lo, hi)), (m("I"), r("Y", lo, hi))])
+                act(r("AB", lo, hi), b, F.Relu if step == 1 else F.Abs, scale=-1.0)
             else:
-                ts(r("AB", lo, hi), b, -1.0, A.mult, 0.0, A.max)
-                if scale > 0:
-                    ts(r("EX", lo, hi), b, 0.0, A.max)
-                    for a in range(lo // 128, hi // 128):
-                        mm(r("PD", 0, 128), r("WD", 128 * a, 128 * a + 128), r("EX", 128 * a, 128 * a + 128), False, False)
+                tt(r("AB", lo, hi), r("Y", lo, hi), b, A.min)
+                if step > 1:
+                    tt(r("EX", lo, hi), r("Y", lo, hi), b, A.max)
             for a in range(lo // 128, hi // 128):
-                mm(r("PD", 0, 128), r("WD", 128 * a, 128 * a + 128), r("AB", 128 * a, 128 * a + 128), False, a == 15)
-                if sums:
-                    mm(r("PX", 0, 128), r("WD", 128 * a, 128 * a + 128), r("Y", 128 * a, 128 * a + 128), a == 0, False)
+                blk = (128 * a, 128 * a + 128)
+                if step == 2:
+                    mm(r("PX", 0, 128), r("WD", *blk), r("Y", *blk), a == 0, False)
+                both = te == "v" and step > 1
+                mm(pd, r("WD" if te == "a" else "WN", *blk), r("AB", *blk), False, a == 15 and not both)
+                if both:
+                    mm(pd, r("WD", *blk), r("EX", *blk), False, a == 15)
+
+    def least():
         scan(r("rm"), r("RB", 0, 128), r("PD", 0, 128), 0.0, A.add, A.min)
 
     def decode(out, src, t0, t1, flip=False):
@@ -436,58 +615,66 @@ def rank_program(g, core, T, topo):
             ts(out, r(t1), r("COL", 2, 3), A.add)
 
     def send_log(s):
-        lg = r("LG", 136 * s, 136 * s + 136)
+        lg = r("LG", LW * s, LW * s + LW)
         sem = "lt%d" % s
         dma("s", T.LS[8 * s:8 * s + 8], lg[0], sem, rd=[lg], wr=[dr("LS", s, s + 1)])
-        dma("s", T.LL[8 * s + rank], T.LG[me, 136 * s:136 * s + 136], sem, rd=[lg], wr=[dr("LL", s, s + 1)])
-        _, l = remote(single, lambda d: T.LS[8 * s + d], T.LL[8 * s + rank], "la%d" % s, [dr("LS", s, s + 1)], 3.5)
-        hl = r("HL", 136 * s, 136 * s + 136)
+        dma("s", T.LL[8 * s + rank], T.LG[me, LW * s:LW * s + LW], sem, rd=[lg], wr=[dr("LL", s, s + 1)])
+        _, l = remote(single, lambda d: T.LS[8 * s + d], T.LL[8 * s + rank], "la%d" % s, [dr("LS", s, s + 1)], 3.0)
+        hl = r("HL", LW * s, LW * s + LW)
         late = [l] if s >= NL - 2 else [op("link2", None, [], [], 3.0, None, "", (), [l])]
         dma("s", hl[0], T.LL[8 * s:8 * s + 8], "lh%d" % s, rd=[dr("LL", s, s + 1)], wr=[hl], pre=[("la%d" % s, N - 1)], after=late)
+        keep, part[0] = part[0], 8
         for k in range(4 * (s == 0)):
             o, i = r("HB", CO + 256 * k, CO + 256 * k + 256), r("CI", 256 * k, 256 * k + 256)
             op("v", lambda o=o, i=i: V.tensor_copy(o[0], i[0]), [i, r("posm")], [o], vcost(o, [i]))
-        cp(r("ho16"), r("HL", 136 * s + 128, 136 * s + 136))
-        cp(ind(r("HB"), r("ho16")), r("HL", 136 * s, 136 * s + 128))
+        part[0] = keep
+        ts(r("ho16"), r("HL", LW * s + 256, LW * s + 264), acol, A.add)
+        tt(ind(r("HB"), r("ho16")), r("HL", LW * s, LW * s + 128), r("HL", LW * s + 128, LW * s + 256), A.add)
 
-    def keys():
+    def keys(vc):
         mm(r("PM", 0, 128), m("I"), r("MASK", 0, 128), True, False)
-        mm(r("PM", 0, 128), m("BO32"), r("ks"), False, True)
-        b = bank()
-        mm(b, m("BO32"), r("ks"), True, True)
-        act(r("KR"), b)
+        mm(r("PM", 0, 128), m("BOK"), r("ks"), False, True)
+        for e, cs in (("E1", vc), ("E2", [c for c in range(8) if c not in vc])):
+            if cs:
+                wa = 17 + 16 * max(cs)
+                mm(r(e, 0, wa), m("I"), r("SENT", 0, wa), True, False)
+                mm(r(e, 1, wa), m("BOK"), r("ks", 0, wa - 1), False, True)
         scan(r("DK", 0, 128), r("RB", 0, 128), r("PM", 0, 128), 0.0, A.add, A.min)
         for c in range(7, -1, -1):
-            o, i, own = r("CMP", SEG[c] + 2, SEG[c] + 18 + 16 * c), r("KR", 0, 16 * c + 16), r("DK", 16 * c + 15, 16 * c + 16)
-            if c in VCMP:
-                ts(o, i, own, A.not_equal)
+            o, own_ = r("CMP", SEG[c] + 1, SEG[c] + 18 + 16 * c), r("DK", 16 * c + 15, 16 * c + 16)
+            if c in vc:
+                ts(o, r("E1", 0, 16 * c + 17), own_, A.not_equal, KS_, A.mult)
             else:
-                act(o, i, F.Abs, bias=own, scale=-1.0)
+                act(o, r("E2", 0, 16 * c + 17), F.Abs, bias=own_, scale=-1.0)
+        ts(r("DKp"), r("DK", 15, 256, 16), 1 / KS_, A.mult, acol, A.subtract)
 
     def winners(s):
-        scan(r("WO"), r("CMP"), r("CD"), 1.0, A.min, A.add)
-        tt(r("tf"), ind(r("WO"), r("FL", 0, 1)), r("DK", 15, 256, 16), A.mult)
-        o = r("LG", 136 * s + 128, 136 * s + 136)
-        tt(o, r("tf", 0, 8), lane, A.max)
+        scan(r("WO"), r("CMP"), r("CD"), 0.0, A.min, A.add)
+        o = r("LG", LW * s + 256, LW * s + 272)
+        tt(o, ind(r("WO"), r("FL", 0, 1)), r("DKp"), A.min)
         if s < NL - 1:
-            cp(r("off16"), o)
+            ts(r("off16"), r("LG", LW * s + 256, LW * s + 264), acol, A.add)
+            tt(ind(AW, r("off16")), r("LG", LW * s, LW * s + 128), r("LG", LW * s + 128, LW * s + 256), A.add)
 
     def rev(n):
         return (T[n][:, 127::-1], n, 0, 128, 128)
 
-    k0, k4 = r("K2", 0, 256, 2), r("K4", 0, 512, 4)
+    kM, k4 = r("K3", 1, 512, 4), r("K4", 0, 512, 4)
+    blA, blB, bl4, pos, posm = r("blA"), r("blB"), r("bl4"), r("pos"), r("posm")
     for t in range(RO):
         last = t == RO - 1
-        part[0] = 1
+        la, lb = r("LG", LW * 2 * t, LW * 2 * t + 128), r("LG", LW * 2 * t + 128, LW * 2 * t + 256)
+        part[:] = [1, t]
         cp(r("L16"), ind(CW, per))
         act(r("Lf"), ind(CW, nat), bias=float(XO))
-        b = bank(8, AX)
-        mms(b, [(m("S"), r("par")), (m("I"), l64)])
+        b = r("PX", 0, 8)
+        mms(b, [(m("S"), par), (m("I"), l128)])
         act(r("RC", 0, 128, 16), b)
-        probe(F.Relu, -1.0, False)
-        decode(r("pos"), "rm", "ti", "tj")
-        cp(x, ind(Y, r("pos")))
-        tt(r("sel"), ind(oh, r("pos")), r("Lf"), A.mult)
+        probe(1)
+        least()
+        decode(pos, "rm", "ti", "tj")
+        cp(x, ind(Y, pos))
+        tt(r("sel"), ind(oh, pos), r("Lf"), A.mult)
         part[0] = 2
         spread(m("WUm"), "xx")
         turn(x, m("S"))
@@ -498,76 +685,66 @@ def rank_program(g, core, T, topo):
         b = r("A0", 0, 128)
         mm(b, m("S"), x, True, True)
         act(x1, b)
-        act(k0, ind(CW, nat), bias=float(XO))
-        act(r("K2", 1, 256, 2), ind(r("IOT"), nat), bias=float(CO))
-        mm(b, m("BS32"), r("sel"), True, True)
-        tt(r("nm"), b, k0, A.subtract)
-        probe(F.Abs, 1.0, True)
+        act(kM, ind(CW, nat), bias=MG + XO)
+        act(r("K3", 2, 512, 4), ind(r("IOT"), nat), bias=MG + CO)
+        mms(b, [(m("BS32"), r("sel")), (m("nI32"), kM)])
+        act(r("NM", 1, 512, 4), b, bias=MG)
+        probe(2)
         part[0] = 5
         act(r("LT"), r("PD", 0, 128), F.Sign, bias=-(240 * 2048 - 0.5))
+        least()
         act(r("PDs"), r("PD", 0, 128), bias=8388608.0 + 2047.0, scale=-1.0)
         mm(r("PX", 0, 128), m("I32"), r("PDs"), False, True)
-        decode(r("pos"), "rm", "ti", "tj")
+        decode(pos, "rm", "ti", "tj")
         scan(r("U"), r("RC"), r("LT"), -BIG, A.max, A.add)
-        ts(r("bl2"), r("U", 15, 128, 16), 3.0, A.add, 1.0 / 32, A.mult)
-        act(r("Kb"), ind(r("K2"), r("bl2")))
-        act(r("yj"), ind(Y, r("pos")))
+        ts(blB, r("U", 15, 128, 16), 35.0, A.add, 1.0 / 32, A.mult)
+        ts(blA, r("U", 15, 128, 16), 3.0, A.add, 1.0 / 32, A.mult)
+        act(r("Kb"), ind(r("K3"), blB), bias=-MG)
+        act(r("yj"), ind(Y, pos))
         scan(rev("hold"), rev("RR"), rev("rm"), 0.0, A.add, A.min)
         tt(r("ne"), r("PD", 0, 128), r("hold"), A.not_equal)
         tt(r("mk"), r("PX", 0, 128), r("ne"), A.mult)
         scan(r("rm2"), r("R0"), r("mk"), 0.0, A.mult, A.max)
-        decode(r("posm"), "rm2", "tk", "tl", True)
-        tt(f, ind(Y, r("posm")), x1, A.max)
-        tt(r("ks"), ind(oh, r("pos")), r("Kb"), A.mult)
+        decode(posm, "rm2", "tk", "tl", True)
+        tt(f, ind(Y, posm), x1, A.max)
+        tt(r("ks"), ind(oh, pos), r("Kb"), A.mult)
         bq = r("PX", 0, 128)
-        mm(bq, m("BSb"), m("CH"), True, False)
+        mm(bq, m("I"), m("Z"), True, False)
         permuted(bq, m("KP"), "ff", True)
-        act(r("q1"), bq, bias=MG, scale=1.0 / 4096)
-        act(r("q2"), r("q1"), bias=-MG)
-        keys()
-        tt(r("tt"), ind(oh, r("pos")), r("nm"), A.mult)
+        cp(r("hi"), bq)
+        ts(r("ci"), r("hi"), 4095, A.bitwise_and)
+        cp(r("L16"), r("ci"))
+        keys(VCMP[0])
+        act(r("nmz"), ind(r("NM"), blA))
+        tt(lb, ind(oh, pos), r("nmz"), A.mult)
         b, b3 = r("PD", 0, 128), r("PD", 256, 384)
         mms(b, [(m("I"), x1), (m("I"), r("yj"))])
         mms(b3, [(m("S"), z), (m("nI"), r("yj"))])
-        act(r("h2"), b, bias=MG, scale=0.4995)
-        act(r("DC", 0, 256, 2), r("h2"), bias=XO - MG)
-        tt(r("DC", 1, 256, 2), k0, r("tt"), A.add)
-        act(r("h1"), b3, F.Abs)
-        act(r("ZC", 0, 256, 2), r("h1"), bias=MG)
-        lg = r("LG", 136 * 2 * t, 136 * 2 * t + 128)
-        act(lg, ind(r("DC"), r("bl2")), bias=-float(XO))
-        winners(2 * t)
+        act(r("K3", 0, 512, 4), b, bias=MG + XO, scale=0.4995)
+        act(r("ZC", 0, 512, 4), b3, bias=MG)
+        act(la, ind(r("K3"), blA), bias=-(MG + XO))
         turn(f, m("S"))
-        mm(r("PM", 0, 128), m("I4"), r("q2"), True, False)
-        permuted(r("PM", 0, 128), m("KP"), "ff", True)
-        cp(r("L16"), r("PM", 0, 128))
-        cp(ind(AW, r("off16")), lg)
+        winners(2 * t)
         send_log(2 * t)
         tt(r("exG"), r("U", 15, 128, 16), th, A.is_lt)
-        tt(r("selm"), ind(oh, r("posm")), k0, A.mult)
+        tt(r("selm"), ind(oh, posm), kM, A.mult)
         if last:
             cp(r("vG"), r("bi", 0, 8))
         part[0] = 3
-        b = r("PX", 0, 128)
-        mm(b, m("KP"), f, True, False)
-        for k in range(8):
-            mm(r("PX", 16 * k, 16 * k + 16), m("I4"), r("q2", k, 128, 8), False, k == 7)
-        act(k4, b, bias=float(XO))
-        act(r("q3"), k4, bias=192 - 639.5 / 1024, scale=1.0 / 1024)
+        la, lb = r("LG", LW * (2 * t + 1), LW * (2 * t + 1) + 128), r("LG", LW * (2 * t + 1) + 128, LW * (2 * t + 1) + 256)
+        act(k4, ind(r("ci"), r("LP")), bias=float(XO))
+        ts(r("hi"), r("ci"), 1023, A.bitwise_and)
+        act(r("K4", 1, 512, 4), ind(r("hi"), r("LP")), bias=float(CO))
         b = r("A0", 0, 128)
         mm(b, m("BS32"), r("selm"), True, True)
         act(r("nm3"), b, bias=-float(XO))
-        b = r("PX", 0, 128)
-        mms(b, [(m("I32"), k4), (m("I1"), r("q3"))])
-        act(r("K4", 1, 512, 4), b, bias=196608.0 + CO - XO)
         l4e = r("PM", 0, 8)
         mms(l4e, [(m("I"), l4), (m("S2"), r("exG"))])
-        mms(r("A0", 0, 8), [(m("S"), r("par")), (m("nI2"), r("exG"))])
-        mms(r("A0", 8, 16), [(m("S"), r("aG")), (m("I"), r("exG"))])
-        act(r("par"), r("A0", 0, 8), F.Abs)
-        act(r("aG"), r("A0", 8, 16))
+        mms(r("A0", 0, 8), [(m("S"), par), (m("nI2"), r("exG"))])
+        mms(r("A0", 8, 16), [(m("S"), aG), (m("I"), r("exG"))])
+        act(r("PA"), r("A0", 0, 16), F.Abs)
         if last:
-            cp(r("a16"), r("aG"))
+            cp(r("a16"), aG)
             act(r("ar"), ind(r("IOT"), r("a16")))
             dma("s", T.VS[:, 0:64, :], T.vG[:], "dvs", rd=[r("vG")], wr=[dr("VS", 0, 1)])
             dma("s", T.VS[:, 64:128, :], T.ar[0:128:16, :], "dvs", rd=[r("ar")], wr=[dr("VS", 0, 1)])
@@ -575,44 +752,39 @@ def rank_program(g, core, T, topo):
             dma("s", T.VL[rank], T.VS[rank], "dvo", rd=[dr("VS", 0, 1)], wr=[dr("VL", 0, 1)])
             dma("s", T.yv[:], T.VL[:, 0:64, :], "dout", rd=[dr("VL", 0, 1)], pre=[("av", N - 1)], after=[l])
             dma("s", T.ya[:], T.VL[:, 64:128, :], "dout", rd=[dr("VL", 0, 1)], pre=[("av", N - 1)], after=[l])
-        probe(F.Abs, 1.0, False)
+        probe(3)
+        least()
         part[0] = 4
         ts(r("th"), r("rm", 15, 128, 16), 640.0 * 2048, A.is_ge)
         tt(r("tg"), l4e, r("th"), A.add)
-        cp(r("bl4"), r("tg"))
-        act(r("Kb"), ind(r("K4"), r("bl4")))
-        decode(r("pos"), "rm", "ti", "tj")
-        act(r("wq"), ind(Y, r("pos")))
-        tt(r("ks"), ind(oh, r("pos")), r("Kb"), A.mult)
-        keys()
-        tt(r("TC", 1, 512, 4), ind(oh, r("pos")), r("nm3"), A.mult)
+        cp(bl4, r("tg"))
+        act(r("Kb"), ind(r("K4"), bl4))
+        decode(pos, "rm", "ti", "tj")
+        act(r("wq"), ind(Y, pos))
+        tt(r("ks"), ind(oh, pos), r("Kb"), A.mult)
+        keys(VCMP[1])
+        tt(r("TC", 1, 512, 4), ind(r("W2"), pos), r("nm3"), A.min)
         bz, bh = r("PX", 0, 128), r("PD", 0, 128)
         mms(bh, [(m("S"), f), (m("I"), r("wq"))])
         mms(bz, [(m("S"), z), (m("SB"), r("wq"))])
-        act(r("NC", 1, 512, 4), ind(oh, r("pos")), bias=1.0, scale=-1.0)
-        cp(r("key16"), r("DK", 15, 128, 16))
-        act(r("nb"), ind(r("NC"), r("bl4")))
-        act(r("h2"), bh, bias=MG, scale=0.4995)
-        act(r("TC", 0, 512, 4), r("h2"), bias=-MG)
-        act(r("t1"), ind(r("TC"), r("bl4")))
+        act(r("noh"), ind(oh, pos), bias=1.0, scale=-1.0)
+        ts(r("key16"), r("DK", 15, 128, 16), 1 / KS_, A.mult, float(ZP), A.subtract)
+        act(r("TC", 0, 512, 4), bh, bias=MG, scale=0.4995)
+        act(la, ind(r("TC"), bl4), bias=-MG)
+        tt(lb, ind(ZW, r("key16")), r("noh"), A.mult)
+        act(r("ZC", 1, 512, 4), bz, bias=MG, scale=0.4995)
+        act(z, ind(r("ZC"), blA), F.Abs, bias=-MG)
         winners(2 * t + 1)
-        tt(r("tt"), ind(AW, r("key16")), r("nb"), A.mult)
-        lg = r("LG", 136 * (2 * t + 1), 136 * (2 * t + 1) + 128)
-        act(r("ZC", 1, 256, 2), bz, bias=MG, scale=0.4995)
-        act(z, ind(r("ZC"), r("bl2")), bias=-MG)
-        if last:
-            tt(lg, r("tt"), r("t1"), A.add)
-        else:
-            tt(ind(AW, r("off16")), r("tt"), r("t1"), A.add)
+        if not last:
             turn(z, m("I"))
-            tt(lg, r("tt"), r("t1"), A.add)
         send_log(2 * t + 1)
 
+    part[:] = [9, RO]
     dma("a", T.ZS[:], T.z[:], "dzs", rd=[z], wr=[dr("ZS", 0, 1)])
     dma("a", T.ZL[rank], T.z[me, :], "dzs", rd=[z], wr=[dr("ZL", 0, 1)])
     _, l = remote(single, lambda d: T.ZS[d], T.ZL[rank], "az", [dr("ZS", 0, 1)], 0.5)
     dma("a", T.yz[:], T.ZL[:], "dout", rd=[dr("ZL", 0, 1)], pre=[("az", N - 1)], after=[l])
-    dma("g", T.yx[:], T.HB[:, XO:CO], "dyx", rd=[r("HB")], lat=6.0)
+    dma("g", T.yx[:], T.HB[:, XO:ZP], "dyx", rd=[r("HB")], lat=6.0)
     dma("s", T.yc[:], T.HB[:, CO:TW], "dout", rd=[r("HB")], lat=4.0)
 
     cnt, waited, done = {}, {}, {}
@@ -622,20 +794,28 @@ def rank_program(g, core, T, topo):
             Q[q].wait_ge(T.sem[sem], val)
             waited[(q, sem)] = val
 
-    needed = set()
+    order = _order(ops)
+    place = {i: k for k, i in enumerate(order)}
+    ends = {ops[i]["sum"]: i for i in order if ops[i]["q"] == "p"}
+    needed, waits = set(), []
     for o in ops:
-        needed |= o["wait"]
-    for i in _order(ops):
+        late = {}
+        for d in o["wait"]:
+            k = ops[d]["lab"][2] if ops[d]["q"] == "p" else d
+            late[k] = max(late.get(k, d), d, key=lambda j: place[j])
+        waits.append(sorted(late.values()))
+        needed |= set(waits[-1])
+    for i in order:
         o = ops[i]
         if o["fn"] is None:
             continue
         need = dict(o["pre"])
-        for d in o["wait"]:
+        for d in waits[i]:
             s, val = done[d]
             need[s] = max(need.get(s, 0), val)
         for s in sorted(need):
             wait(o["q"], s, need[s])
-        ins = o["fn"]()
+        ins = o["fn"](ends[o["sum"]] == i) if o["q"] == "p" else o["fn"]()
         if o["sem"]:
             cnt[o["sem"]] = cnt.get(o["sem"], 0) + 16
             ins.then_inc(T.sem[o["sem"]], 16)

@@ -8,22 +8,27 @@ XO, ZP, CO, TW, SM = 128, 4224, 4232, 5256, 5416
 MG = 12582912.0
 BIG = 268435456.0
 KS_ = 8192.0
-SEG = [8 * c * (c + 1) + 3 * c for c in range(8)]
+SEG = [134 * c + 131 if c < 4 else 150 * (7 - c) for c in range(8)]
 NL = 2 * RO
+CUTS = ((0, 1024), (1024, 2048), (2048, 3072), (3072, 3584), (3584, 4096))
 LW = 272
 f32, bf, i32, u16 = "float32", "bfloat16", "int32", "uint16"
 MB = ("I", "S", "SB", "S2", "nI", "nI2", "BSb", "WUm", "KP", "PM1", "POS", "Z", "POS2")
 MF = ("I32", "BO32", "BS32", "BOK", "nI32")
 PS = ("E0", "E1", "E2", "E3", "PD", "PX", "PM", "A0")
 CYC, PCYC, HOP = 0.95e-3, 0.5e-3, 0.09
-VCMP = ((7, 6), (7, 6, 5))
-PASSES = 8
+VCMP = ((7, 6), (7, 6, 5, 4))
+PASSES = 4
 KEPT = {}
-TRIES, REACH, SLACK, MEAN = 24000, 1.0, 0.03, 0.1
-MARK = (1, "v", "rm", 0)
-CHUNKS = ((0, 512, "E3", "a", "a"), (512, 896, "E0", "v", "a"), (896, 1408, "E1", "v", "a"), (1408, 1792, "E2", "v", "a"),
-          (1792, 2048, "E0", "v", "v"))
-TAIL = min(c[0] for c in CHUNKS if c[4] == "v")
+TRIES, REACH, SLACK, MEAN = 10000, 1.0, 0.03, 0.1
+MARK, MARK2 = (1, "v", "rm", 0), (2, "v", "DG", 0)
+G_, X_ = "gather", "take"
+FAR = ((G_, "a", 4, 6), (G_, "v", 10, 12), (G_, "a", 14, 16), (G_, "v", 0, 4), (X_, "a", 10, 12), (X_, "a", 4, 6), (G_, "v", 12, 14), (X_, "a", 14, 16),
+       (G_, "v", 8, 10), (X_, "a", 0, 4), (G_, "v", 6, 8), (X_, "a", 12, 14), (X_, "v", 6, 8), (X_, "a", 8, 10))
+NEAR = ((G_, "a", 0, 2), (G_, "v", 4, 8), (X_, "v", 0, 2), (G_, "a", 12, 16), (X_, "v", 4, 8), (G_, "a", 8, 11), (X_, "v", 12, 16), (G_, "a", 2, 4),
+        (X_, "v", 8, 11), (G_, "a", 11, 12), (X_, "v", 2, 4), (X_, "v", 11, 12))
+PLAN = (NEAR, FAR, FAR)
+SPARE = ({}, {8: "PM", 12: "A0"}, {8: "PM", 12: "PX"})
 
 
 def _sb(w, d):
@@ -32,18 +37,18 @@ def _sb(w, d):
 
 SCRATCH = {
     "TB": _sb(SM, f32), "HB": _sb(TW, f32), "HU": _sb(1184, u16), "WU": _sb(1184, u16), "CI": _sb(1032, i32), "SF": _sb(160, f32), "SH": _sb(176, bf),
-    "EX": _sb(2048, bf), "GB": _sb(8, bf), "EN": _sb(2048, bf), "WN": _sb(2048, bf), "W2": _sb(2048, bf), "SENT": _sb(136, bf),
+    "EX": _sb(2048, bf), "GB": _sb(16, bf), "ALL": _sb(64, u16), "WN": _sb(2048, bf), "W2": _sb(2048, bf), "SENT": _sb(136, bf),
     "Y": _sb(2048, bf), "AB": _sb(2048, bf), "EP": _sb(2048, bf), "OH": _sb(2048, bf), "WD": _sb(2048, bf),
     "MB": _sb(128 * len(MB), bf), "MF": _sb(128 * len(MF), f32),
-    "IOT": _sb(1024, f32), "CP": _sb(128, f32), "PI": _sb(8, i32), "COL": _sb(16, f32), "G8": _sb(16, f32),
+    "IOT": _sb(1024, f32), "CP": _sb(128, f32), "CQ": _sb(256, f32), "PI": _sb(8, i32), "COL": _sb(16, f32), "G8": _sb(16, f32),
     "MASK": _sb(256, bf), "RB": _sb(256, f32), "RR": _sb(128, f32), "R0": _sb(128, f32), "RC": _sb(128, f32),
     "GL": _sb(32, f32), "FL": _sb(2, u16), "CMP": _sb(600, bf), "CD": _sb(600, bf), "WO": _sb(600, bf),
-    "SMB": _sb(32, bf), "KS": _sb(32, f32), "VR": _sb(128, f32), "L128": _sb(8, bf),
+    "SMB": _sb(32, bf), "KS": _sb(32, f32), "VR": _sb(128, f32),
     "vl": _sb(16, u16), "L16": _sb(128, u16), "Lf": _sb(128, f32), "rm": _sb(128, f32), "hold": _sb(128, f32), "ne": _sb(128, f32),
     "mk": _sb(128, f32), "rm2": _sb(128, f32), "PDs": _sb(128, f32), "ti": _sb(16, i32), "tj": _sb(8, i32), "tk": _sb(8, i32), "tl": _sb(8, i32),
     "bi": _sb(16, i32), "pos": _sb(8, u16), "posm": _sb(8, u16),
     "blA": _sb(8, u16), "blB": _sb(8, u16), "bl4": _sb(8, u16), "key16": _sb(8, u16), "off16": _sb(8, u16), "ho16": _sb(8, u16), "a16": _sb(8, u16),
-    "tg": _sb(8, f32), "th": _sb(8, f32), "z": _sb(128, bf), "xx": _sb(128, bf), "x1": _sb(128, bf), "TT": _sb(128, bf),
+    "tg": _sb(16, f32), "z": _sb(128, bf), "xx": _sb(128, bf), "x1": _sb(128, bf), "TT": _sb(128, bf),
     "yj": _sb(128, bf), "wq": _sb(128, bf), "ff": _sb(128, bf),
     "sel": _sb(128, f32), "selm": _sb(128, f32), "nmz": _sb(128, f32), "nm3": _sb(128, f32), "ks": _sb(128, f32), "noh": _sb(128, f32),
     "Kb": _sb(128, f32), "DKp": _sb(16, f32),
@@ -51,14 +56,17 @@ SCRATCH = {
     "ZC": _sb(512, f32), "K4": _sb(512, f32), "TC": _sb(512, f32), "hi": _sb(128, i32), "ci": _sb(128, i32),
     "LP": _sb(8, u16), "exG": _sb(8, bf), "PA": _sb(16, bf),
     "vG": _sb(8, f32), "ar": _sb(128, f32), "LG": _sb(NL * LW, f32), "HL": _sb(NL * LW, f32),
-    "PXS": ("dram", [8, 128, 512], bf), "PXL": ("dram", [8, 128, 512], bf), "CS": ("dram", [8, 128, 148], u16), "CL": ("dram", [8, 128, 148], u16),
+    "PXB": _sb(4096, bf), "XS": _sb(256, f32), "XR": _sb(256, f32), "XD": ("dram", [8, 128, 32], f32), "XL": ("dram", [8, 128, 32], f32),
+    "XB": _sb(4096, bf), "CS": ("dram", [8, 128, 148], u16), "CL": ("dram", [8, 128, 148], u16),
     "LS": ("dram", [NL * 8, 128, LW // 8], f32), "LL": ("dram", [NL * 8, 128, LW // 8], f32), "ZS": ("dram", [8, 128, 16], bf), "ZL": ("dram", [8, 128, 16], bf),
     "VS": ("dram", [8, 128, 2], f32), "VL": ("dram", [8, 128, 2], f32),
 }
+for _k, (_lo, _hi) in enumerate(CUTS):
+    SCRATCH["PS%d" % _k] = SCRATCH["PL%d" % _k] = ("dram", [8, 128, (_hi - _lo) // 8], bf)
 for _m in PS:
     SCRATCH[_m] = ("psum", [128, 512], f32)
-SEMAPHORES = (["qv", "qa", "qp", "qg", "ls", "dce", "dsm", "dsw", "dcs", "ac", "dwu", "dtb", "dhb", "dvs", "dvo", "av", "dzs", "az", "dout", "dyx"]
-              + ["xs%d" % k for k in range(3)] + ["ax%d" % k for k in range(8)]
+SEMAPHORES = (["qv", "qa", "qp", "qg", "ls", "dce", "dsm", "xo", "dxo", "dv0", "dz0", "dcs", "ac", "dwu", "dhb", "dvs", "dvo", "av", "dzs", "az", "dout", "dyx", "dpb", "dxs", "dxr", "ah"]
+              + ["%s%d" % (p, k) for p in ("xs", "ay", "xl") for k in range(len(CUTS))]
               + ["%s%d" % (p, k) for p in ("lt", "la", "lh") for k in range(NL)])
 
 
@@ -80,10 +88,12 @@ def _calls(src, cores, topo):
         kinds[k].sort(key=lambda r: topo.die(cores[r]) != topo.die(src))
     off = topo.engines(src, cores[kinds["far"][0]])
     on = [e for e in topo.engines(src, cores[kinds["on"][0]]) if e not in off]
-    h = len(off) // 2
-    lo, hi = off[:h], off[h:]
-    calls = [[(kinds["far"][0], lo), (kinds["far"][1], hi), (kinds["on"][0], on)],
-             [(kinds["mate"][0], lo), (kinds["plane"][0], hi)], [(kinds["mate"][1], lo), (kinds["plane"][1], hi)]]
+    calls = []
+    for k, two in enumerate(("far", "mate", "plane")):
+        es = off[2 * k:] + off[:2 * k]
+        rest = [r for kind in ("far", "mate", "plane") if kind != two for r in kinds[kind]]
+        calls.append([(r, es[2 * i:2 * i + 2]) for i, r in enumerate(kinds[two])] + [(r, [es[4 + i]]) for i, r in enumerate(rest)]
+                     + [(kinds["on"][0], on[:2])])
     outs = kinds["far"] + kinds["plane"] + kinds["mate"]
     single = [(r, [off[i]]) for i, r in enumerate(outs)] + [(kinds["on"][0], [on[0]])]
     return calls, single
@@ -142,12 +152,12 @@ def _alike(ops, pred, succ, order, mid):
     ph = {ops[i]["lab"]: st[i] for i in mid if ops[i]["t"] == 2}
     span = (st[[i for i in mid if ops[i]["t"] == 3 and ops[i]["lab"] == MARK][0]] - ph[MARK])
     st = _times(ops, order)[1]
-    t0 = st[[i for i in order if ops[i]["t"] == 0 and ops[i]["lab"] == MARK][0]] - ph[MARK]
+    t1, t0 = [st[[i for i in order if ops[i]["t"] == 0 and ops[i]["lab"] == k][0]] - ph[k] for k in (MARK, MARK2)]
     key = {}
     for i in range(len(ops)):
         o = ops[i]
         if o["t"] >= 0 and o["lab"] in ph:
-            key[i] = t0 + o["t"] * span + ph[o["lab"]]
+            key[i] = (t1 if (o["t"], o["lab"][0]) == (0, 1) else t0) + o["t"] * span + ph[o["lab"]]
         elif o["t"] <= 0:
             key[i] = st[i]
         else:
@@ -237,8 +247,9 @@ def _improve(ops, pred, succ, order, tries, alike):
             v = mates[(w, u)[kind]]
         else:
             v = labs[(seed >> 8) % len(labs)]
-        lo = max([key[d] - key[k] for k in v for d in pr[k]] + [-REACH])
-        hi = min([key[d] - key[k] for k in v for d in su[k]] + [REACH])
+        reach = REACH * (1, 1, 4)[it % 3]
+        lo = max([key[d] - key[k] for k in v for d in pr[k]] + [-reach])
+        hi = min([key[d] - key[k] for k in v for d in su[k]] + [reach])
         if kind == 0 and chain:
             hi = key[u] - key[w]
         elif kind == 1 and chain:
@@ -308,7 +319,7 @@ def rank_program(g, core, T, topo):
     def dr(name, lo, hi):
         return (None, name, lo, hi, 0)
 
-    banks = {}
+    banks, behind, line = {}, [], {}
 
     def op(q, fn, rd, wr, hold, lat=None, sem=None, pre=(), after=(), start=False):
         me_ = len(ops)
@@ -317,7 +328,11 @@ def rank_program(g, core, T, topo):
             if len(x) > 5:
                 acc.append((x[5][1], x[5][2], x[5][3], False, 1))
             acc.append((x[1], x[2], x[3], w, -(-(x[3] - x[2]) // x[4]) if len(x) == 5 and x[4] > 1 else 1))
-        deps, soft = set(), set(after)
+        deps, soft = set(), set(after) | set(behind)
+        behind[:] = []
+        if q in line:
+            soft.update(line[q])
+            line[q] = [me_]
         for name, lo, hi, w, st in acc:
             if name in PS:
                 bk = banks.setdefault(name, {"pe": [], "np": [], "first": None})
@@ -422,138 +437,54 @@ def rank_program(g, core, T, topo):
     me = slice(16 * rank, 16 * rank + 16)
     XW, CW, AW, ZW = r("TB", XO, ZP), r("TB", CO, TW), r("TB", 0, TW), r("TB", ZP, TW)
 
-    last_s = []
-    for k, cl in enumerate(calls):
-        for d, _ in cl:
-            last_s = [dma("s", T.PXS[d], T.px[16 * d:16 * d + 16, :], "xs%d" % k, wr=[dr("PXS", k, k + 1)], after=last_s)]
-        if k == 0:
-            last_s = [dma("s", T.CI[:, 0:1024], T.ce[:], "dce", wr=[r("CI", 0, 1024)], lat=4.5, after=last_s)]
-    dma("a", T.CI[:, 1024:1032], T.v0[:], "dce", wr=[r("CI", 1024, 1032)])
-    dma("a", T.SH[:, 0:128], T.z0[:], "dsm", wr=[r("SH", 0, 128)])
-    dma("a", T.SH[:, 128:144], T.kap[:], "dsm", wr=[r("SH", 128, 144)])
-    i0 = op("g", lambda: g.iota(T.PI[:, 0:1], [[0, 1]], 0, 1), [], [r("PI", 0, 1)], 0.15)
-    i1 = op("g", lambda: g.iota(T.CP[:], [[1, 128]], 0, -1, allow_small_or_imprecise_dtypes=True), [], [r("CP")], 0.4)
-    i2 = op("g", lambda: g.iota(T.IOT[:, 0:128], [[1, 128]], 0, 0, allow_small_or_imprecise_dtypes=True), [], [r("IOT", 0, 128)], 0.4)
-    ax = "ax%d" % rank
-    c0, l0 = remote(calls[0], lambda d: T.PXS[d], T.PXL[rank], ax, [dr("PXS", 0, 1)], 5.0, [i0, i1, i2], 2.7)
-    c1, l1 = remote(calls[1], lambda d: T.PXS[d], T.PXL[rank], ax, [dr("PXS", 1, 2)], 2.2, [c0])
-    w0 = dma("g", T.SH[:, 160:161], T.wu[:], "dsw", wr=[r("SH", 160, 161)], after=[c1], hold=2.8, lat=4.3, allow_slow_non_contiguous=True)
-    cp(r("SF", 0, 144), r("SH", 0, 144))
-    cp(r("SF", 144, 145), r("SH", 160, 161))
-    ms(r("HU", 1168, 1184), 0)
-    cp(r("HU", 0, 1032), r("CI"))
-    cp(r("HU", 1032, 1177), r("SF", 0, 145))
-    dma("a", T.CS[:], T.HU[:], "dcs", rd=[r("HU")], wr=[dr("CS", 0, 1)], lat=2.5)
-    dma("a", T.CL[rank], T.HU[me, :], "dcs", rd=[r("HU")], wr=[dr("CL", 0, 1)])
-    own = dma("g", T.TB[me, XO:ZP], T.px[me, :], "dtb", wr=[XW], after=[w0])
-    got = {}
-    for k in range(3):
-        for s in range(N):
-            if s != rank:
-                for d, es in _calls(cores[s], cores, topo)[0][k]:
-                    if d == rank:
-                        got.setdefault(k, []).append((s, len(es)))
+    def stage(k, lat):
+        dma("s", T["PS%d" % k][:], T.px[:, CUTS[k][0]:CUTS[k][1]], "xs%d" % k, wr=[dr("PS%d" % k, 0, 1)], lat=lat)
 
-    def land(k, after):
-        for s, n in got[k]:
-            after = [dma("g", T.TB[16 * s:16 * s + 16, XO:ZP], T.PXL[s], "dtb", wr=[XW], lat=3.0, pre=[("ax%d" % s, n)], after=after)]
-        return after
-    cc, lc = remote(single, lambda d: T.CS[d], T.CL[rank], "ac", [dr("CS", 0, 1)], 2.5, [own])
-    c2, l2 = remote(calls[2], lambda d: T.PXS[d], T.PXL[rank], ax, [dr("PXS", 2, 3)], 2.2, [cc])
-    lg_ = land(2, land(1, land(0, [c2, l0]) + [l1]) + [l2])
-    dma("s", T.WU[:], T.CL[:], "dwu", rd=[dr("CL", 0, 1)], wr=[r("WU")], lat=2.5, pre=[("ac", N - 1)], after=[lc])
-    dma("g", T.HB[:, XO:ZP], T.px[:], "dhb", wr=[r("HB", XO, ZP)], lat=9.0, after=lg_)
+    def iota(o, pattern, base, step):
+        op("g", lambda: g.iota(o[0], pattern, base, step, allow_small_or_imprecise_dtypes=True), [], [o], 0.13 + 2 * o[4] * CYC)
 
-    ts(r("PI", 2, 3), r("PI", 0, 1), 15, A.bitwise_and)
-    ts(r("PI", 4, 5), r("PI", 0, 1), 4, A.arith_shift_right)
-    acol, gcol = r("COL", 0, 1), r("COL", 1, 2)
-    cp(acol, r("PI", 2, 3))
-    cp(gcol, r("PI", 4, 5))
-    ts(m("I32"), r("CP"), 0.0, A.is_equal)
-    cp(m("I"), m("I32"))
-    ts(r("G8", 0, 8), r("IOT", 0, 8), gcol, A.is_equal)
-    ts(r("OH", 0, 16), r("IOT", 0, 16), acol, A.is_equal)
-    for w in (128, 256, 512):
-        act(r("IOT", w, 2 * w), r("IOT", 0, w), bias=float(w))
+    def fill(name, val):
+        iota(r(name), [[0, SCRATCH[name][1][1]]], int(val), 0)
 
-    def roll(dst, src, k):
-        act(m(dst, k, 128), m(src, 0, 128 - k))
-        act(m(dst, 0, k), m(src, 128 - k, 128))
-    roll("S", "I", 16)
-    roll("SB", "I", 112)
-    for k in range(8):
-        act(m("PM1", k, 128, 8), m("I", 16 * k, 16 * k + 16))
-    for k in range(16):
-        act(r("EP", k, 2048, 16), m("PM1"))
-    ts(r("EN", TAIL, 2048), r("EP", TAIL, 2048), -1.0, A.mult)
-    w = 16
-    while w < 2048:
-        cp(r("OH", w, 2 * w), r("OH", 0, w))
-        w *= 2
-    ts(r("W2"), r("OH"), 2 * BIG / 16 - MG, A.mult, MG, A.add)
-    for k in range(16):
-        cp(m("BO32", k, 128, 16), r("G8", 0, 8))
-    roll("BS32", "BO32", 16)
-    act(m("BSb"), m("BS32"))
-    act(r("G8", 9, 16), r("G8", 0, 7))
-    act(r("G8", 8, 9), r("G8", 7, 8))
-    for nme, src, sc in (("S2", "S", 2.0), ("nI", "I", -1.0), ("nI2", "I", -2.0), ("BOK", "BO32", KS_),
-                         ("nI32", "I32", -1.0)):
-        act(m(nme), m(src), scale=sc)
-    ms(r("WD"), 0.0)
-    for k in range(16):
-        ts(r("WD", 128 * k + k, 128 * k + 128, 16), r("G8", 0, 8), 2048.0, A.mult)
-    ts(r("WN", TAIL, 2048), r("WD", TAIL, 2048), -1.0, A.mult)
-    ts(r("MASK"), r("OH", 0, 256), -BIG / 2, A.mult, BIG / 2, A.add)
-    ts(r("COL", 2, 3), acol, 128.0, A.mult)
-    ts(r("COL", 3, 4), acol, 128.0, A.mult, 2047.0, A.add)
-    cp(m("POS"), r("IOT", 0, 128))
-    ts(r("COL", 8, 9), acol, TAIL // 128 - 0.5, A.is_gt, 8388608.0, A.mult)
-    ts(m("POS2"), r("IOT", 0, 128), 0.0, A.mult, r("COL", 8, 9), A.add)
-    ms(m("Z"), 0.0)
-    ts(r("COL", 6, 7), acol, 8.0, A.mult)
-    ts(r("LP"), r("IOT", 0, 8), r("COL", 6, 7), A.add)
-    for nme, v0, vs, at in (("RB", 0.0, BIG, 0), ("RR", 0.0, BIG, 15), ("R0", 1.0, 0.0, 0)):
-        ms(r(nme), v0)
-        ms(r(nme, at, None, 16), vs)
-    ms(r("RC"), -BIG)
-    ms(r("SENT"), 0.0)
-    ms(r("SENT", 0, 1), ZP * KS_)
-    lane, l128, l4, th = r("GL", 0, 8), r("L128"), r("GB", 0, 8), r("GL", 24, 32)
-    ts(lane, r("IOT", 0, 128, 16), acol, A.add)
-    ts(l128, lane, 128.0, A.mult)
-    ts(l4, lane, 4.0, A.mult)
-    ts(th, lane, 128.0, A.mult, 13.0, A.add)
-    ts(r("COL", 4, 5), acol, 8.0, A.mult, 27.0, A.add)
-    ts(r("COL", 5, 6), r("COL", 4, 5), acol, A.mult, 18.0, A.add)
-    ts(r("FL", 0, 1), r("COL", 5, 6), 599.0, A.min)
-    ms(r("CMP"), KS_)
-    ms(r("CD"), 0.0)
-    for c in range(8):
-        ms(r("CD", SEG[c], SEG[c] + 1), KS_)
-        ts(r("CD", SEG[c] + 1 + 16 * c, SEG[c] + 17 + 16 * c), r("OH", 0, 16), -4 * KS_, A.mult)
-        ms(r("CD", SEG[c] + 17 + 16 * c, SEG[c] + 18 + 16 * c), 4 * KS_)
-        if c:
-            ms(r("CD", SEG[c] + 18 + 16 * c, SEG[c] + 19 + 16 * c), 16.0 * c)
-    for nme, val in (("DK", 0.0), ("TC", MG), ("K4", float(ZP)), ("K3", 0.0), ("NM", 0.0), ("ZC", 0.0), ("PA", 0.0)):
-        act(r(nme), r("IOT", 0, SCRATCH[nme][1][1]), scale=0.0, bias=val)
-    for nme in ("TB", "HB"):
-        ms(r(nme, 0, XO), 0.0)
-        ms(r(nme, ZP, CO), 0.0)
+    line.update({"s": [], "a": [], "v": [], "g": []})
+    stage(0, 2.8)
+    dma("s", T.CI[:, 0:1024], T.ce[:], "dce", wr=[r("CI", 0, 1024)], lat=4.8)
+    stage(1, 5.6)
+    dma("s", T.PXB[:], T.px[:], "dpb", wr=[r("PXB")], lat=9.0)
+    dma("a", T.CI[:, 1024:1032], T.v0[:], "dv0", wr=[r("CI", 1024, 1032)])
+    dma("a", T.SH[:, 0:128], T.z0[:], "dz0", wr=[r("SH", 0, 128)], lat=2.8)
+    dma("a", T.SH[:, 128:144], T.kap[:], "dsm", wr=[r("SH", 128, 144)], lat=4.6)
+    dma("a", T.SH[:, 160:161], T.wu[:], "dsm", wr=[r("SH", 160, 161)], lat=5.6)
+    op("g", lambda: g.iota(T.PI[:, 0:1], [[0, 1]], 0, 1), [], [r("PI", 0, 1)], 0.15)
+    iota(r("IOT", 0, 128), [[1, 128]], 0, 0)
+    iota(r("CQ", 0, 128), [[1, 16], [16, 8]], 0, -1)
+    iota(r("CP"), [[1, 128]], 0, -1)
+    iota(r("CQ", 128, 256), [[1, 8], [0, 16]], 0, 0)
+    ways = {}
 
-    cp(r("TB", TW, SM), r("WU", 1024, 1184))
-    cp(r("vl", 0, 8), r("TB", TW, TW + 8))
-    cp(r("z"), r("TB", TW + 8, TW + 136))
-    cp(r("SMB", 0, 17), r("TB", TW + 136, TW + 153))
-    cp(CW, r("WU", 0, 1024))
+    def piece(k):
+        ways[k] = remote(calls[k % len(calls)], lambda d: T["PS%d" % k][d], T["PL%d" % k][rank], "ay%d" % k, [dr("PS%d" % k, 0, 1)],
+                         (CUTS[k][1] - CUTS[k][0]) / 470 + 1.4 * (k == 0), (), 0.7 if k else 2.7)[1]
+
+    def land(k):
+        lo, hi = CUTS[k]
+        n = sum(len(es) for _, es in calls[k % len(calls)])
+        dma("s", T.XB[:, lo:hi], T["PL%d" % k][:], "xl%d" % k, rd=[dr("PL%d" % k, 0, 1)], wr=[r("XB", lo, hi)], pre=[("ay%d" % k, n)], after=[ways[k]])
+        mid = lo if k < 3 else (lo + hi) // 2
+        if mid > lo:
+            cp(r("TB", XO + lo, XO + mid), r("XB", lo, mid))
+        act(r("TB", XO + mid, XO + hi), r("XB", mid, hi))
+
     z, x, x1, f = r("z"), r("xx"), r("x1"), r("ff")
     nat, per, oh, Y = r("vl", 0, 8), r("vl", 8, 16), r("OH"), r("Y")
     par, aG = r("PA", 0, 8), r("PA", 8, 16)
+    acol, gcol = r("COL", 0, 1), r("COL", 1, 2)
+    lane, l128, l4, th = r("GL", 0, 8), r("GB", 8, 16), r("GB", 0, 8), r("GL", 24, 32)
 
     def turn(src, sh):
         b = r("A0", 0, 128)
         mm(b, src, sh, True, True)
-        act(r("TT"), b, scale=-1.0)
+        act(r("TT"), b)
 
     def permuted(o, l, src, stop):
         for k in range(8):
@@ -563,45 +494,186 @@ def rank_program(g, core, T, topo):
         mm(r("PM", 0, 256), m("I"), r("MASK"), True, False)
         mm(r("PM", 0, 128), l, r(src), False, False)
         permuted(r("PM", 128, 256), l, src, True)
+
+    def lists():
         scan(r("DG"), r("RB"), r("PM", 0, 256), 0.0, A.add, A.min)
 
+    piece(0)
+    piece(1)
+    for nme, val in (("K3", 0), ("NM", 0), ("ZC", 0)):
+        fill(nme, val)
+    ms(r("WN"), 0.0)
+    ms(r("RB"), 0.0)
+    ms(m("POS2"), 8388608.0)
+    ms(r("HU", 1168, 1184), 0)
+    ts(r("PI", 2, 3), r("PI", 0, 1), 15, A.bitwise_and)
+    ts(r("PI", 4, 5), r("PI", 0, 1), 4, A.arith_shift_right)
+    cp(acol, r("PI", 2, 3))
+    cp(gcol, r("PI", 4, 5))
+    ms(r("RB", 0, None, 16), BIG)
+    ts(r("OH", 0, 16), r("IOT", 0, 16), acol, A.is_equal)
+    cp(nat, r("CI", 1024, 1032))
+    cp(r("OH", 16, 32), r("OH", 0, 16))
+    ts(m("PM1"), r("CQ", 0, 128), 0.0, A.is_equal)
+    cp(r("OH", 32, 64), r("OH", 0, 32))
+    ts(m("I"), r("CP"), 0.0, A.is_equal)
+    cp(r("OH", 64, 128), r("OH", 0, 64))
+    ts(m("I32"), r("CP"), 0.0, A.is_equal)
+    cp(r("OH", 128, 256), r("OH", 0, 128))
+    ts(r("G8", 0, 8), r("IOT", 0, 8), gcol, A.is_equal)
+    ts(r("MASK"), r("OH", 0, 256), -BIG / 2, A.mult, BIG / 2, A.add)
+    for w in (128, 256, 512):
+        act(r("IOT", w, 2 * w), r("IOT", 0, w), bias=float(w))
     act(r("VR"), ind(r("IOT"), nat))
     spread(m("I32"), "VR")
+    for k in range(16):
+        ts(r("WN", 128 * k + k, 128 * k + 128, 16), r("G8", 0, 8), -2048.0, A.mult)
+        act(r("EP", k, 2048, 16), m("PM1"))
+    turn(r("SH", 0, 128), m("I"))
+    cp(r("HU", 0, 1032), r("CI"))
+    cp(r("SF", 0, 144), r("SH", 0, 144))
+    cp(r("SF", 144, 145), r("SH", 160, 161))
+    lists()
+    cp(r("HU", 1032, 1177), r("SF", 0, 145))
     cp(per, r("DG", 143, 256, 16))
-    b = r("E1", 0, 17)
-    mm(b, m("SB"), r("SMB", 0, 17), True, True)
-    act(r("KS", 0, 17), b)
-    ts(m("WUm"), m("BSb"), r("KS", 16, 17), A.mult)
-    for k in range(8):
-        ts(m("KP", 16 * k, 16 * k + 16), r("KS", 0, 16), r("G8", 8 + k, 9 + k), A.mult)
-    turn(z, m("I"))
+    cp(m("POS"), r("IOT", 0, 128))
+    ts(r("COL", 2, 3), acol, 128.0, A.mult)
+    for w in (256, 512, 1024):
+        cp(r("OH", w, 2 * w), r("OH", 0, w))
+    dma("s", T.CS[:], T.HU[:], "dcs", rd=[r("HU")], wr=[dr("CS", 0, 1)], lat=3.8)
+    for k in range(2, len(CUTS)):
+        stage(k, 3.5 + 0.6 * k)
+    dma("s", T.CL[rank], T.HU[me, :], "xo", rd=[r("HU")], wr=[dr("CL", 0, 1)], lat=6.0)
+    for k, (lo, hi) in enumerate(CUTS):
+        dma("s", T["PL%d" % k][rank], T.px[me, lo:hi], "xo", wr=[dr("PL%d" % k, 0, 1)], lat=6.0)
+    lc = remote(calls[0], lambda d: T.CS[d], T.CL[rank], "ac", [dr("CS", 0, 1)], 3.9)[1]
+    piece(2)
 
-    def probe(step):
+    def hand_over():
+        dma("s", T.XD[:], T.XS[:], "dxs", rd=[r("XS")], wr=[dr("XD", 0, 1)])
+        dma("s", T.XL[rank], T.XS[me, :], "dxo", rd=[r("XS")], wr=[dr("XL", 0, 1)])
+        for nme, val in (("PA", 0), ("K4", ZP), ("TC", MG), ("DK", 0)):
+            fill(nme, val)
+        lx = remote(single, lambda d: T.XD[d], T.XL[rank], "ah", [dr("XD", 0, 1)], 1.8)[1]
+        piece(3)
+        piece(4)
+
+        def roll(dst, src, k):
+            act(m(dst, k, 128), m(src, 0, 128 - k))
+            act(m(dst, 0, k), m(src, 128 - k, 128))
+        ts(m("BO32"), r("CQ", 128, 256), gcol, A.is_equal)
+        roll("S", "I", 16)
+        roll("SB", "I", 112)
+        roll("BS32", "BO32", 16)
+        act(m("BSb"), m("BS32"))
+        act(m("nI"), m("I"), scale=-1.0)
+        act(r("WD", 0, 1024), r("WN", 0, 1024), scale=-1.0)
+        ts(r("WD", 1024, 2048), r("WN", 1024, 2048), -1.0, A.mult)
+        ts(r("ALL"), r("IOT", 0, 1024, 16), acol, A.add)
+        for nme in ("TB", "HB"):
+            ms(r(nme, 0, XO), 0.0)
+            ms(r(nme, ZP, CO), 0.0)
+        ts(lane, r("IOT", 0, 128, 16), acol, A.add)
+        ms(r("RC"), -BIG)
+        ts(l128, lane, 128.0, A.mult)
+        ts(l4, lane, 4.0, A.mult)
+        ts(th, lane, 128.0, A.mult, 13.0, A.add)
+        act(r("G8", 9, 16), r("G8", 0, 7))
+        act(r("G8", 8, 9), r("G8", 7, 8))
+        for nme, src, sc in (("nI32", "I32", -1.0), ("BOK", "BO32", KS_), ("S2", "S", 2.0), ("nI2", "I", -2.0)):
+            act(m(nme), m(src), scale=sc)
+        counts()
+        for nme, v0, vs, at in (("RR", 0.0, BIG, 15), ("R0", 1.0, 0.0, 0), ("SENT", 0.0, ZP * KS_, 0)):
+            ms(r(nme), v0)
+        ms(m("Z"), 0.0)
+        ms(r("CMP"), KS_)
+        ms(r("CD"), 0.0)
+        ms(r("RR", 15, None, 16), BIG)
+        ms(r("R0", 0, None, 16), 0.0)
+        ms(r("SENT", 0, 1), ZP * KS_)
+        ts(r("COL", 3, 4), acol, 128.0, A.mult, 2047.0, A.add)
+        ts(r("COL", 6, 7), acol, 8.0, A.mult)
+        ts(r("COL", 4, 5), acol, 150.0, A.mult, 149.0, A.add)
+        ts(r("COL", 5, 6), acol, -134.0, A.mult, 1068.0, A.add)
+        ts(r("LP"), r("IOT", 0, 8), r("COL", 6, 7), A.add)
+        ts(r("FL", 0, 1), r("COL", 4, 5), r("COL", 5, 6), A.min)
+        for c in range(8):
+            ts(r("CD", SEG[c] + 1 + 16 * c, SEG[c] + 17 + 16 * c), r("OH", 0, 16), -4 * KS_, A.mult)
+        for at, st, val in ((0, 150, KS_), (131, 134, KS_), (129, 134, 4 * KS_), (148, 150, 4 * KS_)):
+            ms(r("CD", at, at + 3 * st + 1, st), val)
+        ts(r("CD", 130, 130 + 3 * 134 + 1, 134), r("IOT", 0, 4), -16.0, A.mult, 112.0, A.add)
+        ts(r("CD", 149, 149 + 3 * 150 + 1, 150), r("IOT", 0, 4), 16.0, A.mult)
+        land(0)
+        land(1)
+        dma("s", T.WU[:], T.CL[:], "dwu", rd=[dr("CL", 0, 1)], wr=[r("WU")], lat=2.5, pre=[("ac", sum(len(es) for _, es in calls[0]))], after=[lc])
+        cp(r("TB", TW, SM), r("WU", 1024, 1184))
+        cp(r("SMB", 0, 17), r("TB", TW + 136, TW + 153))
+        b = r("PX", 0, 17)
+        mm(b, m("SB"), r("SMB", 0, 17), True, True)
+        act(r("KS", 0, 17), b)
+        cp(CW, r("WU", 0, 1024))
+        ts(m("WUm"), m("BSb"), r("KS", 16, 17), A.mult)
+        land(2)
+        dma("s", T.XR[:], T.XL[:], "dxr", rd=[dr("XL", 0, 1)], wr=[r("XR")], pre=[("ah", N - 1)], after=[lx])
+        cp(r("z"), r("TB", TW + 8, TW + 136))
+        cp(x, r("XR", 0, 128))
+        keep = {"s": line["s"], "g": line["g"]}
+        line.clear()
+        line.update(keep)
+        land(3)
+        land(4)
+        dma("g", T.HB[:, XO:ZP], T.px[:], "dhb", rd=[r("XB")], wr=[r("HB", XO, ZP)], lat=11.0, hold=2.8)
+        line.clear()
+        for k in range(8):
+            ts(m("KP", 16 * k, 16 * k + 16), r("KS", 0, 16), r("G8", 8 + k, 9 + k), A.mult)
+        for k in range(4):
+            act(r("W2", 512 * k, 512 * k + 512), r("OH", 0, 512), scale=2 * BIG / 16 - MG, bias=MG)
+            act(r("HB", CO + 256 * k, CO + 256 * k + 256), ind(r("CI", 0, 1024), r("ALL", 16 * k, 16 * k + 16)))
+
+
+    def probe(step, win=XW):
         pd = r("PD", 0, 128)
         mm(pd, m("I"), m("POS"), True, False)
         if step == 1:
             mm(pd, m("I"), m("POS2"), False, False)
-        for lo, hi, e, ge, te in CHUNKS:
-            b = r(e, 0, hi - lo)
-            src = ind(XW, r("L16", lo // 16, hi // 16))
-            if te == "v":
-                mm(b, r("TT"), r("EN", lo, hi), True, True)
-            (act if ge == "a" else cp)(r("Y", lo, hi), src)
-            if te == "a":
-                mms(b, [(r("TT"), r("EP", lo, hi)), (m("I"), r("Y", lo, hi))])
-                act(r("AB", lo, hi), b, F.Relu if step == 1 else F.Abs, scale=-1.0)
+        def bank(a0, a1):
+            spare = SPARE[step - 1].get(a0)
+            return r(spare, 0, 128 * (a1 - a0)) if spare else r("E%d" % (a0 // 4), 128 * (a0 % 4), 128 * (a0 % 4 + a1 - a0))
+        takes = sorted((e == "a", a0, a1) for what, e, a0, a1 in PLAN[step - 1] if what == "take")
+        if step == 1:
+            takes = [(False, 4 * k, 4 * k + 4) for k in range(4)]
+        for opened, a0, a1 in takes:
+            mm(bank(a0, a1), r("TT"), r("EP", 128 * a0, 128 * a1), True, False)
+        prev, first = {}, True
+        for what, e, a0, a1 in PLAN[step - 1]:
+            lo, hi = 128 * a0, 128 * a1
+            b = bank(a0, a1)
+            if what == "take" and e == "a":
+                mm(b, m("nI"), r("Y", lo, hi), False, True)
+            behind[:] = prev.get(e, [])
+            if what == "gather":
+                (act if e == "a" else cp)(r("Y", lo, hi), ind(win, r("L16", lo // 16, hi // 16)))
+            elif e == "a":
+                act(r("AB", lo, hi), b, F.Relu if step == 1 else F.Abs)
             else:
                 tt(r("AB", lo, hi), r("Y", lo, hi), b, A.min)
                 if step > 1:
                     tt(r("EX", lo, hi), r("Y", lo, hi), b, A.max)
-            for a in range(lo // 128, hi // 128):
+            prev[e] = [len(ops) - 1]
+            for a in range(a0, a1):
                 blk = (128 * a, 128 * a + 128)
-                if step == 2:
-                    mm(r("PX", 0, 128), r("WD", *blk), r("Y", *blk), a == 0, False)
-                both = te == "v" and step > 1
-                mm(pd, r("WD" if te == "a" else "WN", *blk), r("AB", *blk), False, a == 15 and not both)
-                if both:
-                    mm(pd, r("WD", *blk), r("EX", *blk), False, a == 15)
+                if what == "gather" and step == 2:
+                    mm(r("PX", 0, 128), r("WD", *blk), r("Y", *blk), first, False)
+                    first = False
+                if what == "take":
+                    mm(pd, r("WD" if e == "a" else "WN", *blk), r("AB", *blk), False, False)
+                    if e == "v" and step > 1:
+                        mm(pd, r("WD", *blk), r("EX", *blk), False, False)
+
+    def counts():
+        b = r("PX", 0, 8)
+        mms(b, [(m("S"), par), (m("I"), l128)])
+        act(r("RC", 0, 128, 16), b)
 
     def least():
         scan(r("rm"), r("RB", 0, 128), r("PD", 0, 128), 0.0, A.add, A.min)
@@ -621,14 +693,14 @@ def rank_program(g, core, T, topo):
         dma("s", T.LL[8 * s + rank], T.LG[me, LW * s:LW * s + LW], sem, rd=[lg], wr=[dr("LL", s, s + 1)])
         _, l = remote(single, lambda d: T.LS[8 * s + d], T.LL[8 * s + rank], "la%d" % s, [dr("LS", s, s + 1)], 3.0)
         hl = r("HL", LW * s, LW * s + LW)
-        late = [l] if s >= NL - 2 else [op("link2", None, [], [], 3.0, None, "", (), [l])]
-        dma("s", hl[0], T.LL[8 * s:8 * s + 8], "lh%d" % s, rd=[dr("LL", s, s + 1)], wr=[hl], pre=[("la%d" % s, N - 1)], after=late)
-        keep, part[0] = part[0], 8
-        for k in range(4 * (s == 0)):
-            o, i = r("HB", CO + 256 * k, CO + 256 * k + 256), r("CI", 256 * k, 256 * k + 256)
-            op("v", lambda o=o, i=i: V.tensor_copy(o[0], i[0]), [i, r("posm")], [o], vcost(o, [i]))
-        part[0] = keep
+        dma("s", hl[0], T.LL[8 * s:8 * s + 8], "lh%d" % s, rd=[dr("LL", s, s + 1)], wr=[hl], pre=[("la%d" % s, N - 1)], after=[l])
+
+    def apply_log(s):
+        if s < 0:
+            return
+        last_ = len(ops) - 1
         ts(r("ho16"), r("HL", LW * s + 256, LW * s + 264), acol, A.add)
+        behind[:] = [last_]
         tt(ind(r("HB"), r("ho16")), r("HL", LW * s, LW * s + 128), r("HL", LW * s + 128, LW * s + 256), A.add)
 
     def keys(vc):
@@ -665,18 +737,24 @@ def rank_program(g, core, T, topo):
         last = t == RO - 1
         la, lb = r("LG", LW * 2 * t, LW * 2 * t + 128), r("LG", LW * 2 * t + 128, LW * 2 * t + 256)
         part[:] = [1, t]
-        cp(r("L16"), ind(CW, per))
-        act(r("Lf"), ind(CW, nat), bias=float(XO))
-        b = r("PX", 0, 8)
-        mms(b, [(m("S"), par), (m("I"), l128)])
-        act(r("RC", 0, 128, 16), b)
-        probe(1)
+        cells = CW if t else r("CI", 0, 1024)
+        cp(r("L16"), ind(cells, per))
+        act(r("Lf"), ind(cells, nat), bias=float(XO))
+        if t:
+            counts()
+        probe(1, XW if t else r("PXB"))
         least()
         decode(pos, "rm", "ti", "tj")
-        cp(x, ind(Y, pos))
-        tt(r("sel"), ind(oh, pos), r("Lf"), A.mult)
+        sel = r("sel") if t else r("XR", 128, 256)
+        cp(x if t else r("XS", 0, 128), ind(Y, pos))
+        apply_log(2 * t - 3)
+        tt(sel if t else r("XS", 128, 256), ind(oh, pos), r("Lf"), A.mult)
+        if not t:
+            part[0] = 7
+            hand_over()
         part[0] = 2
         spread(m("WUm"), "xx")
+        lists()
         turn(x, m("S"))
         cp(r("ti"), r("DG", 15, 256, 16))
         ts(r("bi"), r("ti"), 1023, A.bitwise_and)
@@ -687,9 +765,10 @@ def rank_program(g, core, T, topo):
         act(x1, b)
         act(kM, ind(CW, nat), bias=MG + XO)
         act(r("K3", 2, 512, 4), ind(r("IOT"), nat), bias=MG + CO)
-        mms(b, [(m("BS32"), r("sel")), (m("nI32"), kM)])
-        act(r("NM", 1, 512, 4), b, bias=MG)
         probe(2)
+        apply_log(2 * t - 2)
+        mms(b, [(m("BS32"), sel), (m("nI32"), kM)])
+        act(r("NM", 1, 512, 4), b, bias=MG)
         part[0] = 5
         act(r("LT"), r("PD", 0, 128), F.Sign, bias=-(240 * 2048 - 0.5))
         least()
@@ -738,7 +817,7 @@ def rank_program(g, core, T, topo):
         b = r("A0", 0, 128)
         mm(b, m("BS32"), r("selm"), True, True)
         act(r("nm3"), b, bias=-float(XO))
-        l4e = r("PM", 0, 8)
+        l4e = r("A0", 256, 264)
         mms(l4e, [(m("I"), l4), (m("S2"), r("exG"))])
         mms(r("A0", 0, 8), [(m("S"), par), (m("nI2"), r("exG"))])
         mms(r("A0", 8, 16), [(m("S"), aG), (m("I"), r("exG"))])
@@ -755,31 +834,35 @@ def rank_program(g, core, T, topo):
         probe(3)
         least()
         part[0] = 4
-        ts(r("th"), r("rm", 15, 128, 16), 640.0 * 2048, A.is_ge)
-        tt(r("tg"), l4e, r("th"), A.add)
-        cp(bl4, r("tg"))
+        ts(r("tg", 8, 16), r("rm", 15, 128, 16), 640.0 * 2048, A.is_ge)
+        tt(r("tg", 0, 8), l4e, r("tg", 8, 16), A.add)
+        cp(bl4, r("tg", 0, 8))
+        line["a"] = []
         act(r("Kb"), ind(r("K4"), bl4))
         decode(pos, "rm", "ti", "tj")
         act(r("wq"), ind(Y, pos))
         tt(r("ks"), ind(oh, pos), r("Kb"), A.mult)
-        keys(VCMP[1])
-        tt(r("TC", 1, 512, 4), ind(r("W2"), pos), r("nm3"), A.min)
         bz, bh = r("PX", 0, 128), r("PD", 0, 128)
-        mms(bh, [(m("S"), f), (m("I"), r("wq"))])
         mms(bz, [(m("S"), z), (m("SB"), r("wq"))])
+        act(r("ZC", 1, 512, 4), bz, bias=MG, scale=0.4995)
+        act(z, ind(r("ZC"), blA), F.Abs, bias=-MG)
+        keys(VCMP[1])
+        if not last:
+            turn(z, m("I"))
+        line.clear()
+        tt(r("TC", 1, 512, 4), ind(r("W2"), pos), r("nm3"), A.min)
+        mms(bh, [(m("S"), f), (m("I"), r("wq"))])
         act(r("noh"), ind(oh, pos), bias=1.0, scale=-1.0)
         ts(r("key16"), r("DK", 15, 128, 16), 1 / KS_, A.mult, float(ZP), A.subtract)
         act(r("TC", 0, 512, 4), bh, bias=MG, scale=0.4995)
         act(la, ind(r("TC"), bl4), bias=-MG)
         tt(lb, ind(ZW, r("key16")), r("noh"), A.mult)
-        act(r("ZC", 1, 512, 4), bz, bias=MG, scale=0.4995)
-        act(z, ind(r("ZC"), blA), F.Abs, bias=-MG)
         winners(2 * t + 1)
-        if not last:
-            turn(z, m("I"))
         send_log(2 * t + 1)
 
     part[:] = [9, RO]
+    for s in range(NL - 3, NL):
+        apply_log(s)
     dma("a", T.ZS[:], T.z[:], "dzs", rd=[z], wr=[dr("ZS", 0, 1)])
     dma("a", T.ZL[rank], T.z[me, :], "dzs", rd=[z], wr=[dr("ZL", 0, 1)])
     _, l = remote(single, lambda d: T.ZS[d], T.ZL[rank], "az", [dr("ZS", 0, 1)], 0.5)

@@ -13,8 +13,9 @@ NL = 2 * RO
 CUTS = ((0, 1024), (1024, 2048), (2048, 3072), (3072, 3584), (3584, 4096))
 LW = 272
 f32, bf, i32, u16 = "float32", "bfloat16", "int32", "uint16"
-MB = ("I", "S", "SB", "S2", "nI", "nI2", "BSb", "WUm", "KP", "PM1", "POS", "Z", "POS2")
-MF = ("I32", "BO32", "BS32", "BOK", "nI32")
+MB = ("I", "S", "SB", "S2", "nI", "nI2", "BSb", "WUm", "KP", "PM1", "POS", "POS2", "POS1")
+U16AND, U16TT, FQ, PIN = False, True, "a", 0
+MF = ("I32", "BO32", "BS32", "BOK")
 PS = ("E0", "E1", "E2", "E3", "PD", "PX", "PM", "A0")
 CYC, PCYC, HOP = 0.95e-3, 0.5e-3, 0.09
 VCMP = ((7, 6), (7, 6, 5, 4))
@@ -40,21 +41,21 @@ SCRATCH = {
     "EX": _sb(2048, bf), "GB": _sb(16, bf), "ALL": _sb(64, u16), "WN": _sb(2048, bf), "W2": _sb(2048, bf), "SENT": _sb(136, bf),
     "Y": _sb(2048, bf), "AB": _sb(2048, bf), "EP": _sb(2048, bf), "OH": _sb(2048, bf), "WD": _sb(2048, bf),
     "MB": _sb(128 * len(MB), bf), "MF": _sb(128 * len(MF), f32),
-    "IOT": _sb(1024, f32), "CP": _sb(128, f32), "CQ": _sb(256, f32), "PI": _sb(8, i32), "COL": _sb(16, f32), "G8": _sb(16, f32),
-    "MASK": _sb(256, bf), "RB": _sb(256, f32), "RR": _sb(128, f32), "R0": _sb(128, f32), "RC": _sb(128, f32),
+    "IOT": _sb(1024, f32), "CP": _sb(128, f32), "CQ": _sb(264, f32), "PI": _sb(8, i32), "COL": _sb(16, f32), "G8": _sb(16, f32),
+    "MASK": _sb(256, bf), "RB": _sb(256, f32), "RR": _sb(128, f32), "RC": _sb(128, f32),
     "GL": _sb(32, f32), "FL": _sb(2, u16), "CMP": _sb(600, bf), "CD": _sb(600, bf), "WO": _sb(600, bf),
-    "SMB": _sb(32, bf), "KS": _sb(32, f32), "VR": _sb(128, f32),
-    "vl": _sb(16, u16), "L16": _sb(128, u16), "Lf": _sb(128, f32), "rm": _sb(128, f32), "hold": _sb(128, f32), "ne": _sb(128, f32),
-    "mk": _sb(128, f32), "rm2": _sb(128, f32), "PDs": _sb(128, f32), "ti": _sb(16, i32), "tj": _sb(8, i32), "tk": _sb(8, i32), "tl": _sb(8, i32),
+    "SMB": _sb(32, bf), "KS": _sb(32, f32), "VR": _sb(384, f32),
+    "vl": _sb(24, u16), "L16": _sb(128, u16), "Lf": _sb(128, f32), "rm": _sb(128, i32), "hold": _sb(128, f32), "ne": _sb(128, f32),
+    "mk": _sb(128, f32), "rm2": _sb(128, i32), "PDs": _sb(128, f32), "tj": _sb(8, i32), "tl": _sb(8, i32), "cc": _sb(128, i32),
     "bi": _sb(16, i32), "pos": _sb(8, u16), "posm": _sb(8, u16),
-    "blA": _sb(8, u16), "blB": _sb(8, u16), "bl4": _sb(8, u16), "key16": _sb(8, u16), "off16": _sb(8, u16), "ho16": _sb(8, u16), "a16": _sb(8, u16),
+    "blA": _sb(8, u16), "blB": _sb(8, u16), "bl4": _sb(8, u16), "key16": _sb(8, u16), "off16": _sb(16, u16), "ho16": _sb(16, u16), "a16": _sb(8, u16),
     "tg": _sb(16, f32), "z": _sb(128, bf), "xx": _sb(128, bf), "x1": _sb(128, bf), "TT": _sb(128, bf),
     "yj": _sb(128, bf), "wq": _sb(128, bf), "ff": _sb(128, bf),
     "sel": _sb(128, f32), "selm": _sb(128, f32), "nmz": _sb(128, f32), "nm3": _sb(128, f32), "ks": _sb(128, f32), "noh": _sb(128, f32),
     "Kb": _sb(128, f32), "DKp": _sb(16, f32),
-    "DG": _sb(256, f32), "DK": _sb(256, f32), "LT": _sb(128, f32), "U": _sb(128, f32), "K3": _sb(512, f32), "NM": _sb(512, f32),
+    "DG": _sb(256, i32), "DK": _sb(256, f32), "LT": _sb(128, f32), "U": _sb(128, f32), "K3": _sb(512, f32), "NM": _sb(512, f32),
     "ZC": _sb(512, f32), "K4": _sb(512, f32), "TC": _sb(512, f32), "hi": _sb(128, i32), "ci": _sb(128, i32),
-    "LP": _sb(8, u16), "exG": _sb(8, bf), "PA": _sb(16, bf),
+    "LP": _sb(24, u16), "PW": _sb(384, f32), "QW": _sb(256, bf), "exG": _sb(8, bf), "PA": _sb(16, bf),
     "vG": _sb(8, f32), "ar": _sb(128, f32), "LG": _sb(NL * LW, f32), "HL": _sb(NL * LW, f32),
     "PXB": _sb(4096, bf), "XS": _sb(256, f32), "XR": _sb(256, f32), "XD": ("dram", [8, 128, 32], f32), "XL": ("dram", [8, 128, 32], f32),
     "XB": _sb(4096, bf), "CS": ("dram", [8, 128, 148], u16), "CL": ("dram", [8, 128, 148], u16),
@@ -119,12 +120,22 @@ def _order(ops):
         order = best[1]
         mid = [i for i in order if ops[i]["t"] in (1, 2, 3)]
         order = _alike(ops, pred, succ, order, _improve(ops, pred, succ, mid, TRIES, True))
-        head = [i for i in order if ops[i]["t"] in (-1, 0)]
-        tail = [i for i in order if ops[i]["t"] in (RO - 1, RO)]
-        for sub in (head, tail):
-            new = iter(_improve(ops, pred, succ, sub, TRIES // 4, False))
-            inside = set(sub)
-            order = _valid(pred, succ, [next(new) if i in inside else i for i in order])
+        for rounds, free in (((-1, 0, 1), (-1, 0)), ((RO - 2, RO - 1, RO), (RO - 1, RO))):
+            sub = [i for i in order if ops[i]["t"] in rounds]
+            new, inside = _improve(ops, pred, succ, sub, TRIES // 4, False, free), set(sub)
+            lines = {}
+            for q in sorted(set(o["q"] for o in ops)):
+                mine = iter([i for i in new if ops[i]["q"] == q])
+                lines[q] = [next(mine) if i in inside else i for i in order if ops[i]["q"] == q][::-1]
+            order, seen = [], set()
+            while len(order) < n:
+                for q in lines:
+                    while lines[q] and all(d in seen for d in pred[lines[q][-1]]):
+                        seen.add(lines[q][-1])
+                        order.append(lines[q].pop())
+            st = _times(ops, order)[1]
+            place = {i: k for k, i in enumerate(order)}
+            order.sort(key=lambda i: (st[i], place[i]))
         KEPT[n] = order
     return KEPT[n]
 
@@ -179,7 +190,7 @@ def _times(ops, order):
     return max(fin.values()), st
 
 
-def _improve(ops, pred, succ, order, tries, alike):
+def _improve(ops, pred, succ, order, tries, alike, free=(1, 2, 3)):
     n = len(order)
     at = {i: k for k, i in enumerate(order)}
     qs = sorted(set(ops[i]["q"] for i in order))
@@ -190,7 +201,7 @@ def _improve(ops, pred, succ, order, tries, alike):
     same = {}
     for k, i in enumerate(order):
         same.setdefault(ops[i]["lab"] if alike else k, []).append(k)
-    labs = [v for v in same.values() if ops[order[v[0]]]["fn"]]
+    labs = [v for v in same.values() if ops[order[v[0]]]["fn"] and ops[order[v[0]]]["t"] in free]
 
     def run(seq):
         free, fin, end, why, prev = [0.0] * len(qs), [0.0] * n, [0.0] * n, [-1] * n, [-1] * len(qs)
@@ -225,7 +236,7 @@ def _improve(ops, pred, succ, order, tries, alike):
         k, out = res[3].index(max(res[3])), []
         while res[2][k] >= 0:
             y = res[2][k]
-            if rows[y][0] == rows[k][0] and y not in pr[k]:
+            if rows[y][0] == rows[k][0] and y not in pr[k] and rnd[y] in free and rnd[k] in free:
                 out.append((y, k))
             k = y
         return out
@@ -266,7 +277,7 @@ def _improve(ops, pred, succ, order, tries, alike):
         if res[0] <= cur + SLACK * (1 - it / tries):
             cur, chain = res[0], links(res)
             new = places(seq, res[1])
-            if all(new[d] < new[k] for k in range(n) for d in pr[k]) and run(sorted(range(n), key=lambda k: new[k]))[0] <= cur + 1e-6:
+            if alike and all(new[d] < new[k] for k in range(n) for d in pr[k]) and run(sorted(range(n), key=lambda k: new[k]))[0] <= cur + 1e-6:
                 key = new
             if cur < best:
                 best, kept = cur, list(key)
@@ -427,7 +438,7 @@ def rank_program(g, core, T, topo):
                                         src=src(d), dst=dst))
             sent[0] += len(es)
         a = op("g", lambda: g.remote_dma_fused(tr, local_sem=T.sem.ls), rd, [], issue, None, "", (), after)
-        return a, op("link", None, [], [], hold, None, "", (), [a])
+        return a, op("link" if part[1] < 0 or part[0] == 7 else sem[:2], None, [], [], hold, None, "", (), [a])
 
     def m(n, lo=0, hi=128, st=1):
         buf, k = ("MB", MB.index(n)) if n in MB else ("MF", MF.index(n))
@@ -457,8 +468,9 @@ def rank_program(g, core, T, topo):
     dma("a", T.SH[:, 160:161], T.wu[:], "dsm", wr=[r("SH", 160, 161)], lat=5.6)
     op("g", lambda: g.iota(T.PI[:, 0:1], [[0, 1]], 0, 1), [], [r("PI", 0, 1)], 0.15)
     iota(r("IOT", 0, 128), [[1, 128]], 0, 0)
-    iota(r("CQ", 0, 128), [[1, 16], [16, 8]], 0, -1)
+    iota(r("CQ", 256, 264), [[1, 2], [32, 4]], 0, 0)
     iota(r("CP"), [[1, 128]], 0, -1)
+    iota(r("CQ", 0, 128), [[1, 8], [8, 16]], 0, -1)
     iota(r("CQ", 128, 256), [[1, 8], [0, 16]], 0, 0)
     ways = {}
 
@@ -476,7 +488,9 @@ def rank_program(g, core, T, topo):
         act(r("TB", XO + mid, XO + hi), r("XB", mid, hi))
 
     z, x, x1, f = r("z"), r("xx"), r("x1"), r("ff")
-    nat, per, oh, Y = r("vl", 0, 8), r("vl", 8, 16), r("OH"), r("Y")
+    per, per2, nat, oh, Y = r("vl", 0, 8), r("vl", 8, 16), r("vl", 16, 24), r("OH"), r("Y")
+    LP, LQ1, LQ2 = r("LP", 0, 8), r("LP", 8, 16), r("LP", 16, 24)
+    Mp, Bp, NMp, fq, zq = r("PW", 0, 128), r("PW", 128, 256), r("PW", 256, 384), r("QW", 0, 128), r("QW", 128, 256)
     par, aG = r("PA", 0, 8), r("PA", 8, 16)
     acol, gcol = r("COL", 0, 1), r("COL", 1, 2)
     lane, l128, l4, th = r("GL", 0, 8), r("GB", 8, 16), r("GB", 0, 8), r("GL", 24, 32)
@@ -486,17 +500,12 @@ def rank_program(g, core, T, topo):
         mm(b, src, sh, True, True)
         act(r("TT"), b)
 
-    def permuted(o, l, src, stop):
-        for k in range(8):
-            mm(r(o[1], o[2] + k, o[2] + 128, 8), l, r(src, 16 * k, 16 * k + 16), False, stop and k == 7)
+    def spread(e, l, src):
+        mms(r(e, 0, src[4]), [(m("I"), r("MASK", 0, src[4])), (l, src)])
 
-    def spread(l, src):
-        mm(r("PM", 0, 256), m("I"), r("MASK"), True, False)
-        mm(r("PM", 0, 128), l, r(src), False, False)
-        permuted(r("PM", 128, 256), l, src, True)
-
-    def lists():
-        scan(r("DG"), r("RB"), r("PM", 0, 256), 0.0, A.add, A.min)
+    def lists(e, lo, w):
+        scan(r("DG", lo, lo + w), r("RB", 0, w), r(e, 0, w), 0.0, A.add, A.min)
+        return r("DG", lo + 15, lo + w, 16)
 
     piece(0)
     piece(1)
@@ -514,7 +523,14 @@ def rank_program(g, core, T, topo):
     ts(r("OH", 0, 16), r("IOT", 0, 16), acol, A.is_equal)
     cp(nat, r("CI", 1024, 1032))
     cp(r("OH", 16, 32), r("OH", 0, 16))
-    ts(m("PM1"), r("CQ", 0, 128), 0.0, A.is_equal)
+    ts(r("PI", 5, 6), r("PI", 0, 1), 7, A.bitwise_and)
+    ts(r("PI", 6, 7), r("PI", 2, 3), 3, A.arith_shift_right)
+    cp(r("COL", 8, 10), r("PI", 5, 7))
+    ts(r("COL", 10, 11), r("COL", 8, 9), 16.0, A.mult, r("COL", 9, 10), A.add)
+    ts(r("COL", 12, 13), r("COL", 8, 9), 2.0, A.mult)
+    ts(LQ1, r("IOT", 0, 16, 2), r("COL", 10, 11), A.add)
+    ts(r("COL", 11, 12), r("COL", 9, 10), 16.0, A.mult, r("COL", 12, 13), A.add)
+    ts(LQ2, r("CQ", 256, 264), r("COL", 11, 12), A.add)
     cp(r("OH", 32, 64), r("OH", 0, 32))
     ts(m("I"), r("CP"), 0.0, A.is_equal)
     cp(r("OH", 64, 128), r("OH", 0, 64))
@@ -524,20 +540,23 @@ def rank_program(g, core, T, topo):
     ts(r("MASK"), r("OH", 0, 256), -BIG / 2, A.mult, BIG / 2, A.add)
     for w in (128, 256, 512):
         act(r("IOT", w, 2 * w), r("IOT", 0, w), bias=float(w))
-    act(r("VR"), ind(r("IOT"), nat))
-    spread(m("I32"), "VR")
+    act(r("VR", 0, 128), ind(r("IOT"), nat))
+    act(r("VR", 128, 384), ind(r("VR", 0, 128), r("LP", 8, 24)))
+    spread("PM", m("I32"), r("VR", 128, 384))
+    act(zq, ind(r("SH", 0, 128), LQ2))
     for k in range(16):
         ts(r("WN", 128 * k + k, 128 * k + 128, 16), r("G8", 0, 8), -2048.0, A.mult)
-        act(r("EP", k, 2048, 16), m("PM1"))
-    turn(r("SH", 0, 128), m("I"))
+        act(r("EP", k, 2048, 16), m("I"))
+    turn(zq, m("I"))
     cp(r("HU", 0, 1032), r("CI"))
     cp(r("SF", 0, 144), r("SH", 0, 144))
     cp(r("SF", 144, 145), r("SH", 160, 161))
-    lists()
+    both = lists("PM", 0, 256)
     cp(r("HU", 1032, 1177), r("SF", 0, 145))
-    cp(per, r("DG", 143, 256, 16))
+    cp(r("vl", 0, 16), both)
     cp(m("POS"), r("IOT", 0, 128))
     ts(r("COL", 2, 3), acol, 128.0, A.mult)
+    ts(m("POS1"), r("IOT", 0, 128), 0.0, A.mult, r("COL", 2, 3), A.add)
     for w in (256, 512, 1024):
         cp(r("OH", w, 2 * w), r("OH", 0, w))
     dma("s", T.CS[:], T.HU[:], "dcs", rd=[r("HU")], wr=[dr("CS", 0, 1)], lat=3.8)
@@ -562,6 +581,7 @@ def rank_program(g, core, T, topo):
             act(m(dst, k, 128), m(src, 0, 128 - k))
             act(m(dst, 0, k), m(src, 128 - k, 128))
         ts(m("BO32"), r("CQ", 128, 256), gcol, A.is_equal)
+        ts(m("PM1"), r("CQ", 0, 128), 0.0, A.is_equal)
         roll("S", "I", 16)
         roll("SB", "I", 112)
         roll("BS32", "BO32", 16)
@@ -580,29 +600,26 @@ def rank_program(g, core, T, topo):
         ts(th, lane, 128.0, A.mult, 13.0, A.add)
         act(r("G8", 9, 16), r("G8", 0, 7))
         act(r("G8", 8, 9), r("G8", 7, 8))
-        for nme, src, sc in (("nI32", "I32", -1.0), ("BOK", "BO32", KS_), ("S2", "S", 2.0), ("nI2", "I", -2.0)):
+        for nme, src, sc in (("BOK", "BO32", KS_), ("S2", "S", 2.0), ("nI2", "I", -2.0)):
             act(m(nme), m(src), scale=sc)
         counts()
-        for nme, v0, vs, at in (("RR", 0.0, BIG, 15), ("R0", 1.0, 0.0, 0), ("SENT", 0.0, ZP * KS_, 0)):
-            ms(r(nme), v0)
-        ms(m("Z"), 0.0)
+        ms(r("RR"), 0.0)
+        ms(r("SENT"), 0.0)
         ms(r("CMP"), KS_)
         ms(r("CD"), 0.0)
         ms(r("RR", 15, None, 16), BIG)
-        ms(r("R0", 0, None, 16), 0.0)
         ms(r("SENT", 0, 1), ZP * KS_)
-        ts(r("COL", 3, 4), acol, 128.0, A.mult, 2047.0, A.add)
         ts(r("COL", 6, 7), acol, 8.0, A.mult)
         ts(r("COL", 4, 5), acol, 150.0, A.mult, 149.0, A.add)
         ts(r("COL", 5, 6), acol, -134.0, A.mult, 1068.0, A.add)
-        ts(r("LP"), r("IOT", 0, 8), r("COL", 6, 7), A.add)
+        ts(LP, r("IOT", 0, 8), r("COL", 6, 7), A.add)
         ts(r("FL", 0, 1), r("COL", 4, 5), r("COL", 5, 6), A.min)
         for c in range(8):
             ts(r("CD", SEG[c] + 1 + 16 * c, SEG[c] + 17 + 16 * c), r("OH", 0, 16), -4 * KS_, A.mult)
         for at, st, val in ((0, 150, KS_), (131, 134, KS_), (129, 134, 4 * KS_), (148, 150, 4 * KS_)):
             ms(r("CD", at, at + 3 * st + 1, st), val)
-        ts(r("CD", 130, 130 + 3 * 134 + 1, 134), r("IOT", 0, 4), -16.0, A.mult, 112.0, A.add)
-        ts(r("CD", 149, 149 + 3 * 150 + 1, 150), r("IOT", 0, 4), 16.0, A.mult)
+        cp(r("CD", 130, 130 + 3 * 134 + 1, 134), (T.GL[:, 7:3:-1], "GL", 4, 8, 4))
+        cp(r("CD", 149, 149 + 3 * 150 + 1, 150), r("GL", 0, 4))
         land(0)
         land(1)
         dma("s", T.WU[:], T.CL[:], "dwu", rd=[dr("CL", 0, 1)], wr=[r("WU")], lat=2.5, pre=[("ac", sum(len(es) for _, es in calls[0]))], after=[lc])
@@ -634,6 +651,7 @@ def rank_program(g, core, T, topo):
     def probe(step, win=XW):
         pd = r("PD", 0, 128)
         mm(pd, m("I"), m("POS"), True, False)
+        mm(pd, m("I"), m("POS1"), False, False)
         if step == 1:
             mm(pd, m("I"), m("POS2"), False, False)
         def bank(a0, a1):
@@ -663,12 +681,13 @@ def rank_program(g, core, T, topo):
             for a in range(a0, a1):
                 blk = (128 * a, 128 * a + 128)
                 if what == "gather" and step == 2:
-                    mm(r("PX", 0, 128), r("WD", *blk), r("Y", *blk), first, False)
+                    mm(r("PX", 0, 128), r("WN", *blk), r("Y", *blk), first, False)
                     first = False
                 if what == "take":
                     mm(pd, r("WD" if e == "a" else "WN", *blk), r("AB", *blk), False, False)
                     if e == "v" and step > 1:
                         mm(pd, r("WD", *blk), r("EX", *blk), False, False)
+        return prev["v"]
 
     def counts():
         b = r("PX", 0, 8)
@@ -678,13 +697,15 @@ def rank_program(g, core, T, topo):
     def least():
         scan(r("rm"), r("RB", 0, 128), r("PD", 0, 128), 0.0, A.add, A.min)
 
-    def decode(out, src, t0, t1, flip=False):
-        cp(r(t0, 0, 8), r(src, 15, 128, 16))
-        ts(r(t1), r(t0, 0, 8), 2047, A.bitwise_and)
-        if flip:
-            ts(out, r(t1), -1.0, A.mult, r("COL", 3, 4), A.add)
+    def low(out, src, mask, tmp):
+        if U16AND:
+            ts(out, src, mask, A.bitwise_and)
         else:
-            ts(out, r(t1), r("COL", 2, 3), A.add)
+            ts(tmp, src, mask, A.bitwise_and)
+            cp(out, tmp)
+
+    def decode(out, src, tmp):
+        low(out, r(src, 15, 128, 16), 2047, r(tmp))
 
     def send_log(s):
         lg = r("LG", LW * s, LW * s + LW)
@@ -695,13 +716,16 @@ def rank_program(g, core, T, topo):
         hl = r("HL", LW * s, LW * s + LW)
         dma("s", hl[0], T.LL[8 * s:8 * s + 8], "lh%d" % s, rd=[dr("LL", s, s + 1)], wr=[hl], pre=[("la%d" % s, N - 1)], after=[l])
 
-    def apply_log(s):
+    def apply_log(s, after=()):
         if s < 0:
-            return
-        last_ = len(ops) - 1
-        ts(r("ho16"), r("HL", LW * s + 256, LW * s + 264), acol, A.add)
-        behind[:] = [last_]
-        tt(ind(r("HB"), r("ho16")), r("HL", LW * s, LW * s + 128), r("HL", LW * s + 128, LW * s + 256), A.add)
+            return []
+        ho = r("ho16", 8 * (s % 2), 8 * (s % 2) + 8)
+        keep, part[0] = part[0], 10 + s % 2 if part[1] < RO else part[0]
+        cp(ho, r("HL", LW * s + 256, LW * s + 264))
+        behind[:] = after
+        tt(ind(r("HB"), ho), r("HL", LW * s, LW * s + 128), r("HL", LW * s + 128, LW * s + 256), A.add)
+        part[0] = keep
+        return [len(ops) - 1]
 
     def keys(vc):
         mm(r("PM", 0, 128), m("I"), r("MASK", 0, 128), True, False)
@@ -718,15 +742,18 @@ def rank_program(g, core, T, topo):
                 ts(o, r("E1", 0, 16 * c + 17), own_, A.not_equal, KS_, A.mult)
             else:
                 act(o, r("E2", 0, 16 * c + 17), F.Abs, bias=own_, scale=-1.0)
-        ts(r("DKp"), r("DK", 15, 256, 16), 1 / KS_, A.mult, acol, A.subtract)
+        ts(r("DKp"), r("DK", 15, 256, 16), 1 / KS_, A.mult)
 
     def winners(s):
         scan(r("WO"), r("CMP"), r("CD"), 0.0, A.min, A.add)
         o = r("LG", LW * s + 256, LW * s + 272)
+        if s < NL - 1 and U16TT:
+            tt(r("off16"), ind(r("WO"), r("FL", 0, 1)), r("DKp"), A.min)
         tt(o, ind(r("WO"), r("FL", 0, 1)), r("DKp"), A.min)
         if s < NL - 1:
-            ts(r("off16"), r("LG", LW * s + 256, LW * s + 264), acol, A.add)
-            tt(ind(AW, r("off16")), r("LG", LW * s, LW * s + 128), r("LG", LW * s + 128, LW * s + 256), A.add)
+            if not U16TT:
+                cp(r("off16", 0, 8), r("LG", LW * s + 256, LW * s + 264))
+            tt(ind(AW, r("off16", 0, 8)), r("LG", LW * s, LW * s + 128), r("LG", LW * s + 128, LW * s + 256), A.add)
 
     def rev(n):
         return (T[n][:, 127::-1], n, 0, 128, 128)
@@ -738,43 +765,43 @@ def rank_program(g, core, T, topo):
         la, lb = r("LG", LW * 2 * t, LW * 2 * t + 128), r("LG", LW * 2 * t + 128, LW * 2 * t + 256)
         part[:] = [1, t]
         cells = CW if t else r("CI", 0, 1024)
-        cp(r("L16"), ind(cells, per))
-        act(r("Lf"), ind(cells, nat), bias=float(XO))
+        cp(r("L16"), ind(cells, per2))
+        act(r("Lf"), ind(cells, per), bias=float(XO))
         if t:
             counts()
         probe(1, XW if t else r("PXB"))
         least()
-        decode(pos, "rm", "ti", "tj")
+        decode(pos, "rm", "tj")
         sel = r("sel") if t else r("XR", 128, 256)
         cp(x if t else r("XS", 0, 128), ind(Y, pos))
-        apply_log(2 * t - 3)
         tt(sel if t else r("XS", 128, 256), ind(oh, pos), r("Lf"), A.mult)
         if not t:
             part[0] = 7
             hand_over()
         part[0] = 2
-        spread(m("WUm"), "xx")
-        lists()
+        spread("PM", m("WUm"), x)
         turn(x, m("S"))
-        cp(r("ti"), r("DG", 15, 256, 16))
-        ts(r("bi"), r("ti"), 1023, A.bitwise_and)
-        cp(r("vl"), r("bi"))
+        low(per, lists("PM", 0, 128), 1023, r("bi", 0, 8))
         cp(r("L16"), ind(CW, per))
-        b = r("A0", 0, 128)
-        mm(b, m("S"), x, True, True)
+        b, bn = r("A0", 0, 128), r("E3", 0, 128)
+        mm(b, r("TT"), m("PM1"), True, True)
         act(x1, b)
-        act(kM, ind(CW, nat), bias=MG + XO)
-        act(r("K3", 2, 512, 4), ind(r("IOT"), nat), bias=MG + CO)
-        probe(2)
-        apply_log(2 * t - 2)
-        mms(b, [(m("BS32"), sel), (m("nI32"), kM)])
-        act(r("NM", 1, 512, 4), b, bias=MG)
+        mm(bn, m("BS32"), sel, True, True)
+        act(Mp, ind(CW, per), bias=MG + XO)
+        act(Bp, ind(r("IOT"), per), bias=MG + CO)
+        act(kM, ind(Mp, LP))
+        act(r("K3", 2, 512, 4), ind(Bp, LP))
+        taken = probe(2)
+        homes = (apply_log(2 * t - 3, taken) + apply_log(2 * t - 2, taken))[:PIN]
+        tt(NMp, bn, Mp, A.subtract)
+        act(r("NM", 1, 512, 4), ind(NMp, LP), bias=MG)
         part[0] = 5
         act(r("LT"), r("PD", 0, 128), F.Sign, bias=-(240 * 2048 - 0.5))
+        behind[:] = homes
         least()
-        act(r("PDs"), r("PD", 0, 128), bias=8388608.0 + 2047.0, scale=-1.0)
+        act(r("PDs"), r("PD", 0, 128), bias=-8388608.0)
         mm(r("PX", 0, 128), m("I32"), r("PDs"), False, True)
-        decode(pos, "rm", "ti", "tj")
+        decode(pos, "rm", "tj")
         scan(r("U"), r("RC"), r("LT"), -BIG, A.max, A.add)
         ts(blB, r("U", 15, 128, 16), 35.0, A.add, 1.0 / 32, A.mult)
         ts(blA, r("U", 15, 128, 16), 3.0, A.add, 1.0 / 32, A.mult)
@@ -783,16 +810,15 @@ def rank_program(g, core, T, topo):
         scan(rev("hold"), rev("RR"), rev("rm"), 0.0, A.add, A.min)
         tt(r("ne"), r("PD", 0, 128), r("hold"), A.not_equal)
         tt(r("mk"), r("PX", 0, 128), r("ne"), A.mult)
-        scan(r("rm2"), r("R0"), r("mk"), 0.0, A.mult, A.max)
-        decode(posm, "rm2", "tk", "tl", True)
+        scan(r("rm2"), r("RB", 0, 128), r("mk"), 0.0, A.add, A.min)
+        decode(posm, "rm2", "tl")
         tt(f, ind(Y, posm), x1, A.max)
         tt(r("ks"), ind(oh, pos), r("Kb"), A.mult)
         bq = r("PX", 0, 128)
-        mm(bq, m("I"), m("Z"), True, False)
-        permuted(bq, m("KP"), "ff", True)
+        (act if FQ == "a" else cp)(fq, ind(f, LQ1))
+        mm(bq, m("KP"), fq, True, True)
         cp(r("hi"), bq)
-        ts(r("ci"), r("hi"), 4095, A.bitwise_and)
-        cp(r("L16"), r("ci"))
+        low(r("L16"), r("hi"), 4095, r("ci"))
         keys(VCMP[0])
         act(r("nmz"), ind(r("NM"), blA))
         tt(lb, ind(oh, pos), r("nmz"), A.mult)
@@ -802,18 +828,18 @@ def rank_program(g, core, T, topo):
         act(r("K3", 0, 512, 4), b, bias=MG + XO, scale=0.4995)
         act(r("ZC", 0, 512, 4), b3, bias=MG)
         act(la, ind(r("K3"), blA), bias=-(MG + XO))
-        turn(f, m("S"))
+        turn(fq, m("S"))
         winners(2 * t)
         send_log(2 * t)
         tt(r("exG"), r("U", 15, 128, 16), th, A.is_lt)
         tt(r("selm"), ind(oh, posm), kM, A.mult)
-        if last:
-            cp(r("vG"), r("bi", 0, 8))
         part[0] = 3
         la, lb = r("LG", LW * (2 * t + 1), LW * (2 * t + 1) + 128), r("LG", LW * (2 * t + 1) + 128, LW * (2 * t + 1) + 256)
-        act(k4, ind(r("ci"), r("LP")), bias=float(XO))
-        ts(r("hi"), r("ci"), 1023, A.bitwise_and)
-        act(r("K4", 1, 512, 4), ind(r("hi"), r("LP")), bias=float(CO))
+        if U16AND:
+            ts(r("ci"), r("hi"), 4095, A.bitwise_and)
+        act(k4, ind(r("ci"), LP), bias=float(XO))
+        ts(r("cc"), r("hi"), 1023, A.bitwise_and)
+        act(r("K4", 1, 512, 4), ind(r("cc"), LP), bias=float(CO))
         b = r("A0", 0, 128)
         mm(b, m("BS32"), r("selm"), True, True)
         act(r("nm3"), b, bias=-float(XO))
@@ -822,6 +848,9 @@ def rank_program(g, core, T, topo):
         mms(r("A0", 0, 8), [(m("S"), par), (m("nI2"), r("exG"))])
         mms(r("A0", 8, 16), [(m("S"), aG), (m("I"), r("exG"))])
         act(r("PA"), r("A0", 0, 16), F.Abs)
+        act(r("VR", 0, 128), ind(Bp, LP if last else LQ1), bias=-(MG + CO))
+        spread("A0", m("I32"), r("VR", 0, 128))
+        cp(r("vG") if last else per2, lists("A0", 128, 128))
         if last:
             cp(r("a16"), aG)
             act(r("ar"), ind(r("IOT"), r("a16")))
@@ -835,11 +864,14 @@ def rank_program(g, core, T, topo):
         least()
         part[0] = 4
         ts(r("tg", 8, 16), r("rm", 15, 128, 16), 640.0 * 2048, A.is_ge)
-        tt(r("tg", 0, 8), l4e, r("tg", 8, 16), A.add)
-        cp(bl4, r("tg", 0, 8))
+        if U16TT:
+            tt(bl4, l4e, r("tg", 8, 16), A.add)
+        else:
+            tt(r("tg", 0, 8), l4e, r("tg", 8, 16), A.add)
+            cp(bl4, r("tg", 0, 8))
         line["a"] = []
         act(r("Kb"), ind(r("K4"), bl4))
-        decode(pos, "rm", "ti", "tj")
+        decode(pos, "rm", "tj")
         act(r("wq"), ind(Y, pos))
         tt(r("ks"), ind(oh, pos), r("Kb"), A.mult)
         bz, bh = r("PX", 0, 128), r("PD", 0, 128)
@@ -848,7 +880,8 @@ def rank_program(g, core, T, topo):
         act(z, ind(r("ZC"), blA), F.Abs, bias=-MG)
         keys(VCMP[1])
         if not last:
-            turn(z, m("I"))
+            act(zq, ind(z, LQ2))
+            turn(zq, m("I"))
         line.clear()
         tt(r("TC", 1, 512, 4), ind(r("W2"), pos), r("nm3"), A.min)
         mms(bh, [(m("S"), f), (m("I"), r("wq"))])

from concourse.bass import DstId, RemoteDMATransfer
from concourse.mybir import AluOpType, ActivationFunctionType

A = AluOpType
F = ActivationFunctionType
N, RO = 8, 5
XO, ZP, CO, TW, SM = 128, 4224, 4232, 5256, 5416
MG = 12582912.0
BIG = 268435456.0
KS_ = 8192.0
SEG = [134 * c + 131 if c < 4 else 150 * (7 - c) for c in range(8)]
NL = 2 * RO
CUTS = ((0, 1024), (1024, 2048), (2048, 3072), (3072, 3584), (3584, 4096))
LW = 272
f32, bf, i32, u16 = "float32", "bfloat16", "int32", "uint16"
MB = ("I", "S", "SB", "S2", "nI", "nI2", "BSb", "WUm", "KP", "PM1", "POS", "POS2", "POS1")
U16AND, U16TT, FQ, PIN = False, True, "a", 0
MF = ("I32", "BO32", "BS32", "BOK")
PS = ("E0", "E1", "E2", "E3", "PD", "PX", "PM", "A0")
CYC, PCYC, HOP = 0.95e-3, 0.5e-3, 0.09
VCMP = ((7, 6), (7, 6, 5, 4))
PASSES = 4
KEPT = {}
TRIES, REACH, SLACK, MEAN = 10000, 1.0, 0.03, 0.1
MARK, MARK2 = (1, "v", "rm", 0), (2, "v", "DG", 0)
G_, X_ = "gather", "take"
FAR = ((G_, "a", 4, 6), (G_, "v", 10, 12), (G_, "a", 14, 16), (G_, "v", 0, 4), (X_, "a", 10, 12), (X_, "a", 4, 6), (G_, "v", 12, 14), (X_, "a", 14, 16),
       (G_, "v", 8, 10), (X_, "a", 0, 4), (G_, "v", 6, 8), (X_, "a", 12, 14), (X_, "v", 6, 8), (X_, "a", 8, 10))
NEAR = ((G_, "a", 0, 2), (G_, "v", 4, 8), (X_, "v", 0, 2), (G_, "a", 12, 16), (X_, "v", 4, 8), (G_, "a", 8, 11), (X_, "v", 12, 16), (G_, "a", 2, 4),
        (X_, "v", 8, 11), (G_, "a", 11, 12), (X_, "v", 2, 4), (X_, "v", 11, 12))
PLAN = (NEAR, FAR, FAR)
SPARE = ({}, {8: "PM", 12: "A0"}, {8: "PM", 12: "PX"})


def _sb(w, d):
    return ("sbuf", [128, w], d)


SCRATCH = {
    "TB": _sb(SM, f32), "HB": _sb(TW, f32), "HU": _sb(1184, u16), "WU": _sb(1184, u16), "CI": _sb(1032, i32), "SF": _sb(160, f32), "SH": _sb(176, bf),
    "EX": _sb(2048, bf), "GB": _sb(16, bf), "ALL": _sb(64, u16), "WN": _sb(2048, bf), "W2": _sb(2048, bf), "SENT": _sb(136, bf),
    "Y": _sb(2048, bf), "AB": _sb(2048, bf), "EP": _sb(2048, bf), "OH": _sb(2048, bf), "WD": _sb(2048, bf),
    "MB": _sb(128 * len(MB), bf), "MF": _sb(128 * len(MF), f32),
    "IOT": _sb(1024, f32), "CP": _sb(128, f32), "CQ": _sb(264, f32), "PI": _sb(8, i32), "COL": _sb(16, f32), "G8": _sb(16, f32),
    "MASK": _sb(256, bf), "RB": _sb(256, f32), "RR": _sb(128, f32), "RC": _sb(128, f32),
    "GL": _sb(32, f32), "FL": _sb(2, u16), "CMP": _sb(600, bf), "CD": _sb(600, bf), "WO": _sb(600, bf),
    "SMB": _sb(32, bf), "KS": _sb(32, f32), "VR": _sb(384, f32),
    "vl": _sb(24, u16), "L16": _sb(128, u16), "Lf": _sb(128, f32), "rm": _sb(128, i32), "hold": _sb(128, f32), "ne": _sb(128, f32),
    "mk": _sb(128, f32), "rm2": _sb(128, i32), "PDs": _sb(128, f32), "tj": _sb(8, i32), "tl": _sb(8, i32), "cc": _sb(128, i32),
    "bi": _sb(16, i32), "pos": _sb(8, u16), "posm": _sb(8, u16),
    "blA": _sb(8, u16), "blB": _sb(8, u16), "bl4": _sb(8, u16), "key16": _sb(8, u16), "off16": _sb(16, u16), "ho16": _sb(16, u16), "a16": _sb(8, u16),
    "tg": _sb(16, f32), "z": _sb(128, bf), "xx": _sb(128, bf), "x1": _sb(128, bf), "TT": _sb(128, bf),
    "yj": _sb(128, bf), "wq": _sb(128, bf), "ff": _sb(128, bf),
    "sel": _sb(128, f32), "selm": _sb(128, f32), "nmz": _sb(128, f32), "nm3": _sb(128, f32), "ks": _sb(128, f32), "noh": _sb(128, f32),
    "Kb": _sb(128, f32), "DKp": _sb(16, f32),
    "DG": _sb(256, i32), "DK": _sb(256, f32), "LT": _sb(128, f32), "U": _sb(128, f32), "K3": _sb(512, f32), "NM": _sb(512, f32),
    "ZC": _sb(512, f32), "K4": _sb(512, f32), "TC": _sb(512, f32), "hi": _sb(128, i32), "ci": _sb(128, i32),
    "LP": _sb(24, u16), "PW": _sb(384, f32), "QW": _sb(256, bf), "exG": _sb(8, bf), "PA": _sb(16, bf),
    "vG": _sb(8, f32), "ar": _sb(128, f32), "LG": _sb(NL * LW, f32), "HL": _sb(NL * LW, f32),
    "PXB": _sb(4096, bf), "XS": _sb(256, f32), "XR": _sb(256, f32), "XD": ("dram", [8, 128, 32], f32), "XL": ("dram", [8, 128, 32], f32),
    "XB": _sb(4096, bf), "CS": ("dram", [8, 128, 148], u16), "CL": ("dram", [8, 128, 148], u16),
    "LS": ("dram", [NL * 8, 128, LW // 8], f32), "LL": ("dram", [NL * 8, 128, LW // 8], f32), "ZS": ("dram", [8, 128, 16], bf), "ZL": ("dram", [8, 128, 16], bf),
    "VS": ("dram", [8, 128, 2], f32), "VL": ("dram", [8, 128, 2], f32),
}
for _k, (_lo, _hi) in enumerate(CUTS):
    SCRATCH["PS%d" % _k] = SCRATCH["PL%d" % _k] = ("dram", [8, 128, (_hi - _lo) // 8], bf)
for _m in PS:
    SCRATCH[_m] = ("psum", [128, 512], f32)
SEMAPHORES = (["qv", "qa", "qp", "qg", "ls", "dce", "dsm", "xo", "dxo", "dv0", "dz0", "dcs", "ac", "dwu", "dhb", "dvs", "dvo", "av", "dzs", "az", "dout", "dyx", "dpb", "dxs", "dxr", "ah"]
              + ["%s%d" % (p, k) for p in ("xs", "ay", "xl") for k in range(len(CUTS))]
              + ["%s%d" % (p, k) for p in ("lt", "la", "lh") for k in range(NL)])


def _mask(es):
    m = 0
    for e in es:
        m |= 1 << e
    return m


def _calls(src, cores, topo):
    me = cores.index(src)
    kinds = {"on": [], "mate": [], "plane": [], "far": []}
    for k in range(1, N):
        r = (me + k) % N
        a, b = topo.chip(src), topo.chip(cores[r])
        kinds["on" if a == b else "mate" if topo.mates(a, b) else "plane" if topo.same_plane(a, b) else "far"].append(r)
    for k in ("mate", "plane", "far"):
        kinds[k].sort(key=lambda r: topo.die(cores[r]) != topo.die(src))
    off = topo.engines(src, cores[kinds["far"][0]])
    on = [e for e in topo.engines(src, cores[kinds["on"][0]]) if e not in off]
    calls = []
    for k, two in enumerate(("far", "mate", "plane")):
        es = off[2 * k:] + off[:2 * k]
        rest = [r for kind in ("far", "mate", "plane") if kind != two for r in kinds[kind]]
        calls.append([(r, es[2 * i:2 * i + 2]) for i, r in enumerate(kinds[two])] + [(r, [es[4 + i]]) for i, r in enumerate(rest)]
                     + [(kinds["on"][0], on[:2])])
    outs = kinds["far"] + kinds["plane"] + kinds["mate"]
    single = [(r, [off[i]]) for i, r in enumerate(outs)] + [(kinds["on"][0], [on[0]])]
    return calls, single


def _order(ops):
    n = len(ops)
    if n not in KEPT:
        pred = [sorted(o["deps"]) for o in ops]
        succ = [[] for _ in ops]
        for i in range(n):
            for d in pred[i]:
                succ[d].append(i)
        prio = [0.0] * n
        for i in range(n - 1, -1, -1):
            prio[i] = ops[i]["lat"] + max([prio[s] + HOP for s in succ[i]] + [0.0])
        best = None
        for _ in range(PASSES):
            out, fin = _pass(ops, pred, succ, prio, False)
            if best is None or max(fin) < best[0]:
                best = (max(fin), out, prio)
            prio = _pass(ops, succ, pred, fin, True)[1]
        order = best[1]
        mid = [i for i in order if ops[i]["t"] in (1, 2, 3)]
        order = _alike(ops, pred, succ, order, _improve(ops, pred, succ, mid, TRIES, True))
        for rounds, free in (((-1, 0, 1), (-1, 0)), ((RO - 2, RO - 1, RO), (RO - 1, RO))):
            sub = [i for i in order if ops[i]["t"] in rounds]
            new, inside = _improve(ops, pred, succ, sub, TRIES // 4, False, free), set(sub)
            lines = {}
            for q in sorted(set(o["q"] for o in ops)):
                mine = iter([i for i in new if ops[i]["q"] == q])
                lines[q] = [next(mine) if i in inside else i for i in order if ops[i]["q"] == q][::-1]
            order, seen = [], set()
            while len(order) < n:
                for q in lines:
                    while lines[q] and all(d in seen for d in pred[lines[q][-1]]):
                        seen.add(lines[q][-1])
                        order.append(lines[q].pop())
            st = _times(ops, order)[1]
            place = {i: k for k, i in enumerate(order)}
            order.sort(key=lambda i: (st[i], place[i]))
        KEPT[n] = order
    return KEPT[n]


def _valid(pred, succ, order):
    place = {i: k for k, i in enumerate(order)}
    left, out, seen = [len(p) for p in pred], [], set()
    for i in order:
        stack = [i]
        while stack:
            j = stack[-1]
            wait = [d for d in pred[j] if d not in seen]
            if j in seen:
                stack.pop()
            elif wait:
                stack.extend(sorted(wait, key=lambda d: -place[d]))
            else:
                seen.add(j)
                out.append(stack.pop())
    return out


def _alike(ops, pred, succ, order, mid):
    st = _times(ops, mid)[1]
    ph = {ops[i]["lab"]: st[i] for i in mid if ops[i]["t"] == 2}
    span = (st[[i for i in mid if ops[i]["t"] == 3 and ops[i]["lab"] == MARK][0]] - ph[MARK])
    st = _times(ops, order)[1]
    t1, t0 = [st[[i for i in order if ops[i]["t"] == 0 and ops[i]["lab"] == k][0]] - ph[k] for k in (MARK, MARK2)]
    key = {}
    for i in range(len(ops)):
        o = ops[i]
        if o["t"] >= 0 and o["lab"] in ph:
            key[i] = (t1 if (o["t"], o["lab"][0]) == (0, 1) else t0) + o["t"] * span + ph[o["lab"]]
        elif o["t"] <= 0:
            key[i] = st[i]
        else:
            key[i] = max(key[d] + ops[d]["lat"] for d in pred[i])
    return _valid(pred, succ, sorted(range(len(ops)), key=lambda i: key[i]))


def _times(ops, order):
    free, fin, end, st = {}, {}, {}, {}
    for i in order:
        o = ops[i]
        t = free.get(o["q"], 0.0)
        for d in o["deps"]:
            if d in fin:
                t = max(t, fin[d] + HOP if d in o["wait"] else end[d])
        st[i] = t
        free[o["q"]] = end[i] = t + o["hold"]
        fin[i] = t + o["lat"]
    return max(fin.values()), st


def _improve(ops, pred, succ, order, tries, alike, free=(1, 2, 3)):
    n = len(order)
    at = {i: k for k, i in enumerate(order)}
    qs = sorted(set(ops[i]["q"] for i in order))
    rows = [(qs.index(ops[i]["q"]), ops[i]["hold"], ops[i]["lat"] + HOP, [at[d] for d in ops[i]["wait"] if d in at],
             [at[d] for d in ops[i]["deps"] if d in at and d not in ops[i]["wait"]]) for i in order]
    pr = [w + s for _, _, _, w, s in rows]
    su = [[at[d] for d in succ[i] if d in at] for i in order]
    same = {}
    for k, i in enumerate(order):
        same.setdefault(ops[i]["lab"] if alike else k, []).append(k)
    labs = [v for v in same.values() if ops[order[v[0]]]["fn"] and ops[order[v[0]]]["t"] in free]

    def run(seq):
        free, fin, end, why, prev = [0.0] * len(qs), [0.0] * n, [0.0] * n, [-1] * n, [-1] * len(qs)
        for k in seq:
            q, hold, lat, w, s = rows[k]
            t, y = free[q], prev[q]
            for d in w:
                if fin[d] > t:
                    t, y = fin[d], d
            for d in s:
                if end[d] > t:
                    t, y = end[d], d
            free[q] = end[k] = t + hold
            fin[k] = t + lat
            why[k], prev[q] = y, k
        return max(fin) + MEAN * sum(fin) / n, end, why, fin

    rnd = [ops[i]["t"] for i in order]
    ref = [([j for j in same[ops[i]["lab"]] if rnd[j] == 2] + [k])[0] if alike else k for k, i in enumerate(order)]
    mates = [same[ops[i]["lab"] if alike else k] for k, i in enumerate(order)]

    def places(seq, end):
        key = [0.0] * n
        for p, k in enumerate(seq):
            key[k] = end[k] - rows[k][1] + 1e-8 * p
        if alike:
            span = key[same[MARK][2]] - key[same[MARK][1]]
            key = [key[ref[k]] + span * (rnd[k] - rnd[ref[k]]) for k in range(n)]
        return key

    def links(res):
        k, out = res[3].index(max(res[3])), []
        while res[2][k] >= 0:
            y = res[2][k]
            if rows[y][0] == rows[k][0] and y not in pr[k] and rnd[y] in free and rnd[k] in free:
                out.append((y, k))
            k = y
        return out

    key = places(range(n), run(range(n))[1])
    seq = _valid(pr, su, sorted(range(n), key=lambda k: key[k]))
    srt = sorted(key)
    for p, k in enumerate(seq):
        key[k] = srt[p] + 1e-8 * p
    res = run(seq)
    cur, chain = res[0], links(res)
    best, kept, seed = cur, list(key), 12345
    for it in range(tries):
        seed = (seed * 1103515245 + 12345) % 2147483648
        kind = (seed >> 8) % 4
        seed = (seed * 1103515245 + 12345) % 2147483648
        if kind < 2 and chain:
            u, w = chain[(seed >> 8) % len(chain)]
            v = mates[(w, u)[kind]]
        else:
            v = labs[(seed >> 8) % len(labs)]
        reach = REACH * (1, 1, 4)[it % 3]
        lo = max([key[d] - key[k] for k in v for d in pr[k]] + [-reach])
        hi = min([key[d] - key[k] for k in v for d in su[k]] + [reach])
        if kind == 0 and chain:
            hi = key[u] - key[w]
        elif kind == 1 and chain:
            lo = key[w] - key[u]
        if lo >= hi:
            continue
        seed = (seed * 1103515245 + 12345) % 2147483648
        step = ((seed >> 8) % 998 + 1) / 1000.0
        step = hi - (hi - lo) * step ** 3 if kind == 0 else lo + (hi - lo) * step ** (3 if kind == 1 else 1)
        for k in v:
            key[k] += step
        seq = sorted(range(n), key=lambda k: key[k])
        res = run(seq)
        if res[0] <= cur + SLACK * (1 - it / tries):
            cur, chain = res[0], links(res)
            new = places(seq, res[1])
            if alike and all(new[d] < new[k] for k in range(n) for d in pr[k]) and run(sorted(range(n), key=lambda k: new[k]))[0] <= cur + 1e-6:
                key = new
            if cur < best:
                best, kept = cur, list(key)
        else:
            for k in v:
                key[k] -= step
    return [order[k] for k in sorted(range(n), key=lambda k: kept[k])]


def _pass(ops, pred, succ, prio, back):
    n = len(ops)
    left = [len(p) for p in pred]
    ready = {i: 0.0 for i in range(n) if not left[i]}
    at, fin, free, out = [0.0] * n, [0.0] * n, {}, []
    while ready:
        best = min(ready, key=lambda i: max(ready[i], free.get(ops[i]["q"], 0.0)) + ops[i]["hold"])
        q = ops[best]["q"]
        end = max(ready[best], free.get(q, 0.0)) + ops[best]["hold"]
        i = max((j for j in ready if ops[j]["q"] == q and (ready[j] < end or j == best)), key=lambda j: (prio[j], -j))
        st = max(ready.pop(i), free.get(q, 0.0))
        free[q] = st + ops[i]["hold"]
        fin[i] = st + (ops[i]["hold"] if back else ops[i]["lat"])
        out.append(i)
        for s in succ[i]:
            a, b = (s, i) if back else (i, s)
            gap = 0.0 if b in ops[a]["soft"] else ops[a]["lat"] - ops[a]["hold"] + HOP
            at[s] = max(at[s], st + ops[i]["hold"] + gap)
            left[s] -= 1
            if not left[s]:
                ready[s] = at[s]
    return out, fin


def rank_program(g, core, T, topo):
    rank = T.rank_of(core)
    if rank is None:
        return
    cores = list(T.cores)
    Q = {"v": g.vector, "a": g.scalar, "p": g.tensor, "g": g, "s": g.sync}
    V, S_, P = g.vector, g.scalar, g.tensor
    ops, hist, bysem, part, seen = [], {}, {}, [0, -1], {}

    def r(name, lo=0, hi=None, st=1):
        hi = SCRATCH[name][1][1] if hi is None else hi
        return (T[name][:, lo:hi:st] if st != 1 else T[name][:, lo:hi], name, lo, hi, len(range(lo, hi, st)))

    def ind(win, off):
        return (win[0].indirect(off[0]), win[1], win[2], win[3], 16 * off[4], off)

    def dr(name, lo, hi):
        return (None, name, lo, hi, 0)

    banks, behind, line = {}, [], {}

    def op(q, fn, rd, wr, hold, lat=None, sem=None, pre=(), after=(), start=False):
        me_ = len(ops)
        acc = []
        for x, w in [(x, False) for x in rd] + [(x, True) for x in wr]:
            if len(x) > 5:
                acc.append((x[5][1], x[5][2], x[5][3], False, 1))
            acc.append((x[1], x[2], x[3], w, -(-(x[3] - x[2]) // x[4]) if len(x) == 5 and x[4] > 1 else 1))
        deps, soft = set(), set(after) | set(behind)
        behind[:] = []
        if q in line:
            soft.update(line[q])
            line[q] = [me_]
        for name, lo, hi, w, st in acc:
            if name in PS:
                bk = banks.setdefault(name, {"pe": [], "np": [], "first": None})
                if q != "p":
                    deps.update(bk["pe"] + [e for e in bk["np"] if ops[e]["q"] != q])
                    bk["np"].append(me_)
                elif start:
                    deps.update(bk["np"])
                    soft.update(bk["pe"])
                    banks[name] = {"pe": ([] if bk["np"] else bk["pe"]) + [me_], "np": [], "first": me_}
                else:
                    deps.update(bk["np"])
                    soft.add(bk["first"])
                    bk["pe"].append(me_)
                continue
            for e in hist.get(name, []):
                if lo < e[1] and e[0] < hi and (w or e[2]) and not (st > 1 and st == e[4] and (lo - e[0]) % st):
                    deps.update(bysem.get(ops[e[3]]["sem"], [e[3]]))
        deps.discard(me_)
        if sem:
            deps -= set(bysem.get(sem, []))
            bysem.setdefault(sem, []).append(me_)
        soft -= deps
        for d in soft:
            ops[d]["soft"].add(me_)
        lab = (part[0], q, wr[0][1] if wr else "")
        seen[lab, part[1]] = seen.get((lab, part[1]), -1) + 1
        ops.append({"q": q, "fn": fn, "deps": deps | soft, "wait": deps, "soft": set(), "hold": hold, "lat": lat or hold, "sem": sem, "pre": pre,
                    "lab": lab + (seen[lab, part[1]],), "t": part[1], "sum": banks[wr[0][1]]["first"] if q == "p" else None})
        for name, lo, hi, w, st in acc:
            h = hist.get(name, [])
            if name in PS:
                continue
            if w and st == 1:
                h = [e for e in h if not (lo <= e[0] and e[1] <= hi) or (sem and ops[e[3]]["sem"] == sem)]
            h.append((lo, hi, w, me_, st))
            hist[name] = h
        return me_

    def vcost(o, ins, both=1):
        if len(o) > 5:
            return 0.05 + 3.8 * o[4] * CYC
        if any(len(x) > 5 for x in ins):
            return 0.05 + 1.56 * o[4] * CYC
        two = all(SCRATCH[x[1]][2] in (bf, u16) for x in [o] + ins)
        return 0.03 + max(64, o[4] * both * (0.5 if two else 1)) * CYC

    def cp(o, i):
        op("v", lambda: V.tensor_copy(o[0], i[0]), [i], [o], vcost(o, [i]))

    def tt(o, a, b, f):
        op("v", lambda: V.tensor_tensor(o[0], a[0], b[0], f), [a, b], [o], vcost(o, [a, b], 1 if a[1] in PS or b[1] in PS else 2))

    def ts(o, a, s1, f1, s2=None, f2=None):
        cols = [s for s in (s1, s2) if isinstance(s, tuple)]
        x1 = s1[0] if isinstance(s1, tuple) else s1
        x2 = s2[0] if isinstance(s2, tuple) else s2
        if f2 is None:
            op("v", lambda: V.tensor_scalar(o[0], a[0], x1, None, f1), [a] + cols, [o], vcost(o, [a]))
        else:
            op("v", lambda: V.tensor_scalar(o[0], a[0], x1, x2, f1, f2), [a] + cols, [o], vcost(o, [a]))

    def scan(o, d0, d1, init, f0, f1):
        op("v", lambda: V.tensor_tensor_scan(o[0], d0[0], d1[0], init, f0, f1), [d0, d1], [o], vcost(o, [d0, d1]))

    def ms(o, c):
        op("v", lambda: V.memset(o[0], c), [], [o], vcost(o, []))

    def act(o, i, f=F.Identity, bias=0.0, scale=1.0):
        cols = [bias] if isinstance(bias, tuple) else []
        b = bias[0] if cols else bias
        op("a", lambda: S_.activation(o[0], i[0], f, bias=b, scale=scale), [i] + cols, [o], 0.075 + o[4] * (1.56 if len(i) > 5 else 1) * CYC)

    def mm(o, l, rh, start, stop):
        c = 0.02 + max(64, rh[4]) * (4 if SCRATCH[l[1]][2] == f32 else 1) * PCYC
        op("p", lambda end: P.matmul(o[0], l[0], rh[0], start, end), [l, rh], [o], c, c + 0.1, start=start)

    def mms(o, pairs):
        for k, (l, rh) in enumerate(pairs):
            mm(o, l, rh, k == 0, k == len(pairs) - 1)

    def dma(q, o, i, sem, rd=(), wr=(), lat=2.0, pre=(), after=(), hold=None, **kw):
        return op(q, lambda: Q[q].dma_start(o, i, **kw), list(rd), list(wr), hold or (0.8 if q == "g" else 0.1), lat, sem, pre, after)

    sent = [0]

    def remote(plan, src, dst, sem, rd, hold=3.0, after=(), issue=0.7):
        tr = []
        for d, es in plan:
            rid, pid, _ = topo.addr(cores[d])
            tr.append(RemoteDMATransfer(dst_ids=[DstId(rid=rid, pnc=pid)], dma_engine_mask=_mask(es), remote_sem=T.sem[sem],
                                        src=src(d), dst=dst))
            sent[0] += len(es)
        a = op("g", lambda: g.remote_dma_fused(tr, local_sem=T.sem.ls), rd, [], issue, None, "", (), after)
        return a, op("link" if part[1] < 0 or part[0] == 7 else sem[:2], None, [], [], hold, None, "", (), [a])

    def m(n, lo=0, hi=128, st=1):
        buf, k = ("MB", MB.index(n)) if n in MB else ("MF", MF.index(n))
        return r(buf, 128 * k + lo, 128 * k + hi, st)

    calls, single = _calls(core, cores, topo)
    me = slice(16 * rank, 16 * rank + 16)
    XW, CW, AW, ZW = r("TB", XO, ZP), r("TB", CO, TW), r("TB", 0, TW), r("TB", ZP, TW)

    def stage(k, lat):
        dma("s", T["PS%d" % k][:], T.px[:, CUTS[k][0]:CUTS[k][1]], "xs%d" % k, wr=[dr("PS%d" % k, 0, 1)], lat=lat)

    def iota(o, pattern, base, step):
        op("g", lambda: g.iota(o[0], pattern, base, step, allow_small_or_imprecise_dtypes=True), [], [o], 0.13 + 2 * o[4] * CYC)

    def fill(name, val):
        iota(r(name), [[0, SCRATCH[name][1][1]]], int(val), 0)

    line.update({"s": [], "a": [], "v": [], "g": []})
    stage(0, 2.8)
    dma("s", T.CI[:, 0:1024], T.ce[:], "dce", wr=[r("CI", 0, 1024)], lat=4.8)
    stage(1, 5.6)
    dma("s", T.PXB[:], T.px[:], "dpb", wr=[r("PXB")], lat=9.0)
    dma("a", T.CI[:, 1024:1032], T.v0[:], "dv0", wr=[r("CI", 1024, 1032)])
    dma("a", T.SH[:, 0:128], T.z0[:], "dz0", wr=[r("SH", 0, 128)], lat=2.8)
    dma("a", T.SH[:, 128:144], T.kap[:], "dsm", wr=[r("SH", 128, 144)], lat=4.6)
    dma("a", T.SH[:, 160:161], T.wu[:], "dsm", wr=[r("SH", 160, 161)], lat=5.6)
    op("g", lambda: g.iota(T.PI[:, 0:1], [[0, 1]], 0, 1), [], [r("PI", 0, 1)], 0.15)
    iota(r("IOT", 0, 128), [[1, 128]], 0, 0)
    iota(r("CQ", 256, 264), [[1, 2], [32, 4]], 0, 0)
    iota(r("CP"), [[1, 128]], 0, -1)
    iota(r("CQ", 0, 128), [[1, 8], [8, 16]], 0, -1)
    iota(r("CQ", 128, 256), [[1, 8], [0, 16]], 0, 0)
    ways = {}

    def piece(k):
        ways[k] = remote(calls[k % len(calls)], lambda d: T["PS%d" % k][d], T["PL%d" % k][rank], "ay%d" % k, [dr("PS%d" % k, 0, 1)],
                         (CUTS[k][1] - CUTS[k][0]) / 470 + 1.4 * (k == 0), (), 0.7 if k else 2.7)[1]

    def land(k):
        lo, hi = CUTS[k]
        n = sum(len(es) for _, es in calls[k % len(calls)])
        dma("s", T.XB[:, lo:hi], T["PL%d" % k][:], "xl%d" % k, rd=[dr("PL%d" % k, 0, 1)], wr=[r("XB", lo, hi)], pre=[("ay%d" % k, n)], after=[ways[k]])
        mid = lo if k < 3 else (lo + hi) // 2
        if mid > lo:
            cp(r("TB", XO + lo, XO + mid), r("XB", lo, mid))
        act(r("TB", XO + mid, XO + hi), r("XB", mid, hi))

    z, x, x1, f = r("z"), r("xx"), r("x1"), r("ff")
    per, per2, nat, oh, Y = r("vl", 0, 8), r("vl", 8, 16), r("vl", 16, 24), r("OH"), r("Y")
    LP, LQ1, LQ2 = r("LP", 0, 8), r("LP", 8, 16), r("LP", 16, 24)
    Mp, Bp, NMp, fq, zq = r("PW", 0, 128), r("PW", 128, 256), r("PW", 256, 384), r("QW", 0, 128), r("QW", 128, 256)
    par, aG = r("PA", 0, 8), r("PA", 8, 16)
    acol, gcol = r("COL", 0, 1), r("COL", 1, 2)
    lane, l128, l4, th = r("GL", 0, 8), r("GB", 8, 16), r("GB", 0, 8), r("GL", 24, 32)

    def turn(src, sh):
        b = r("A0", 0, 128)
        mm(b, src, sh, True, True)
        act(r("TT"), b)

    def spread(e, l, src):
        mms(r(e, 0, src[4]), [(m("I"), r("MASK", 0, src[4])), (l, src)])

    def lists(e, lo, w):
        scan(r("DG", lo, lo + w), r("RB", 0, w), r(e, 0, w), 0.0, A.add, A.min)
        return r("DG", lo + 15, lo + w, 16)

    piece(0)
    piece(1)
    for nme, val in (("K3", 0), ("NM", 0), ("ZC", 0)):
        fill(nme, val)
    ms(r("WN"), 0.0)
    ms(r("RB"), 0.0)
    ms(m("POS2"), 8388608.0)
    ms(r("HU", 1168, 1184), 0)
    ts(r("PI", 2, 3), r("PI", 0, 1), 15, A.bitwise_and)
    ts(r("PI", 4, 5), r("PI", 0, 1), 4, A.arith_shift_right)
    cp(acol, r("PI", 2, 3))
    cp(gcol, r("PI", 4, 5))
    ms(r("RB", 0, None, 16), BIG)
    ts(r("OH", 0, 16), r("IOT", 0, 16), acol, A.is_equal)
    cp(nat, r("CI", 1024, 1032))
    cp(r("OH", 16, 32), r("OH", 0, 16))
    ts(r("PI", 5, 6), r("PI", 0, 1), 7, A.bitwise_and)
    ts(r("PI", 6, 7), r("PI", 2, 3), 3, A.arith_shift_right)
    cp(r("COL", 8, 10), r("PI", 5, 7))
    ts(r("COL", 10, 11), r("COL", 8, 9), 16.0, A.mult, r("COL", 9, 10), A.add)
    ts(r("COL", 12, 13), r("COL", 8, 9), 2.0, A.mult)
    ts(LQ1, r("IOT", 0, 16, 2), r("COL", 10, 11), A.add)
    ts(r("COL", 11, 12), r("COL", 9, 10), 16.0, A.mult, r("COL", 12, 13), A.add)
    ts(LQ2, r("CQ", 256, 264), r("COL", 11, 12), A.add)
    cp(r("OH", 32, 64), r("OH", 0, 32))
    ts(m("I"), r("CP"), 0.0, A.is_equal)
    cp(r("OH", 64, 128), r("OH", 0, 64))
    ts(m("I32"), r("CP"), 0.0, A.is_equal)
    cp(r("OH", 128, 256), r("OH", 0, 128))
    ts(r("G8", 0, 8), r("IOT", 0, 8), gcol, A.is_equal)
    ts(r("MASK"), r("OH", 0, 256), -BIG / 2, A.mult, BIG / 2, A.add)
    for w in (128, 256, 512):
        act(r("IOT", w, 2 * w), r("IOT", 0, w), bias=float(w))
    act(r("VR", 0, 128), ind(r("IOT"), nat))
    act(r("VR", 128, 384), ind(r("VR", 0, 128), r("LP", 8, 24)))
    spread("PM", m("I32"), r("VR", 128, 384))
    act(zq, ind(r("SH", 0, 128), LQ2))
    for k in range(16):
        ts(r("WN", 128 * k + k, 128 * k + 128, 16), r("G8", 0, 8), -2048.0, A.mult)
        act(r("EP", k, 2048, 16), m("I"))
    turn(zq, m("I"))
    cp(r("HU", 0, 1032), r("CI"))
    cp(r("SF", 0, 144), r("SH", 0, 144))
    cp(r("SF", 144, 145), r("SH", 160, 161))
    both = lists("PM", 0, 256)
    cp(r("HU", 1032, 1177), r("SF", 0, 145))
    cp(r("vl", 0, 16), both)
    cp(m("POS"), r("IOT", 0, 128))
    ts(r("COL", 2, 3), acol, 128.0, A.mult)
    ts(m("POS1"), r("IOT", 0, 128), 0.0, A.mult, r("COL", 2, 3), A.add)
    for w in (256, 512, 1024):
        cp(r("OH", w, 2 * w), r("OH", 0, w))
    dma("s", T.CS[:], T.HU[:], "dcs", rd=[r("HU")], wr=[dr("CS", 0, 1)], lat=3.8)
    for k in range(2, len(CUTS)):
        stage(k, 3.5 + 0.6 * k)
    dma("s", T.CL[rank], T.HU[me, :], "xo", rd=[r("HU")], wr=[dr("CL", 0, 1)], lat=6.0)
    for k, (lo, hi) in enumerate(CUTS):
        dma("s", T["PL%d" % k][rank], T.px[me, lo:hi], "xo", wr=[dr("PL%d" % k, 0, 1)], lat=6.0)
    lc = remote(calls[0], lambda d: T.CS[d], T.CL[rank], "ac", [dr("CS", 0, 1)], 3.9)[1]
    piece(2)

    def hand_over():
        dma("s", T.XD[:], T.XS[:], "dxs", rd=[r("XS")], wr=[dr("XD", 0, 1)])
        dma("s", T.XL[rank], T.XS[me, :], "dxo", rd=[r("XS")], wr=[dr("XL", 0, 1)])
        for nme, val in (("PA", 0), ("K4", ZP), ("TC", MG), ("DK", 0)):
            fill(nme, val)
        lx = remote(single, lambda d: T.XD[d], T.XL[rank], "ah", [dr("XD", 0, 1)], 1.8)[1]
        piece(3)
        piece(4)

        def roll(dst, src, k):
            act(m(dst, k, 128), m(src, 0, 128 - k))
            act(m(dst, 0, k), m(src, 128 - k, 128))
        ts(m("BO32"), r("CQ", 128, 256), gcol, A.is_equal)
        ts(m("PM1"), r("CQ", 0, 128), 0.0, A.is_equal)
        roll("S", "I", 16)
        roll("SB", "I", 112)
        roll("BS32", "BO32", 16)
        act(m("BSb"), m("BS32"))
        act(m("nI"), m("I"), scale=-1.0)
        act(r("WD", 0, 1024), r("WN", 0, 1024), scale=-1.0)
        ts(r("WD", 1024, 2048), r("WN", 1024, 2048), -1.0, A.mult)
        ts(r("ALL"), r("IOT", 0, 1024, 16), acol, A.add)
        for nme in ("TB", "HB"):
            ms(r(nme, 0, XO), 0.0)
            ms(r(nme, ZP, CO), 0.0)
        ts(lane, r("IOT", 0, 128, 16), acol, A.add)
        ms(r("RC"), -BIG)
        ts(l128, lane, 128.0, A.mult)
        ts(l4, lane, 4.0, A.mult)
        ts(th, lane, 128.0, A.mult, 13.0, A.add)
        act(r("G8", 9, 16), r("G8", 0, 7))
        act(r("G8", 8, 9), r("G8", 7, 8))
        for nme, src, sc in (("BOK", "BO32", KS_), ("S2", "S", 2.0), ("nI2", "I", -2.0)):
            act(m(nme), m(src), scale=sc)
        counts()
        ms(r("RR"), 0.0)
        ms(r("SENT"), 0.0)
        ms(r("CMP"), KS_)
        ms(r("CD"), 0.0)
        ms(r("RR", 15, None, 16), BIG)
        ms(r("SENT", 0, 1), ZP * KS_)
        ts(r("COL", 6, 7), acol, 8.0, A.mult)
        ts(r("COL", 4, 5), acol, 150.0, A.mult, 149.0, A.add)
        ts(r("COL", 5, 6), acol, -134.0, A.mult, 1068.0, A.add)
        ts(LP, r("IOT", 0, 8), r("COL", 6, 7), A.add)
        ts(r("FL", 0, 1), r("COL", 4, 5), r("COL", 5, 6), A.min)
        for c in range(8):
            ts(r("CD", SEG[c] + 1 + 16 * c, SEG[c] + 17 + 16 * c), r("OH", 0, 16), -4 * KS_, A.mult)
        for at, st, val in ((0, 150, KS_), (131, 134, KS_), (129, 134, 4 * KS_), (148, 150, 4 * KS_)):
            ms(r("CD", at, at + 3 * st + 1, st), val)
        cp(r("CD", 130, 130 + 3 * 134 + 1, 134), (T.GL[:, 7:3:-1], "GL", 4, 8, 4))
        cp(r("CD", 149, 149 + 3 * 150 + 1, 150), r("GL", 0, 4))
        land(0)
        land(1)
        dma("s", T.WU[:], T.CL[:], "dwu", rd=[dr("CL", 0, 1)], wr=[r("WU")], lat=2.5, pre=[("ac", sum(len(es) for _, es in calls[0]))], after=[lc])
        cp(r("TB", TW, SM), r("WU", 1024, 1184))
        cp(r("SMB", 0, 17), r("TB", TW + 136, TW + 153))
        b = r("PX", 0, 17)
        mm(b, m("SB"), r("SMB", 0, 17), True, True)
        act(r("KS", 0, 17), b)
        cp(CW, r("WU", 0, 1024))
        ts(m("WUm"), m("BSb"), r("KS", 16, 17), A.mult)
        land(2)
        dma("s", T.XR[:], T.XL[:], "dxr", rd=[dr("XL", 0, 1)], wr=[r("XR")], pre=[("ah", N - 1)], after=[lx])
        cp(r("z"), r("TB", TW + 8, TW + 136))
        cp(x, r("XR", 0, 128))
        keep = {"s": line["s"], "g": line["g"]}
        line.clear()
        line.update(keep)
        land(3)
        land(4)
        dma("g", T.HB[:, XO:ZP], T.px[:], "dhb", rd=[r("XB")], wr=[r("HB", XO, ZP)], lat=11.0, hold=2.8)
        line.clear()
        for k in range(8):
            ts(m("KP", 16 * k, 16 * k + 16), r("KS", 0, 16), r("G8", 8 + k, 9 + k), A.mult)
        for k in range(4):
            act(r("W2", 512 * k, 512 * k + 512), r("OH", 0, 512), scale=2 * BIG / 16 - MG, bias=MG)
            act(r("HB", CO + 256 * k, CO + 256 * k + 256), ind(r("CI", 0, 1024), r("ALL", 16 * k, 16 * k + 16)))


    def probe(step, win=XW):
        pd = r("PD", 0, 128)
        mm(pd, m("I"), m("POS"), True, False)
        mm(pd, m("I"), m("POS1"), False, False)
        if step == 1:
            mm(pd, m("I"), m("POS2"), False, False)
        def bank(a0, a1):
            spare = SPARE[step - 1].get(a0)
            return r(spare, 0, 128 * (a1 - a0)) if spare else r("E%d" % (a0 // 4), 128 * (a0 % 4), 128 * (a0 % 4 + a1 - a0))
        takes = sorted((e == "a", a0, a1) for what, e, a0, a1 in PLAN[step - 1] if what == "take")
        if step == 1:
            takes = [(False, 4 * k, 4 * k + 4) for k in range(4)]
        for opened, a0, a1 in takes:
            mm(bank(a0, a1), r("TT"), r("EP", 128 * a0, 128 * a1), True, False)
        prev, first = {}, True
        for what, e, a0, a1 in PLAN[step - 1]:
            lo, hi = 128 * a0, 128 * a1
            b = bank(a0, a1)
            if what == "take" and e == "a":
                mm(b, m("nI"), r("Y", lo, hi), False, True)
            behind[:] = prev.get(e, [])
            if what == "gather":
                (act if e == "a" else cp)(r("Y", lo, hi), ind(win, r("L16", lo // 16, hi // 16)))
            elif e == "a":
                act(r("AB", lo, hi), b, F.Relu if step == 1 else F.Abs)
            else:
                tt(r("AB", lo, hi), r("Y", lo, hi), b, A.min)
                if step > 1:
                    tt(r("EX", lo, hi), r("Y", lo, hi), b, A.max)
            prev[e] = [len(ops) - 1]
            for a in range(a0, a1):
                blk = (128 * a, 128 * a + 128)
                if what == "gather" and step == 2:
                    mm(r("PX", 0, 128), r("WN", *blk), r("Y", *blk), first, False)
                    first = False
                if what == "take":
                    mm(pd, r("WD" if e == "a" else "WN", *blk), r("AB", *blk), False, False)
                    if e == "v" and step > 1:
                        mm(pd, r("WD", *blk), r("EX", *blk), False, False)
        return prev["v"]

    def counts():
        b = r("PX", 0, 8)
        mms(b, [(m("S"), par), (m("I"), l128)])
        act(r("RC", 0, 128, 16), b)

    def least():
        scan(r("rm"), r("RB", 0, 128), r("PD", 0, 128), 0.0, A.add, A.min)

    def low(out, src, mask, tmp):
        if U16AND:
            ts(out, src, mask, A.bitwise_and)
        else:
            ts(tmp, src, mask, A.bitwise_and)
            cp(out, tmp)

    def decode(out, src, tmp):
        low(out, r(src, 15, 128, 16), 2047, r(tmp))

    def send_log(s):
        lg = r("LG", LW * s, LW * s + LW)
        sem = "lt%d" % s
        dma("s", T.LS[8 * s:8 * s + 8], lg[0], sem, rd=[lg], wr=[dr("LS", s, s + 1)])
        dma("s", T.LL[8 * s + rank], T.LG[me, LW * s:LW * s + LW], sem, rd=[lg], wr=[dr("LL", s, s + 1)])
        _, l = remote(single, lambda d: T.LS[8 * s + d], T.LL[8 * s + rank], "la%d" % s, [dr("LS", s, s + 1)], 3.0)
        hl = r("HL", LW * s, LW * s + LW)
        dma("s", hl[0], T.LL[8 * s:8 * s + 8], "lh%d" % s, rd=[dr("LL", s, s + 1)], wr=[hl], pre=[("la%d" % s, N - 1)], after=[l])

    def apply_log(s, after=()):
        if s < 0:
            return []
        ho = r("ho16", 8 * (s % 2), 8 * (s % 2) + 8)
        keep, part[0] = part[0], 10 + s % 2 if part[1] < RO else part[0]
        cp(ho, r("HL", LW * s + 256, LW * s + 264))
        behind[:] = after
        tt(ind(r("HB"), ho), r("HL", LW * s, LW * s + 128), r("HL", LW * s + 128, LW * s + 256), A.add)
        part[0] = keep
        return [len(ops) - 1]

    def keys(vc):
        mm(r("PM", 0, 128), m("I"), r("MASK", 0, 128), True, False)
        mm(r("PM", 0, 128), m("BOK"), r("ks"), False, True)
        for e, cs in (("E1", vc), ("E2", [c for c in range(8) if c not in vc])):
            if cs:
                wa = 17 + 16 * max(cs)
                mm(r(e, 0, wa), m("I"), r("SENT", 0, wa), True, False)
                mm(r(e, 1, wa), m("BOK"), r("ks", 0, wa - 1), False, True)
        scan(r("DK", 0, 128), r("RB", 0, 128), r("PM", 0, 128), 0.0, A.add, A.min)
        for c in range(7, -1, -1):
            o, own_ = r("CMP", SEG[c] + 1, SEG[c] + 18 + 16 * c), r("DK", 16 * c + 15, 16 * c + 16)
            if c in vc:
                ts(o, r("E1", 0, 16 * c + 17), own_, A.not_equal, KS_, A.mult)
            else:
                act(o, r("E2", 0, 16 * c + 17), F.Abs, bias=own_, scale=-1.0)
        ts(r("DKp"), r("DK", 15, 256, 16), 1 / KS_, A.mult)

    def winners(s):
        scan(r("WO"), r("CMP"), r("CD"), 0.0, A.min, A.add)
        o = r("LG", LW * s + 256, LW * s + 272)
        if s < NL - 1 and U16TT:
            tt(r("off16"), ind(r("WO"), r("FL", 0, 1)), r("DKp"), A.min)
        tt(o, ind(r("WO"), r("FL", 0, 1)), r("DKp"), A.min)
        if s < NL - 1:
            if not U16TT:
                cp(r("off16", 0, 8), r("LG", LW * s + 256, LW * s + 264))
            tt(ind(AW, r("off16", 0, 8)), r("LG", LW * s, LW * s + 128), r("LG", LW * s + 128, LW * s + 256), A.add)

    def rev(n):
        return (T[n][:, 127::-1], n, 0, 128, 128)

    kM, k4 = r("K3", 1, 512, 4), r("K4", 0, 512, 4)
    blA, blB, bl4, pos, posm = r("blA"), r("blB"), r("bl4"), r("pos"), r("posm")
    for t in range(RO):
        last = t == RO - 1
        la, lb = r("LG", LW * 2 * t, LW * 2 * t + 128), r("LG", LW * 2 * t + 128, LW * 2 * t + 256)
        part[:] = [1, t]
        cells = CW if t else r("CI", 0, 1024)
        cp(r("L16"), ind(cells, per2))
        act(r("Lf"), ind(cells, per), bias=float(XO))
        if t:
            counts()
        probe(1, XW if t else r("PXB"))
        least()
        decode(pos, "rm", "tj")
        sel = r("sel") if t else r("XR", 128, 256)
        cp(x if t else r("XS", 0, 128), ind(Y, pos))
        tt(sel if t else r("XS", 128, 256), ind(oh, pos), r("Lf"), A.mult)
        if not t:
            part[0] = 7
            hand_over()
        part[0] = 2
        spread("PM", m("WUm"), x)
        turn(x, m("S"))
        low(per, lists("PM", 0, 128), 1023, r("bi", 0, 8))
        cp(r("L16"), ind(CW, per))
        b, bn = r("A0", 0, 128), r("E3", 0, 128)
        mm(b, r("TT"), m("PM1"), True, True)
        act(x1, b)
        mm(bn, m("BS32"), sel, True, True)
        act(Mp, ind(CW, per), bias=MG + XO)
        act(Bp, ind(r("IOT"), per), bias=MG + CO)
        act(kM, ind(Mp, LP))
        act(r("K3", 2, 512, 4), ind(Bp, LP))
        taken = probe(2)
        homes = (apply_log(2 * t - 3, taken) + apply_log(2 * t - 2, taken))[:PIN]
        tt(NMp, bn, Mp, A.subtract)
        act(r("NM", 1, 512, 4), ind(NMp, LP), bias=MG)
        part[0] = 5
        act(r("LT"), r("PD", 0, 128), F.Sign, bias=-(240 * 2048 - 0.5))
        behind[:] = homes
        least()
        act(r("PDs"), r("PD", 0, 128), bias=-8388608.0)
        mm(r("PX", 0, 128), m("I32"), r("PDs"), False, True)
        decode(pos, "rm", "tj")
        scan(r("U"), r("RC"), r("LT"), -BIG, A.max, A.add)
        ts(blB, r("U", 15, 128, 16), 35.0, A.add, 1.0 / 32, A.mult)
        ts(blA, r("U", 15, 128, 16), 3.0, A.add, 1.0 / 32, A.mult)
        act(r("Kb"), ind(r("K3"), blB), bias=-MG)
        act(r("yj"), ind(Y, pos))
        scan(rev("hold"), rev("RR"), rev("rm"), 0.0, A.add, A.min)
        tt(r("ne"), r("PD", 0, 128), r("hold"), A.not_equal)
        tt(r("mk"), r("PX", 0, 128), r("ne"), A.mult)
        scan(r("rm2"), r("RB", 0, 128), r("mk"), 0.0, A.add, A.min)
        decode(posm, "rm2", "tl")
        tt(f, ind(Y, posm), x1, A.max)
        tt(r("ks"), ind(oh, pos), r("Kb"), A.mult)
        bq = r("PX", 0, 128)
        (act if FQ == "a" else cp)(fq, ind(f, LQ1))
        mm(bq, m("KP"), fq, True, True)
        cp(r("hi"), bq)
        low(r("L16"), r("hi"), 4095, r("ci"))
        keys(VCMP[0])
        act(r("nmz"), ind(r("NM"), blA))
        tt(lb, ind(oh, pos), r("nmz"), A.mult)
        b, b3 = r("PD", 0, 128), r("PD", 256, 384)
        mms(b, [(m("I"), x1), (m("I"), r("yj"))])
        mms(b3, [(m("S"), z), (m("nI"), r("yj"))])
        act(r("K3", 0, 512, 4), b, bias=MG + XO, scale=0.4995)
        act(r("ZC", 0, 512, 4), b3, bias=MG)
        act(la, ind(r("K3"), blA), bias=-(MG + XO))
        turn(fq, m("S"))
        winners(2 * t)
        send_log(2 * t)
        tt(r("exG"), r("U", 15, 128, 16), th, A.is_lt)
        tt(r("selm"), ind(oh, posm), kM, A.mult)
        part[0] = 3
        la, lb = r("LG", LW * (2 * t + 1), LW * (2 * t + 1) + 128), r("LG", LW * (2 * t + 1) + 128, LW * (2 * t + 1) + 256)
        if U16AND:
            ts(r("ci"), r("hi"), 4095, A.bitwise_and)
        act(k4, ind(r("ci"), LP), bias=float(XO))
        ts(r("cc"), r("hi"), 1023, A.bitwise_and)
        act(r("K4", 1, 512, 4), ind(r("cc"), LP), bias=float(CO))
        b = r("A0", 0, 128)
        mm(b, m("BS32"), r("selm"), True, True)
        act(r("nm3"), b, bias=-float(XO))
        l4e = r("A0", 256, 264)
        mms(l4e, [(m("I"), l4), (m("S2"), r("exG"))])
        mms(r("A0", 0, 8), [(m("S"), par), (m("nI2"), r("exG"))])
        mms(r("A0", 8, 16), [(m("S"), aG), (m("I"), r("exG"))])
        act(r("PA"), r("A0", 0, 16), F.Abs)
        act(r("VR", 0, 128), ind(Bp, LP if last else LQ1), bias=-(MG + CO))
        spread("A0", m("I32"), r("VR", 0, 128))
        cp(r("vG") if last else per2, lists("A0", 128, 128))
        if last:
            cp(r("a16"), aG)
            act(r("ar"), ind(r("IOT"), r("a16")))
            dma("s", T.VS[:, 0:64, :], T.vG[:], "dvs", rd=[r("vG")], wr=[dr("VS", 0, 1)])
            dma("s", T.VS[:, 64:128, :], T.ar[0:128:16, :], "dvs", rd=[r("ar")], wr=[dr("VS", 0, 1)])
            _, l = remote(single, lambda d: T.VS[d], T.VL[rank], "av", [dr("VS", 0, 1)])
            dma("s", T.VL[rank], T.VS[rank], "dvo", rd=[dr("VS", 0, 1)], wr=[dr("VL", 0, 1)])
            dma("s", T.yv[:], T.VL[:, 0:64, :], "dout", rd=[dr("VL", 0, 1)], pre=[("av", N - 1)], after=[l])
            dma("s", T.ya[:], T.VL[:, 64:128, :], "dout", rd=[dr("VL", 0, 1)], pre=[("av", N - 1)], after=[l])
        probe(3)
        least()
        part[0] = 4
        ts(r("tg", 8, 16), r("rm", 15, 128, 16), 640.0 * 2048, A.is_ge)
        if U16TT:
            tt(bl4, l4e, r("tg", 8, 16), A.add)
        else:
            tt(r("tg", 0, 8), l4e, r("tg", 8, 16), A.add)
            cp(bl4, r("tg", 0, 8))
        line["a"] = []
        act(r("Kb"), ind(r("K4"), bl4))
        decode(pos, "rm", "tj")
        act(r("wq"), ind(Y, pos))
        tt(r("ks"), ind(oh, pos), r("Kb"), A.mult)
        bz, bh = r("PX", 0, 128), r("PD", 0, 128)
        mms(bz, [(m("S"), z), (m("SB"), r("wq"))])
        act(r("ZC", 1, 512, 4), bz, bias=MG, scale=0.4995)
        act(z, ind(r("ZC"), blA), F.Abs, bias=-MG)
        keys(VCMP[1])
        if not last:
            act(zq, ind(z, LQ2))
            turn(zq, m("I"))
        line.clear()
        tt(r("TC", 1, 512, 4), ind(r("W2"), pos), r("nm3"), A.min)
        mms(bh, [(m("S"), f), (m("I"), r("wq"))])
        act(r("noh"), ind(oh, pos), bias=1.0, scale=-1.0)
        ts(r("key16"), r("DK", 15, 128, 16), 1 / KS_, A.mult, float(ZP), A.subtract)
        act(r("TC", 0, 512, 4), bh, bias=MG, scale=0.4995)
        act(la, ind(r("TC"), bl4), bias=-MG)
        tt(lb, ind(ZW, r("key16")), r("noh"), A.mult)
        winners(2 * t + 1)
        send_log(2 * t + 1)

    part[:] = [9, RO]
    for s in range(NL - 3, NL):
        apply_log(s)
    dma("a", T.ZS[:], T.z[:], "dzs", rd=[z], wr=[dr("ZS", 0, 1)])
    dma("a", T.ZL[rank], T.z[me, :], "dzs", rd=[z], wr=[dr("ZL", 0, 1)])
    _, l = remote(single, lambda d: T.ZS[d], T.ZL[rank], "az", [dr("ZS", 0, 1)], 0.5)
    dma("a", T.yz[:], T.ZL[:], "dout", rd=[dr("ZL", 0, 1)], pre=[("az", N - 1)], after=[l])
    dma("g", T.yx[:], T.HB[:, XO:ZP], "dyx", rd=[r("HB")], lat=6.0)
    dma("s", T.yc[:], T.HB[:, CO:TW], "dout", rd=[r("HB")], lat=4.0)

    cnt, waited, done = {}, {}, {}

    def wait(q, sem, val):
        if waited.get((q, sem), 0) < val:
            Q[q].wait_ge(T.sem[sem], val)
            waited[(q, sem)] = val

    order = _order(ops)
    place = {i: k for k, i in enumerate(order)}
    ends = {ops[i]["sum"]: i for i in order if ops[i]["q"] == "p"}
    needed, waits = set(), []
    for o in ops:
        late = {}
        for d in o["wait"]:
            k = ops[d]["lab"][2] if ops[d]["q"] == "p" else d
            late[k] = max(late.get(k, d), d, key=lambda j: place[j])
        waits.append(sorted(late.values()))
        needed |= set(waits[-1])
    for i in order:
        o = ops[i]
        if o["fn"] is None:
            continue
        need = dict(o["pre"])
        for d in waits[i]:
            s, val = done[d]
            need[s] = max(need.get(s, 0), val)
        for s in sorted(need):
            wait(o["q"], s, need[s])
        ins = o["fn"](ends[o["sum"]] == i) if o["q"] == "p" else o["fn"]()
        if o["sem"]:
            cnt[o["sem"]] = cnt.get(o["sem"], 0) + 16
            ins.then_inc(T.sem[o["sem"]], 16)
            done[i] = (o["sem"], 16 * len(bysem[o["sem"]]))
        elif o["sem"] is None and i in needed:
            s = "q" + o["q"]
            cnt[s] = cnt.get(s, 0) + 1
            ins.then_inc(T.sem[s], 1)
            done[i] = (s, cnt[s])
    cnt["ls"] = sent[0]
    for s in sorted(cnt):
        wait("g", s, cnt[s])
